import numpy as np
import ml_dtypes


def mxq(x, axis, fmt="e4m3"):
    dtype, down = {"e4m3": (ml_dtypes.float8_e4m3fn, 7), "e5m2": (ml_dtypes.float8_e5m2, 14)}[fmt]
    v = np.moveaxis(np.asarray(x, np.float32).astype(ml_dtypes.bfloat16).astype(np.float64), axis, -1)
    blocks = v.reshape(v.shape[:-1] + (-1, 32))
    amax = np.abs(blocks).max(-1, keepdims=True)
    byte = np.maximum(np.where(amax > 0, np.frexp(amax)[1] - 1 + 127, 0) - down, 1)
    scale = np.exp2(byte - 127.0)
    codes = (blocks / scale).astype(np.float32).astype(dtype).astype(np.float64)
    return np.moveaxis((codes * scale).reshape(v.shape), -1, axis)


WIDE = False


def mx_kscale(k):
    if not WIDE:
        return np.ones(k)
    levels = np.array([10, -10, 5, -5, 0])
    if k % 512:
        return np.exp2(np.random.permutation(np.resize(levels, k // 32))).repeat(32)
    a = np.empty((k // 512, 16))
    for p in range(k // 512):
        a[p, :8] = np.random.permutation(np.resize(levels, 8))
        for g in range(8):
            far = levels[np.abs(levels - a[p, g]) >= 10]
            a[p, g + 8] = far[np.random.randint(len(far))]
    return np.exp2(a.ravel()).repeat(32)


def f64(x):
    return np.asarray(x).astype(np.float64)


def striped(idx):
    return np.tile(idx.reshape(-1, 16).T, (8, 1)).astype(np.uint16)


def unstriped(offs):
    return offs[:16].T.reshape(-1).astype(np.int64)


E2M1 = np.array([0.0, 0.5, 1.0, 1.5, 2.0, 3.0, 4.0, 6.0, -0.0, -0.5, -1.0, -1.5, -2.0, -3.0, -4.0, -6.0])


def pack_weight(w, fmt):
    k, n = w.shape
    w = f64(np.asarray(w, np.float32).astype(ml_dtypes.bfloat16)).reshape(k // 32, 32, n)
    amax = np.abs(w).max(1)
    if fmt == "e4m3":
        byte = np.frexp(amax)[1] - 1 + 127 - 7
    else:
        mant, ex = np.frexp(amax / 6.0)
        byte = np.where(mant > 0.5, ex, ex - 1) + 127
    byte = np.clip(np.where(amax > 0, byte, 1), 1, 254)
    scaled = (w * np.exp2(127.0 - byte)[:, None, :]).reshape(k, n).astype(np.float32)
    by_word = np.ascontiguousarray(scaled.reshape(k // 512, 128, 4, n).transpose(0, 1, 3, 2))
    if fmt == "e4m3":
        words = by_word.astype(ml_dtypes.float8_e4m3fn).view(np.uint8)
    else:
        c = by_word.astype(ml_dtypes.float4_e2m1fn).view(np.uint8) & 0xF
        words = (c[..., 0::2] | (c[..., 1::2] << 4)).reshape(k // 512, 128, 2 * n)
    return np.ascontiguousarray(words), np.ascontiguousarray(byte.astype(np.uint8).reshape(k // 512, 16, n))


def unpack_weight(words, scales, fmt):
    g, _, n = scales.shape
    words = np.ascontiguousarray(words).reshape(g, 128, n, -1)
    if fmt == "e4m3":
        vals = words.view(ml_dtypes.float8_e4m3fn).astype(np.float64)
    else:
        nib = np.empty((g, 128, n, 4), np.uint8)
        nib[..., 0::2] = words & 0xF
        nib[..., 1::2] = words >> 4
        vals = E2M1[nib]
    vals = vals * np.repeat(np.exp2(scales.astype(np.float64) - 127.0), 8, axis=1)[..., None]
    return vals.transpose(0, 1, 3, 2).reshape(g * 512, n)


def gelu(v):
    return 0.5 * v * (1.0 + np.tanh(np.sqrt(2.0 / np.pi) * (v + 0.044715 * v**3)))


K, K2, H, T, T2, S = 1024, 512, 1024, 2048, 2048, 1024

def setup_inputs():
    n = np.random.standard_normal
    s = mx_kscale(K)[:, None]
    s2 = mx_kscale(K2)[:, None]
    u = mx_kscale(H)[:, None]
    tab_words, tab_scales = pack_weight(n((K, T)) * s, "e4m3")
    w1_words, w1_scales = pack_weight(n((K, H)) / np.sqrt(K) * u.T / s, "e2m1")
    w3_words, w3_scales = pack_weight(1.5 * n((H, H)) / np.sqrt(H) / u, "e4m3")
    xT = np.round(16 * n((K2, T2))) / 16 * s2
    wl = n((K2, H)) / np.sqrt(K2) / s2
    dec = np.random.uniform(0.3, 1.0, H) / u[:, 0]
    return {
        "tab_words": tab_words, "tab_scales": tab_scales,
        "offs": striped(np.random.permutation(T)[:S]),
        "xT": xT.astype(np.float32),
        "offs2": striped(np.random.permutation(T2)[:S]),
        "offs3": striped(np.random.permutation(T2)[:S]),
        "w1_words": w1_words, "w1_scales": w1_scales,
        "wl": wl.astype(np.float32),
        "w3_words": w3_words, "w3_scales": w3_scales,
        "dec": dec.astype(np.float32),
    }

def reference(tab_words, tab_scales, offs, xT, offs2, offs3, w1_words, w1_scales, wl, w3_words, w3_scales, dec):
    v = unpack_weight(tab_words, tab_scales, "e4m3")[:, unstriped(offs)]
    w1 = unpack_weight(w1_words, w1_scales, "e2m1")
    w3 = unpack_weight(w3_words, w3_scales, "e4m3")
    x = f64(xT)[:, unstriped(offs2)] + f64(xT)[:, unstriped(offs3)]
    a = w1.T @ v
    b = mxq(f64(wl), 0, "e4m3").T @ mxq(x, 0, "e4m3")
    b2 = np.square(b)
    h = b2 / (b2 + 1.0) * a
    y = w3.T @ mxq(h, 0, "e4m3")
    return y - f64(dec)[:, None] * a

@@ -1,0 +1,237 @@
+from contextlib import ExitStack
+
+import concourse.mybir as mybir
+
+K, K2, H, T, S = 1024, 512, 1024, 2048, 1024
+FLOPS = 2 * S * H * (K + K2 + H)
+
+F32 = mybir.dt.float32
+BF16 = mybir.dt.bfloat16
+I32 = mybir.dt.int32
+U32 = mybir.dt.uint32
+U16 = mybir.dt.uint16
+U8 = mybir.dt.uint8
+FP8X4 = mybir.dt.float8_e4m3fn_x4
+FP4X4 = mybir.dt.float4_e2m1fn_x4
+ACT = mybir.ActivationFunctionType
+ALU = mybir.AluOpType
+
+P = 128
+Q = 256
+HALF = 512
+X_HALVES = ((512, (0, 256), 3, ("ga", "gb")), (0, (256, 0), 2, ("wb0", "wb1")))
+Y_CHUNKS = ((0, 512), (512, 256), (768, 256))
+TINY = 2.0 ** -60
+
+
+def tile_list_carbon_flux_features_kernel(
+    tc, tab_words, tab_scales, offs, xT, offs2, offs3, w1_words, w1_scales, wl, w3_words, w3_scales, dec, out
+):
+    nc = tc.nc
+    with ExitStack() as ctx:
+        keep = ctx.enter_context(tc.tile_pool(name="keep", bufs=1))
+        ring = ctx.enter_context(tc.tile_pool(name="ring", bufs=2))
+        psum = ctx.enter_context(tc.psum_pool(name="psum", bufs=1))
+
+        def held(shape, dtype, name, tag=""):
+            return keep.tile(shape, dtype, name=name, tag=tag or name, align_bytes=64)
+
+        o1 = held([P, S // 16], U16, "o1")
+        o2 = held([P, S // 16], U16, "o2")
+        o3 = held([P, S // 16], U16, "o3")
+        planes = [held([P, T], F32, f"plane{i}") for i in range(4)]
+        wraw = [held([P, 4, HALF], F32, f"wraw{b}") for b in range(2)]
+        tabw = [held([P, T], U32, f"tabw{a}") for a in range(2)]
+        tabs = held([P, T], U8, "tabs")
+        wsraw = held([P, H], U8, "wsraw")
+        w1raw = held([P, 2, 2 * H], U8, "w1raw")
+        w3raw = held([P, 2, H], I32, "w3raw")
+        dect = held([P, 2, 4], F32, "dect")
+        vs1 = held([P, S], U8, "vs1")
+        ws1 = held([P, H], U8, "ws1")
+        warm = held([P, 8], F32, "warm")
+        warm2 = held([P, 8], F32, "warm2")
+
+        nc.vector.memset(warm[:], 1.0)
+        nc.scalar.activation(warm2[:], warm[:], ACT.Ln)
+        for t8 in (tabs, wsraw, vs1, ws1):
+            nc.vector.memset(t8[:].bitcast(I32), 0)
+
+        xv = xT.rearrange("(p i) t -> p i t", i=4)
+        wv = wl.rearrange("(p i) r -> p i r", i=4)
+        nc.sync.dma_start(o2[:], offs2)
+        nc.sync.dma_start(o3[:], offs3)
+        for i in range(4):
+            nc.sync.dma_start(planes[i][:], xv[:, i, :])
+        for b in range(2):
+            nc.sync.dma_start(wraw[b][:], wv[:, :, b * HALF:(b + 1) * HALF])
+        nc.sync.dma_start(o1[:], offs)
+        for qd in range(4):
+            rows = slice(4 * qd, 4 * qd + 4)
+            nc.sync.dma_start(tabs[32 * qd:32 * qd + 8, :].bitcast(I32), tab_scales[:, rows, :].bitcast(I32))
+            nc.sync.dma_start(wsraw[32 * qd:32 * qd + 8, :].bitcast(I32), w1_scales[:, rows, :].bitcast(I32))
+            nc.sync.dma_start(wsraw[32 * qd + 8:32 * qd + 16, :].bitcast(I32), w3_scales[:, rows, :].bitcast(I32))
+        nc.sync.dma_start(w1raw[:].bitcast(I32), w1_words.rearrange("a p n -> p a n").bitcast(I32))
+        for a in range(2):
+            nc.sync.dma_start(tabw[a][:].bitcast(I32), tab_words[a].rearrange("p t i -> p (t i)").bitcast(I32))
+        nc.sync.dma_start(dect[:], dec.rearrange("(b p t) -> p b t", b=2, t=4))
+        nc.sync.dma_start(w3raw[:], w3_words.rearrange("a p n i -> p a (n i)").bitcast(I32))
+
+        wq = [held([P, HALF], U32, f"wq{b}") for b in range(2)]
+        wqs = [held([P, HALF], U8, f"wqs{b}") for b in range(2)]
+        for b in range(2):
+            wb = held([P, 4 * HALF], BF16, f"wb{b}")
+            nc.scalar.copy(
+                wb[:].rearrange("p (t m i) -> p m i t", t=4, i=4),
+                wraw[b][:].rearrange("p i (m t) -> p m i t", t=4),
+            )
+            nc.vector.quantize_mx(out=wq[b][:].bitcast(FP8X4), scales=wqs[b][:], in_=wb[:])
+
+        logs = {}
+        for j0, quarters, wide, (tag2, tag3) in X_HALVES:
+            g2 = held([P, 4, HALF], F32, f"g2_{j0}", tag2)
+            g3 = held([P, 4, HALF], F32, f"g3_{j0}", tag3)
+
+            def gather(i, lo, n):
+                cols = slice((j0 + lo) // 16, (j0 + lo + n) // 16)
+                nc.vector.tensor_copy(g2[:, i, lo:lo + n], planes[i][:].indirect(o2[:, cols]))
+                nc.vector.tensor_copy(g3[:, i, lo:lo + n], planes[i][:].indirect(o3[:, cols]))
+
+            for i in range(wide):
+                gather(i, 0, HALF)
+            for jq in quarters:
+                for i in range(wide, 4):
+                    gather(i, jq, Q)
+                xb = ring.tile([P, 4 * Q], BF16, name="xb", tag="xb", align_bytes=64)
+                nc.vector.tensor_tensor(
+                    xb[:].rearrange("p (c e i) -> p c i e", e=4, i=4),
+                    g2[:, :, jq:jq + Q].rearrange("p i (c e) -> p c i e", e=4),
+                    g3[:, :, jq:jq + Q].rearrange("p i (c e) -> p c i e", e=4),
+                    ALU.add,
+                )
+                xq = held([P, Q], U32, f"xq{j0 + jq}")
+                xqs = held([P, Q], U8, f"xqs{j0 + jq}")
+                nc.vector.quantize_mx(out=xq[:].bitcast(FP8X4), scales=xqs[:], in_=xb[:])
+                for b in ((1, 0) if j0 + jq == 0 else (0, 1)):
+                    mag = ring.tile([P, Q // 4, 4, 4], F32, name="mag", tag="act", align_bytes=64)
+                    for tp in range(2):
+                        bank = psum.tile([P, 2, Q], F32, name="bank", tag="ab", bufs=4)
+                        for u in range(2):
+                            t = 2 * tp + u
+                            nc.tensor.matmul_mx(
+                                out=bank[:, u, :],
+                                lhsT=wq[b][:, t * P:(t + 1) * P].bitcast(FP8X4),
+                                lhsT_scale=wqs[b][:, t * P:(t + 1) * P],
+                                rhs=xq[:].bitcast(FP8X4),
+                                rhs_scale=xqs[:],
+                                start=True,
+                                stop=True,
+                            )
+                        nc.scalar.activation(
+                            mag[:, :, 2 * tp:2 * tp + 2, :],
+                            bank[:].rearrange("p u (c e) -> p c u e", e=4),
+                            ACT.Abs,
+                        )
+                    lg = held([P, 4 * Q], F32, f"lg{b}_{j0 + jq}")
+                    nc.scalar.activation(lg[:], mag[:].rearrange("p c t e -> p (c t e)"), ACT.Ln, bias=TINY)
+                    logs[b, (j0 + jq) // Q] = lg
+
+        wsp = held([P, H], U8, "wsp")
+        nc.vector.tensor_copy(
+            wsp[:].rearrange("p (b t c e) -> p b c t e", b=2, t=4, e=16),
+            wsraw[:].rearrange("p (b c e t) -> p b c t e", b=2, t=4, e=16),
+        )
+        nc.sync.dma_start(ws1[0:P - 4, :].bitcast(I32), wsp[4:P, :].bitcast(I32))
+        vs0 = held([P, S], U8, "vs0")
+        nc.vector.tensor_copy(vs0[:], tabs[:].indirect(o1[:]))
+        nc.sync.dma_start(vs1[0:P - 4, :].bitcast(I32), vs0[4:P, :].bitcast(I32))
+        w1p = held([P, 4, 2 * HALF], U8, "w1p")
+        nc.vector.tensor_copy(
+            w1p[:].bitcast(U16).rearrange("p g (t c e) -> p g c t e", t=4, e=8),
+            w1raw[:].bitcast(U16).rearrange("p a (b c e t) -> p (a b) c t e", b=2, t=4, e=8),
+        )
+        vw = {}
+        for hf in range(2):
+            for a in range(2):
+                vw[a, hf] = held([P, HALF], U32, f"vw{a}_{hf}")
+                nc.vector.tensor_copy(vw[a, hf][:], tabw[a][:].indirect(o1[:, hf * 32:(hf + 1) * 32]))
+        w3p = held([P, 4, HALF], I32, "w3p")
+        nc.vector.tensor_copy(
+            w3p[:].rearrange("p g (t c e) -> p g c t e", t=4, e=4),
+            w3raw[:].rearrange("p a (b c e t) -> p (a b) c t e", b=2, t=4, e=4),
+        )
+        ndec = held([P, 2, 4], F32, "ndec")
+        nc.vector.tensor_scalar_mul(ndec[:], dect[:], -1.0)
+        w1_scale = (wsp, ws1)
+        v_scale = (vs0, vs1)
+
+        asb = {}
+
+        def make_a(b, hf):
+            asb[b, hf] = held([P, HALF // 4, 4, 4], F32, f"asb{b}_{hf}", (f"wraw{b}", ("ga", "gb")[b])[hf])
+            for t in range(4):
+                bank = psum.tile([P, HALF], F32, name="bank", tag="ab", bufs=4)
+                for a in range(2):
+                    nc.tensor.matmul_mx(
+                        out=bank[:],
+                        lhsT=w1p[:, 2 * a + b, 2 * t * P:2 * (t + 1) * P].bitcast(FP4X4),
+                        lhsT_scale=w1_scale[a][:, b * HALF + t * P:b * HALF + (t + 1) * P],
+                        rhs=vw[a, hf][:].bitcast(FP8X4),
+                        rhs_scale=v_scale[a][:, hf * HALF:(hf + 1) * HALF],
+                        start=(a == 0),
+                        stop=(a == 1),
+                    )
+                nc.scalar.copy(asb[b, hf][:, :, t, :], bank[:].rearrange("p (c e) -> p c e", e=4))
+
+        def make_gate(b, q):
+            gate = ring.tile([P, 4 * Q], F32, name="gate", tag="act", align_bytes=64)
+            nc.scalar.activation(gate[:], logs[b, q][:], ACT.Sigmoid, scale=2.0)
+            return gate
+
+        def make_h(b, q, gate, codes, scales):
+            hb = ring.tile([P, 4 * Q], BF16, name="hb", tag="hb", align_bytes=64)
+            c0 = (q % 2) * (Q // 4)
+            nc.vector.tensor_tensor(
+                hb[:].rearrange("p (c e t) -> p c t e", e=4, t=4),
+                asb[b, q // 2][:, c0:c0 + Q // 4, :, :],
+                gate[:].rearrange("p (c t e) -> p c t e", e=4, t=4),
+                ALU.mult,
+            )
+            nc.vector.quantize_mx(out=codes.bitcast(FP8X4), scales=scales, in_=hb[:])
+
+        ov = out.rearrange("(b p t) j -> b p t j", b=2, t=4)
+        for j0, n in Y_CHUNKS:
+            hq = [held([P, n], U32, f"hq{b}_{j0}") for b in range(2)]
+            hs = [held([P, n], U8, f"hs{b}_{j0}") for b in range(2)]
+            for b in range(2):
+                gates = [make_gate(b, (j0 + jq) // Q) for jq in range(0, n, Q)]
+                if j0 % HALF == 0:
+                    make_a(b, j0 // HALF)
+                for jq in range(0, n, Q):
+                    make_h(b, (j0 + jq) // Q, gates[jq // Q], hq[b][:, jq:jq + Q], hs[b][:, jq:jq + Q])
+
+            c0 = (j0 % HALF) // 4
+            for nb in range(2):
+                res = ring.tile([P, 4, n], F32, name="res", tag="res", align_bytes=64)
+                for t in range(4):
+                    ybank = psum.tile([P, n], F32, name="ybank", tag="y", bufs=4)
+                    for b in range(2):
+                        nc.tensor.matmul_mx(
+                            out=ybank[:],
+                            lhsT=w3p[:, 2 * b + nb, t * P:(t + 1) * P].bitcast(FP8X4),
+                            lhsT_scale=wsp[8 + 4 * b:P, nb * HALF + t * P:nb * HALF + (t + 1) * P],
+                            rhs=hq[b][:].bitcast(FP8X4),
+                            rhs_scale=hs[b][:],
+                            start=(b == 0),
+                            stop=(b == 1),
+                        )
+                    nc.vector.scalar_tensor_tensor(
+                        res[:, t, :].rearrange("p (c e) -> p c e", e=4),
+                        asb[nb, j0 // HALF][:, c0:c0 + n // 4, t, :],
+                        ndec[:, nb, t:t + 1],
+                        ybank[:].rearrange("p (c e) -> p c e", e=4),
+                        ALU.mult,
+                        ALU.add,
+                    )
+                    if t % 2 == 1:
+                        nc.sync.dma_start(ov[nb, :, t - 1:t + 1, j0:j0 + n], res[:, t - 1:t + 1, :])

@@ -82,8 +82,8 @@ def tile_list_carbon_flux_features_kernel(
         for b in range(2):
             wb = held([P, 4 * HALF], BF16, f"wb{b}")
             nc.scalar.copy(
-                wb[:].rearrange("p (t m i) -> p m i t", t=4, i=4),
-                wraw[b][:].rearrange("p i (m t) -> p m i t", t=4),
+                wb[:].rearrange("p (t m i) -> p m t i", t=4, i=4),
+                wraw[b][:].rearrange("p i (m t) -> p m t i", t=4),
             )
             nc.vector.quantize_mx(out=wq[b][:].bitcast(FP8X4), scales=wqs[b][:], in_=wb[:])
 
@@ -102,115 +102,108 @@ def tile_list_carbon_flux_features_kernel(
             for jq in quarters:
                 for i in range(wide, 4):
                     gather(i, jq, Q)
-                xb = ring.tile([P, 4 * Q], BF16, name="xb", tag="xb", align_bytes=64)
+                xb = held([P, 4 * Q], BF16, f"xb{j0 + jq}", "xb")
                 nc.vector.tensor_tensor(
-                    xb[:].rearrange("p (c e i) -> p c i e", e=4, i=4),
-                    g2[:, :, jq:jq + Q].rearrange("p i (c e) -> p c i e", e=4),
-                    g3[:, :, jq:jq + Q].rearrange("p i (c e) -> p c i e", e=4),
+                    xb[:].rearrange("p (c e i) -> p c i e", e=2, i=4),
+                    g2[:, :, jq:jq + Q].rearrange("p i (c e) -> p c i e", e=2),
+                    g3[:, :, jq:jq + Q].rearrange("p i (c e) -> p c i e", e=2),
                     ALU.add,
                 )
                 xq = held([P, Q], U32, f"xq{j0 + jq}")
                 xqs = held([P, Q], U8, f"xqs{j0 + jq}")
                 nc.vector.quantize_mx(out=xq[:].bitcast(FP8X4), scales=xqs[:], in_=xb[:])
                 for b in ((1, 0) if j0 + jq == 0 else (0, 1)):
-                    mag = ring.tile([P, Q // 4, 4, 4], F32, name="mag", tag="act", align_bytes=64)
-                    for tp in range(2):
-                        bank = psum.tile([P, 2, Q], F32, name="bank", tag="ab", bufs=4)
-                        for u in range(2):
-                            t = 2 * tp + u
+                    mag = ring.tile([P, 4 * Q], F32, name="mag", tag="act", align_bytes=64)
+                    for jb in range(0, Q, P):
+                        bank = psum.tile([P, 4, P], F32, name="bank", tag="ab", bufs=4)
+                        for t in range(4):
                             nc.tensor.matmul_mx(
-                                out=bank[:, u, :],
+                                out=bank[:, t, :],
                                 lhsT=wq[b][:, t * P:(t + 1) * P].bitcast(FP8X4),
                                 lhsT_scale=wqs[b][:, t * P:(t + 1) * P],
-                                rhs=xq[:].bitcast(FP8X4),
-                                rhs_scale=xqs[:],
+                                rhs=xq[:, jb:jb + P].bitcast(FP8X4),
+                                rhs_scale=xqs[:, jb:jb + P],
                                 start=True,
                                 stop=True,
                             )
                         nc.scalar.activation(
-                            mag[:, :, 2 * tp:2 * tp + 2, :],
-                            bank[:].rearrange("p u (c e) -> p c u e", e=4),
+                            mag[:, 4 * jb:4 * (jb + P)].rearrange("p (j t) -> p j t", t=4),
+                            bank[:].rearrange("p t j -> p j t"),
                             ACT.Abs,
                         )
                     lg = held([P, 4 * Q], F32, f"lg{b}_{j0 + jq}")
-                    nc.scalar.activation(lg[:], mag[:].rearrange("p c t e -> p (c t e)"), ACT.Ln, bias=TINY)
+                    nc.scalar.activation(lg[:], mag[:], ACT.Ln, bias=TINY)
                     logs[b, (j0 + jq) // Q] = lg
 
-        wsp = held([P, H], U8, "wsp")
+        wsp = held([P, H], U8, "wsp", "plane2")
         nc.vector.tensor_copy(
-            wsp[:].rearrange("p (b t c e) -> p b c t e", b=2, t=4, e=16),
-            wsraw[:].rearrange("p (b c e t) -> p b c t e", b=2, t=4, e=16),
+            wsp[:].rearrange("p (b t c e) -> p b c t e", b=2, t=4, e=8),
+            wsraw[:].rearrange("p (b c e t) -> p b c t e", b=2, t=4, e=8),
         )
         nc.sync.dma_start(ws1[0:P - 4, :].bitcast(I32), wsp[4:P, :].bitcast(I32))
-        vs0 = held([P, S], U8, "vs0")
+        vs0 = held([P, S], U8, "vs0", "xb")
         nc.vector.tensor_copy(vs0[:], tabs[:].indirect(o1[:]))
         nc.sync.dma_start(vs1[0:P - 4, :].bitcast(I32), vs0[4:P, :].bitcast(I32))
-        w1p = held([P, 4, 2 * HALF], U8, "w1p")
+        w1p = held([P, 4, 2 * HALF], U8, "w1p", "plane3")
         nc.vector.tensor_copy(
-            w1p[:].bitcast(U16).rearrange("p g (t c e) -> p g c t e", t=4, e=8),
-            w1raw[:].bitcast(U16).rearrange("p a (b c e t) -> p (a b) c t e", b=2, t=4, e=8),
+            w1p[:].bitcast(U16).rearrange("p g (t c e) -> p g c t e", t=4, e=4),
+            w1raw[:].bitcast(U16).rearrange("p a (b c e t) -> p (a b) c t e", b=2, t=4, e=4),
         )
-        vw = {}
+        vw = held([P, 2 * S], U32, "vw", "wb0")
         for hf in range(2):
             for a in range(2):
-                vw[a, hf] = held([P, HALF], U32, f"vw{a}_{hf}")
-                nc.vector.tensor_copy(vw[a, hf][:], tabw[a][:].indirect(o1[:, hf * 32:(hf + 1) * 32]))
-        w3p = held([P, 4, HALF], I32, "w3p")
+                lo = a * S + hf * HALF
+                nc.vector.tensor_copy(vw[:, lo:lo + HALF], tabw[a][:].indirect(o1[:, hf * 32:(hf + 1) * 32]))
+        w3p = held([P, 4, HALF], I32, "w3p", "wb1")
         nc.vector.tensor_copy(
-            w3p[:].rearrange("p g (t c e) -> p g c t e", t=4, e=4),
-            w3raw[:].rearrange("p a (b c e t) -> p (a b) c t e", b=2, t=4, e=4),
+            w3p[:].rearrange("p g (t c e) -> p g c t e", t=4, e=2),
+            w3raw[:].rearrange("p a (b c e t) -> p (a b) c t e", b=2, t=4, e=2),
         )
         ndec = held([P, 2, 4], F32, "ndec")
-        nc.vector.tensor_scalar_mul(ndec[:], dect[:], -1.0)
+        nc.gpsimd.tensor_scalar(ndec[:], dect[:], -1.0, 0.0, ALU.mult, ALU.add)
         w1_scale = (wsp, ws1)
         v_scale = (vs0, vs1)
 
         asb = {}
+        for hf in range(2):
+            for b in range(2):
+                asb[b, hf] = held([P, 4, HALF], F32, f"asb{b}_{hf}", (f"wraw{b}", ("ga", "gb")[b])[hf])
 
-        def make_a(b, hf):
-            asb[b, hf] = held([P, HALF // 4, 4, 4], F32, f"asb{b}_{hf}", (f"wraw{b}", ("ga", "gb")[b])[hf])
-            for t in range(4):
-                bank = psum.tile([P, HALF], F32, name="bank", tag="ab", bufs=4)
-                for a in range(2):
-                    nc.tensor.matmul_mx(
-                        out=bank[:],
-                        lhsT=w1p[:, 2 * a + b, 2 * t * P:2 * (t + 1) * P].bitcast(FP4X4),
-                        lhsT_scale=w1_scale[a][:, b * HALF + t * P:b * HALF + (t + 1) * P],
-                        rhs=vw[a, hf][:].bitcast(FP8X4),
-                        rhs_scale=v_scale[a][:, hf * HALF:(hf + 1) * HALF],
-                        start=(a == 0),
-                        stop=(a == 1),
-                    )
-                nc.scalar.copy(asb[b, hf][:, :, t, :], bank[:].rearrange("p (c e) -> p c e", e=4))
-
-        def make_gate(b, q):
+        def make_h(b, q, hb):
             gate = ring.tile([P, 4 * Q], F32, name="gate", tag="act", align_bytes=64)
             nc.scalar.activation(gate[:], logs[b, q][:], ACT.Sigmoid, scale=2.0)
-            return gate
-
-        def make_h(b, q, gate, codes, scales):
-            hb = ring.tile([P, 4 * Q], BF16, name="hb", tag="hb", align_bytes=64)
-            c0 = (q % 2) * (Q // 4)
-            nc.vector.tensor_tensor(
-                hb[:].rearrange("p (c e t) -> p c t e", e=4, t=4),
-                asb[b, q // 2][:, c0:c0 + Q // 4, :, :],
-                gate[:].rearrange("p (c t e) -> p c t e", e=4, t=4),
-                ALU.mult,
-            )
-            nc.vector.quantize_mx(out=codes.bitcast(FP8X4), scales=scales, in_=hb[:])
+            for jb in range(0, Q, P):
+                j = q * Q + jb
+                bank = psum.tile([P, 4, P], F32, name="bank", tag="ab", bufs=4)
+                for t in range(4):
+                    for a in range(2):
+                        nc.tensor.matmul_mx(
+                            out=bank[:, t, :],
+                            lhsT=w1p[:, 2 * a + b, 2 * t * P:2 * (t + 1) * P].bitcast(FP4X4),
+                            lhsT_scale=w1_scale[a][:, b * HALF + t * P:b * HALF + (t + 1) * P],
+                            rhs=vw[:, a * S + j:a * S + j + P].bitcast(FP8X4),
+                            rhs_scale=v_scale[a][:, j:j + P],
+                            start=(a == 0),
+                            stop=(a == 1),
+                        )
+                nc.vector.tensor_tensor(
+                    hb[:, 4 * jb:4 * (jb + P)].rearrange("p (j t) -> p j t", t=4),
+                    bank[:].rearrange("p t j -> p j t"),
+                    gate[:, 4 * jb:4 * (jb + P)].rearrange("p (j t) -> p j t", t=4),
+                    ALU.mult,
+                )
+                nc.scalar.copy(asb[b, j // HALF][:, :, j % HALF:j % HALF + P], bank[:])
 
         ov = out.rearrange("(b p t) j -> b p t j", b=2, t=4)
         for j0, n in Y_CHUNKS:
             hq = [held([P, n], U32, f"hq{b}_{j0}") for b in range(2)]
             hs = [held([P, n], U8, f"hs{b}_{j0}") for b in range(2)]
             for b in range(2):
-                gates = [make_gate(b, (j0 + jq) // Q) for jq in range(0, n, Q)]
-                if j0 % HALF == 0:
-                    make_a(b, j0 // HALF)
+                hb = ring.tile([P, 4 * n], BF16, name="hb", tag="hb", align_bytes=64)
                 for jq in range(0, n, Q):
-                    make_h(b, (j0 + jq) // Q, gates[jq // Q], hq[b][:, jq:jq + Q], hs[b][:, jq:jq + Q])
-
-            c0 = (j0 % HALF) // 4
+                    make_h(b, (j0 + jq) // Q, hb[:, 4 * jq:4 * (jq + Q)])
+                nc.vector.quantize_mx(out=hq[b][:].bitcast(FP8X4), scales=hs[b][:], in_=hb[:])
+            c0 = j0 % HALF
             for nb in range(2):
                 res = ring.tile([P, 4, n], F32, name="res", tag="res", align_bytes=64)
                 for t in range(4):
@@ -226,10 +219,10 @@ def tile_list_carbon_flux_features_kernel(
                             stop=(b == 1),
                         )
                     nc.vector.scalar_tensor_tensor(
-                        res[:, t, :].rearrange("p (c e) -> p c e", e=4),
-                        asb[nb, j0 // HALF][:, c0:c0 + n // 4, t, :],
+                        res[:, t, :],
+                        asb[nb, j0 // HALF][:, t, c0:c0 + n],
                         ndec[:, nb, t:t + 1],
-                        ybank[:].rearrange("p (c e) -> p c e", e=4),
+                        ybank[:],
                         ALU.mult,
                         ALU.add,
                     )

@@ -17,10 +17,10 @@ ACT = mybir.ActivationFunctionType
 ALU = mybir.AluOpType
 
 P = 128
-Q = 256
 HALF = 512
-X_HALVES = ((512, (0, 256), 3, ("ga", "gb")), (0, (256, 0), 2, ("wb0", "wb1")))
-Y_CHUNKS = ((0, 512), (512, 256), (768, 256))
+QUARTER = 256
+PER_COLUMN = 16
+BANKS = 4
 TINY = 2.0 ** -60
 
 
@@ -31,200 +31,225 @@ def tile_list_carbon_flux_features_kernel(
     with ExitStack() as ctx:
         keep = ctx.enter_context(tc.tile_pool(name="keep", bufs=1))
         ring = ctx.enter_context(tc.tile_pool(name="ring", bufs=2))
-        psum = ctx.enter_context(tc.psum_pool(name="psum", bufs=1))
+        psum = ctx.enter_context(tc.psum_pool(name="psum", bufs=BANKS))
 
         def held(shape, dtype, name, tag=""):
             return keep.tile(shape, dtype, name=name, tag=tag or name, align_bytes=64)
 
-        o1 = held([P, S // 16], U16, "o1")
-        o2 = held([P, S // 16], U16, "o2")
-        o3 = held([P, S // 16], U16, "o3")
-        planes = [held([P, T], F32, f"plane{i}") for i in range(4)]
-        wraw = [held([P, 4, HALF], F32, f"wraw{b}") for b in range(2)]
-        tabw = [held([P, T], U32, f"tabw{a}") for a in range(2)]
-        tabs = held([P, T], U8, "tabs")
-        wsraw = held([P, H], U8, "wsraw")
-        w1raw = held([P, 2, 2 * H], U8, "w1raw")
-        w3raw = held([P, 2, H], I32, "w3raw")
-        dect = held([P, 2, 4], F32, "dect")
-        vs1 = held([P, S], U8, "vs1")
-        ws1 = held([P, H], U8, "ws1")
+        def entries(list_tile, j, n):
+            return list_tile[:, j // PER_COLUMN:(j + n) // PER_COLUMN]
+
+        list1 = held([P, S // PER_COLUMN], U16, "list1")
+        list2 = held([P, S // PER_COLUMN], U16, "list2")
+        list3 = held([P, S // PER_COLUMN], U16, "list3")
+        x_rows = [held([P, T], F32, f"x_rows{i}") for i in range(4)]
+        wl_raw = [held([P, 4, HALF], F32, f"wl_raw{b}") for b in range(2)]
+        tab_w = [held([P, T], U32, f"tab_w{g}") for g in range(2)]
+        tab_s = held([P, T], U8, "tab_s")
+        w_s_raw = held([P, H], U8, "w_s_raw")
+        w1_raw = held([P, 2, 2 * H], U8, "w1_raw")
+        w3_raw = held([P, 2, H], I32, "w3_raw")
+        dec_rows = held([P, 2, 4], F32, "dec_rows")
+        v_s1 = held([P, S], U8, "v_s1")
+        w1_s1 = held([P, H], U8, "w1_s1")
+
+        one = held([P, 8], F32, "one")
         warm = held([P, 8], F32, "warm")
-        warm2 = held([P, 8], F32, "warm2")
+        nc.vector.memset(one[:], 1.0)
+        nc.scalar.activation(warm[:], one[:], ACT.Ln)
+        for scale_tile in (tab_s, w_s_raw, v_s1, w1_s1):
+            nc.vector.memset(scale_tile[:].bitcast(I32), 0)
 
-        nc.vector.memset(warm[:], 1.0)
-        nc.scalar.activation(warm2[:], warm[:], ACT.Ln)
-        for t8 in (tabs, wsraw, vs1, ws1):
-            nc.vector.memset(t8[:].bitcast(I32), 0)
-
-        xv = xT.rearrange("(p i) t -> p i t", i=4)
-        wv = wl.rearrange("(p i) r -> p i r", i=4)
-        nc.sync.dma_start(o2[:], offs2)
-        nc.sync.dma_start(o3[:], offs3)
+        x_view = xT.rearrange("(p i) t -> p i t", i=4)
+        wl_view = wl.rearrange("(p i) r -> p i r", i=4)
+        nc.sync.dma_start(list2[:], offs2)
+        nc.sync.dma_start(list3[:], offs3)
         for i in range(4):
-            nc.sync.dma_start(planes[i][:], xv[:, i, :])
+            nc.sync.dma_start(x_rows[i][:], x_view[:, i, :])
         for b in range(2):
-            nc.sync.dma_start(wraw[b][:], wv[:, :, b * HALF:(b + 1) * HALF])
-        nc.sync.dma_start(o1[:], offs)
-        for qd in range(4):
-            rows = slice(4 * qd, 4 * qd + 4)
-            nc.sync.dma_start(tabs[32 * qd:32 * qd + 8, :].bitcast(I32), tab_scales[:, rows, :].bitcast(I32))
-            nc.sync.dma_start(wsraw[32 * qd:32 * qd + 8, :].bitcast(I32), w1_scales[:, rows, :].bitcast(I32))
-            nc.sync.dma_start(wsraw[32 * qd + 8:32 * qd + 16, :].bitcast(I32), w3_scales[:, rows, :].bitcast(I32))
-        nc.sync.dma_start(w1raw[:].bitcast(I32), w1_words.rearrange("a p n -> p a n").bitcast(I32))
-        for a in range(2):
-            nc.sync.dma_start(tabw[a][:].bitcast(I32), tab_words[a].rearrange("p t i -> p (t i)").bitcast(I32))
-        nc.sync.dma_start(dect[:], dec.rearrange("(b p t) -> p b t", b=2, t=4))
-        nc.sync.dma_start(w3raw[:], w3_words.rearrange("a p n i -> p a (n i)").bitcast(I32))
+            nc.sync.dma_start(wl_raw[b][:], wl_view[:, :, b * HALF:(b + 1) * HALF])
+        nc.sync.dma_start(list1[:], offs)
+        for d in range(4):
+            rows = slice(4 * d, 4 * d + 4)
+            nc.sync.dma_start(tab_s[32 * d:32 * d + 8, :].bitcast(I32), tab_scales[:, rows, :].bitcast(I32))
+            nc.sync.dma_start(w_s_raw[32 * d:32 * d + 8, :].bitcast(I32), w1_scales[:, rows, :].bitcast(I32))
+            nc.sync.dma_start(w_s_raw[32 * d + 8:32 * d + 16, :].bitcast(I32), w3_scales[:, rows, :].bitcast(I32))
+        nc.sync.dma_start(w1_raw[:].bitcast(I32), w1_words.rearrange("g p n -> p g n").bitcast(I32))
+        for g in range(2):
+            nc.sync.dma_start(tab_w[g][:].bitcast(I32), tab_words[g].rearrange("p t i -> p (t i)").bitcast(I32))
+        nc.sync.dma_start(dec_rows[:], dec.rearrange("(b p t) -> p b t", b=2, t=4))
+        nc.sync.dma_start(w3_raw[:], w3_words.rearrange("g p n i -> p g (n i)").bitcast(I32))
 
-        wq = [held([P, HALF], U32, f"wq{b}") for b in range(2)]
-        wqs = [held([P, HALF], U8, f"wqs{b}") for b in range(2)]
+        wl_q = [held([P, HALF], U32, f"wl_q{b}") for b in range(2)]
+        wl_s = [held([P, HALF], U8, f"wl_s{b}") for b in range(2)]
         for b in range(2):
-            wb = held([P, 4 * HALF], BF16, f"wb{b}")
+            wl_bf = held([P, 4 * HALF], BF16, f"wl_bf{b}")
             nc.scalar.copy(
-                wb[:].rearrange("p (t m i) -> p m t i", t=4, i=4),
-                wraw[b][:].rearrange("p i (m t) -> p m t i", t=4),
+                wl_bf[:].rearrange("p (t c i) -> p c t i", t=4, i=4),
+                wl_raw[b][:].rearrange("p i (c t) -> p c t i", t=4),
             )
-            nc.vector.quantize_mx(out=wq[b][:].bitcast(FP8X4), scales=wqs[b][:], in_=wb[:])
+            nc.vector.quantize_mx(out=wl_q[b][:].bitcast(FP8X4), scales=wl_s[b][:], in_=wl_bf[:])
 
-        logs = {}
-        for j0, quarters, wide, (tag2, tag3) in X_HALVES:
-            g2 = held([P, 4, HALF], F32, f"g2_{j0}", tag2)
-            g3 = held([P, 4, HALF], F32, f"g3_{j0}", tag3)
+        log_b = {}
 
-            def gather(i, lo, n):
-                cols = slice((j0 + lo) // 16, (j0 + lo + n) // 16)
-                nc.vector.tensor_copy(g2[:, i, lo:lo + n], planes[i][:].indirect(o2[:, cols]))
-                nc.vector.tensor_copy(g3[:, i, lo:lo + n], planes[i][:].indirect(o3[:, cols]))
-
-            for i in range(wide):
-                gather(i, 0, HALF)
-            for jq in quarters:
-                for i in range(wide, 4):
-                    gather(i, jq, Q)
-                xb = held([P, 4 * Q], BF16, f"xb{j0 + jq}", "xb")
-                nc.vector.tensor_tensor(
-                    xb[:].rearrange("p (c e i) -> p c i e", e=2, i=4),
-                    g2[:, :, jq:jq + Q].rearrange("p i (c e) -> p c i e", e=2),
-                    g3[:, :, jq:jq + Q].rearrange("p i (c e) -> p c i e", e=2),
-                    ALU.add,
-                )
-                xq = held([P, Q], U32, f"xq{j0 + jq}")
-                xqs = held([P, Q], U8, f"xqs{j0 + jq}")
-                nc.vector.quantize_mx(out=xq[:].bitcast(FP8X4), scales=xqs[:], in_=xb[:])
-                for b in ((1, 0) if j0 + jq == 0 else (0, 1)):
-                    mag = ring.tile([P, 4 * Q], F32, name="mag", tag="act", align_bytes=64)
-                    for jb in range(0, Q, P):
-                        bank = psum.tile([P, 4, P], F32, name="bank", tag="ab", bufs=4)
-                        for t in range(4):
-                            nc.tensor.matmul_mx(
-                                out=bank[:, t, :],
-                                lhsT=wq[b][:, t * P:(t + 1) * P].bitcast(FP8X4),
-                                lhsT_scale=wqs[b][:, t * P:(t + 1) * P],
-                                rhs=xq[:, jb:jb + P].bitcast(FP8X4),
-                                rhs_scale=xqs[:, jb:jb + P],
-                                start=True,
-                                stop=True,
-                            )
-                        nc.scalar.activation(
-                            mag[:, 4 * jb:4 * (jb + P)].rearrange("p (j t) -> p j t", t=4),
-                            bank[:].rearrange("p t j -> p j t"),
-                            ACT.Abs,
-                        )
-                    lg = held([P, 4 * Q], F32, f"lg{b}_{j0 + jq}")
-                    nc.scalar.activation(lg[:], mag[:], ACT.Ln, bias=TINY)
-                    logs[b, (j0 + jq) // Q] = lg
-
-        wsp = held([P, H], U8, "wsp", "plane2")
-        nc.vector.tensor_copy(
-            wsp[:].rearrange("p (b t c e) -> p b c t e", b=2, t=4, e=8),
-            wsraw[:].rearrange("p (b c e t) -> p b c t e", b=2, t=4, e=8),
-        )
-        nc.sync.dma_start(ws1[0:P - 4, :].bitcast(I32), wsp[4:P, :].bitcast(I32))
-        vs0 = held([P, S], U8, "vs0", "xb")
-        nc.vector.tensor_copy(vs0[:], tabs[:].indirect(o1[:]))
-        nc.sync.dma_start(vs1[0:P - 4, :].bitcast(I32), vs0[4:P, :].bitcast(I32))
-        w1p = held([P, 4, 2 * HALF], U8, "w1p", "plane3")
-        nc.vector.tensor_copy(
-            w1p[:].bitcast(U16).rearrange("p g (t c e) -> p g c t e", t=4, e=4),
-            w1raw[:].bitcast(U16).rearrange("p a (b c e t) -> p (a b) c t e", b=2, t=4, e=4),
-        )
-        vw = held([P, 2 * S], U32, "vw", "wb0")
-        for hf in range(2):
-            for a in range(2):
-                lo = a * S + hf * HALF
-                nc.vector.tensor_copy(vw[:, lo:lo + HALF], tabw[a][:].indirect(o1[:, hf * 32:(hf + 1) * 32]))
-        w3p = held([P, 4, HALF], I32, "w3p", "wb1")
-        nc.vector.tensor_copy(
-            w3p[:].rearrange("p g (t c e) -> p g c t e", t=4, e=2),
-            w3raw[:].rearrange("p a (b c e t) -> p (a b) c t e", b=2, t=4, e=2),
-        )
-        ndec = held([P, 2, 4], F32, "ndec")
-        nc.gpsimd.tensor_scalar(ndec[:], dect[:], -1.0, 0.0, ALU.mult, ALU.add)
-        w1_scale = (wsp, ws1)
-        v_scale = (vs0, vs1)
-
-        asb = {}
-        for hf in range(2):
+        def log_quarter(picked, j0, jq, x_tag):
+            j = j0 + jq
+            x_bf = held([P, 4 * QUARTER], BF16, f"x_bf{j}", x_tag)
+            nc.vector.tensor_tensor(
+                x_bf[:].rearrange("p (c e i) -> p c i e", e=2, i=4),
+                picked[:, 0, :, jq:jq + QUARTER].rearrange("p i (c e) -> p c i e", e=2),
+                picked[:, 1, :, jq:jq + QUARTER].rearrange("p i (c e) -> p c i e", e=2),
+                ALU.add,
+            )
+            x_q = held([P, QUARTER], U32, f"x_q{j}")
+            x_s = held([P, QUARTER], U8, f"x_s{j}")
+            nc.vector.quantize_mx(out=x_q[:].bitcast(FP8X4), scales=x_s[:], in_=x_bf[:])
+            abs_b = held([P, 2, 4 * QUARTER], F32, f"abs_b{j}", "odd_gate")
             for b in range(2):
-                asb[b, hf] = held([P, 4, HALF], F32, f"asb{b}_{hf}", (f"wraw{b}", ("ga", "gb")[b])[hf])
-
-        def make_h(b, q, hb):
-            gate = ring.tile([P, 4 * Q], F32, name="gate", tag="act", align_bytes=64)
-            nc.scalar.activation(gate[:], logs[b, q][:], ACT.Sigmoid, scale=2.0)
-            for jb in range(0, Q, P):
-                j = q * Q + jb
-                bank = psum.tile([P, 4, P], F32, name="bank", tag="ab", bufs=4)
-                for t in range(4):
-                    for a in range(2):
+                for jb in range(0, QUARTER, P):
+                    bank = psum.tile([P, 4, P], F32, name="bank", tag="a_or_b")
+                    for t in range(4):
                         nc.tensor.matmul_mx(
                             out=bank[:, t, :],
-                            lhsT=w1p[:, 2 * a + b, 2 * t * P:2 * (t + 1) * P].bitcast(FP4X4),
-                            lhsT_scale=w1_scale[a][:, b * HALF + t * P:b * HALF + (t + 1) * P],
-                            rhs=vw[:, a * S + j:a * S + j + P].bitcast(FP8X4),
-                            rhs_scale=v_scale[a][:, j:j + P],
-                            start=(a == 0),
-                            stop=(a == 1),
+                            lhsT=wl_q[b][:, t * P:(t + 1) * P].bitcast(FP8X4),
+                            lhsT_scale=wl_s[b][:, t * P:(t + 1) * P],
+                            rhs=x_q[:, jb:jb + P].bitcast(FP8X4),
+                            rhs_scale=x_s[:, jb:jb + P],
+                            start=True,
+                            stop=True,
+                        )
+                    nc.scalar.activation(
+                        abs_b[:, b, 4 * jb:4 * (jb + P)].rearrange("p (j t) -> p j t", t=4),
+                        bank[:].rearrange("p t j -> p j t"),
+                        ACT.Abs,
+                    )
+            log_b[j] = held([P, 2, 4 * QUARTER], F32, f"log_b{j}")
+            nc.scalar.activation(log_b[j][:], abs_b[:], ACT.Ln, bias=TINY)
+
+        def log_half(j0, picked_tag, whole_rows, quarters):
+            picked = held([P, 2, 4, HALF], F32, f"picked{j0}", picked_tag)
+
+            def gather(i, jq, n):
+                for side, list_tile in enumerate((list2, list3)):
+                    nc.vector.tensor_copy(
+                        picked[:, side, i, jq:jq + n], x_rows[i][:].indirect(entries(list_tile, j0 + jq, n))
+                    )
+
+            for i in range(whole_rows):
+                gather(i, 0, HALF)
+            for jq, x_tag in quarters:
+                for i in range(whole_rows, 4):
+                    gather(i, jq, QUARTER)
+                log_quarter(picked, j0, jq, x_tag)
+
+        log_half(HALF, "picked", 3, ((0, "x_bf"), (QUARTER, "wl_bf0")))
+        log_half(0, "wl_bf1", 1, ((QUARTER, "x_bf"), (0, "x_bf")))
+
+        w_s = held([P, H], U8, "w_s", "x_rows1")
+        nc.vector.tensor_copy(
+            w_s[:].rearrange("p (b t c e) -> p b c t e", b=2, t=4, e=8),
+            w_s_raw[:].rearrange("p (b c e t) -> p b c t e", b=2, t=4, e=8),
+        )
+        nc.sync.dma_start(w1_s1[0:P - 4, :].bitcast(I32), w_s[4:P, :].bitcast(I32))
+        v_s0 = held([P, S], U8, "v_s0", "x_bf")
+        nc.vector.tensor_copy(v_s0[:], tab_s[:].indirect(list1[:]))
+        nc.sync.dma_start(v_s1[0:P - 4, :].bitcast(I32), v_s0[4:P, :].bitcast(I32))
+        w1_q = held([P, 4, 2 * HALF], U8, "w1_q", "x_rows3")
+        nc.vector.tensor_copy(
+            w1_q[:].bitcast(U16).rearrange("p gb (t c e) -> p gb c t e", t=4, e=4),
+            w1_raw[:].bitcast(U16).rearrange("p g (b c e t) -> p (g b) c t e", b=2, t=4, e=4),
+        )
+        v_q = [held([P, 2, HALF], U32, f"v_q{half}", tag) for half, tag in enumerate(("wl_bf1", "w1_raw"))]
+
+        def gather_words(half):
+            for g in range(2):
+                nc.vector.tensor_copy(v_q[half][:, g, :], tab_w[g][:].indirect(entries(list1, half * HALF, HALF)))
+
+        gather_words(0)
+        w3_q = held([P, 4, HALF], I32, "w3_q", "x_rows2")
+        nc.vector.tensor_copy(
+            w3_q[:].rearrange("p gb (t c e) -> p gb c t e", t=4, e=2),
+            w3_raw[:].rearrange("p g (b c e t) -> p (g b) c t e", b=2, t=4, e=2),
+        )
+        gather_words(1)
+        minus_dec = held([P, 2, 4], F32, "minus_dec")
+        nc.gpsimd.tensor_scalar(minus_dec[:], dec_rows[:], -1.0, 0.0, ALU.mult, ALU.add)
+        w1_s = (w_s, w1_s1)
+        v_s = (v_s0, v_s1)
+
+        a_kept = [
+            [held([P, 4, HALF], F32, f"a_kept{half}{b}", tag) for b, tag in enumerate(tags)]
+            for half, tags in enumerate((("wl_raw0", "wl_raw1"), ("picked", "x_rows0")))
+        ]
+
+        def make_h(b, j0, gate, h_q, h_s):
+            h_bf = ring.tile([P, 4 * QUARTER], BF16, name="h_bf", align_bytes=64)
+            for jb in range(0, QUARTER, P):
+                j = j0 + jb
+                half, jh = divmod(j, HALF)
+                bank = psum.tile([P, 4, P], F32, name="bank", tag="a_or_b")
+                for t in range(4):
+                    for g in range(2):
+                        nc.tensor.matmul_mx(
+                            out=bank[:, t, :],
+                            lhsT=w1_q[:, 2 * g + b, 2 * t * P:2 * (t + 1) * P].bitcast(FP4X4),
+                            lhsT_scale=w1_s[g][:, b * HALF + t * P:b * HALF + (t + 1) * P],
+                            rhs=v_q[half][:, g, jh:jh + P].bitcast(FP8X4),
+                            rhs_scale=v_s[g][:, j:j + P],
+                            start=(g == 0),
+                            stop=(g == 1),
                         )
                 nc.vector.tensor_tensor(
-                    hb[:, 4 * jb:4 * (jb + P)].rearrange("p (j t) -> p j t", t=4),
+                    h_bf[:, 4 * jb:4 * (jb + P)].rearrange("p (j t) -> p j t", t=4),
                     bank[:].rearrange("p t j -> p j t"),
                     gate[:, 4 * jb:4 * (jb + P)].rearrange("p (j t) -> p j t", t=4),
                     ALU.mult,
                 )
-                nc.scalar.copy(asb[b, j // HALF][:, :, j % HALF:j % HALF + P], bank[:])
+                nc.scalar.copy(a_kept[half][b][:, :, jh:jh + P], bank[:])
+            nc.vector.quantize_mx(out=h_q[:].bitcast(FP8X4), scales=h_s[:], in_=h_bf[:])
 
-        ov = out.rearrange("(b p t) j -> b p t j", b=2, t=4)
-        for j0, n in Y_CHUNKS:
-            hq = [held([P, n], U32, f"hq{b}_{j0}") for b in range(2)]
-            hs = [held([P, n], U8, f"hs{b}_{j0}") for b in range(2)]
+        out_view = out.rearrange("(b p t) j -> b p t j", b=2, t=4)
+
+        def finish(j0, h_q, h_s):
+            half, jh = divmod(j0, HALF)
             for b in range(2):
-                hb = ring.tile([P, 4 * n], BF16, name="hb", tag="hb", align_bytes=64)
-                for jq in range(0, n, Q):
-                    make_h(b, (j0 + jq) // Q, hb[:, 4 * jq:4 * (jq + Q)])
-                nc.vector.quantize_mx(out=hq[b][:].bitcast(FP8X4), scales=hs[b][:], in_=hb[:])
-            c0 = j0 % HALF
-            for nb in range(2):
-                res = ring.tile([P, 4, n], F32, name="res", tag="res", align_bytes=64)
+                result = ring.tile([P, 4, QUARTER], F32, name="result", align_bytes=64)
                 for t in range(4):
-                    ybank = psum.tile([P, n], F32, name="ybank", tag="y", bufs=4)
-                    for b in range(2):
+                    y_bank = psum.tile([P, QUARTER], F32, name="y_bank")
+                    for g in range(2):
                         nc.tensor.matmul_mx(
-                            out=ybank[:],
-                            lhsT=w3p[:, 2 * b + nb, t * P:(t + 1) * P].bitcast(FP8X4),
-                            lhsT_scale=wsp[8 + 4 * b:P, nb * HALF + t * P:nb * HALF + (t + 1) * P],
-                            rhs=hq[b][:].bitcast(FP8X4),
-                            rhs_scale=hs[b][:],
-                            start=(b == 0),
-                            stop=(b == 1),
+                            out=y_bank[:],
+                            lhsT=w3_q[:, 2 * g + b, t * P:(t + 1) * P].bitcast(FP8X4),
+                            lhsT_scale=w_s[8 + 4 * g:P, b * HALF + t * P:b * HALF + (t + 1) * P],
+                            rhs=h_q[g][:].bitcast(FP8X4),
+                            rhs_scale=h_s[g][:],
+                            start=(g == 0),
+                            stop=(g == 1),
                         )
                     nc.vector.scalar_tensor_tensor(
-                        res[:, t, :],
-                        asb[nb, j0 // HALF][:, t, c0:c0 + n],
-                        ndec[:, nb, t:t + 1],
-                        ybank[:],
+                        result[:, t, :],
+                        a_kept[half][b][:, t, jh:jh + QUARTER],
+                        minus_dec[:, b, t:t + 1],
+                        y_bank[:],
                         ALU.mult,
                         ALU.add,
                     )
                     if t % 2 == 1:
-                        nc.sync.dma_start(ov[nb, :, t - 1:t + 1, j0:j0 + n], res[:, t - 1:t + 1, :])
+                        nc.sync.dma_start(out_view[b, :, t - 1:t + 1, j0:j0 + QUARTER], result[:, t - 1:t + 1, :])
+
+        unfinished = None
+        for j0 in range(0, S, QUARTER):
+            gate = held([P, 2, 4 * QUARTER], F32, f"gate{j0}", ("even_gate", "odd_gate")[j0 // QUARTER % 2])
+            h_q = [held([P, QUARTER], U32, f"h_q{b}_{j0}") for b in range(2)]
+            h_s = [held([P, QUARTER], U8, f"h_s{b}_{j0}") for b in range(2)]
+            if unfinished is None:
+                for b in range(2):
+                    nc.scalar.activation(gate[:, b, :], log_b[j0][:, b, :], ACT.Sigmoid, scale=2.0)
+                    make_h(b, j0, gate[:, b, :], h_q[b], h_s[b])
+            else:
+                nc.scalar.activation(gate[:], log_b[j0][:], ACT.Sigmoid, scale=2.0)
+                make_h(0, j0, gate[:, 0, :], h_q[0], h_s[0])
+                finish(*unfinished)
+                make_h(1, j0, gate[:, 1, :], h_q[1], h_s[1])
+            unfinished = (j0, h_q, h_s)
+        finish(*unfinished)

@@ -20,6 +20,7 @@ P = 128
 HALF = 512
 QUARTER = 256
 PER_COLUMN = 16
+WL_PIECE = 256
 BANKS = 4
 TINY = 2.0 ** -60
 
@@ -43,7 +44,7 @@ def tile_list_carbon_flux_features_kernel(
         list2 = held([P, S // PER_COLUMN], U16, "list2")
         list3 = held([P, S // PER_COLUMN], U16, "list3")
         x_rows = [held([P, T], F32, f"x_rows{i}") for i in range(4)]
-        wl_raw = [held([P, 4, HALF], F32, f"wl_raw{b}") for b in range(2)]
+        wl_raw = [held([P, 4, WL_PIECE], F32, f"wl_raw{n}") for n in range(H // WL_PIECE)]
         tab_w = [held([P, T], U32, f"tab_w{g}") for g in range(2)]
         tab_s = held([P, T], U8, "tab_s")
         w_s_raw = held([P, H], U8, "w_s_raw")
@@ -66,8 +67,8 @@ def tile_list_carbon_flux_features_kernel(
         nc.sync.dma_start(list3[:], offs3)
         for i in range(4):
             nc.sync.dma_start(x_rows[i][:], x_view[:, i, :])
-        for b in range(2):
-            nc.sync.dma_start(wl_raw[b][:], wl_view[:, :, b * HALF:(b + 1) * HALF])
+        for n, piece in enumerate(wl_raw):
+            nc.sync.dma_start(piece[:], wl_view[:, :, n * WL_PIECE:(n + 1) * WL_PIECE])
         nc.sync.dma_start(list1[:], offs)
         for d in range(4):
             rows = slice(4 * d, 4 * d + 4)
@@ -84,12 +85,15 @@ def tile_list_carbon_flux_features_kernel(
         wl_s = [held([P, HALF], U8, f"wl_s{b}") for b in range(2)]
         for b in range(2):
             wl_bf = held([P, 4 * HALF], BF16, f"wl_bf{b}")
-            nc.scalar.copy(
-                wl_bf[:].rearrange("p (t c i) -> p c t i", t=4, i=4),
-                wl_raw[b][:].rearrange("p i (c t) -> p c t i", t=4),
-            )
+            by_column = wl_bf[:].rearrange("p (t c i) -> p c t i", t=4, i=4)
+            for n in range(2):
+                nc.scalar.copy(
+                    by_column[:, n * WL_PIECE // 4:(n + 1) * WL_PIECE // 4],
+                    wl_raw[2 * b + n][:].rearrange("p i (c t) -> p c t i", t=4),
+                )
             nc.vector.quantize_mx(out=wl_q[b][:].bitcast(FP8X4), scales=wl_s[b][:], in_=wl_bf[:])
 
+        abs_b = held([P, 2, 4 * QUARTER], F32, "abs_b", "odd_gate")
         log_b = {}
 
         def log_quarter(picked, j0, jq, x_tag):
@@ -104,7 +108,6 @@ def tile_list_carbon_flux_features_kernel(
             x_q = held([P, QUARTER], U32, f"x_q{j}")
             x_s = held([P, QUARTER], U8, f"x_s{j}")
             nc.vector.quantize_mx(out=x_q[:].bitcast(FP8X4), scales=x_s[:], in_=x_bf[:])
-            abs_b = held([P, 2, 4 * QUARTER], F32, f"abs_b{j}", "odd_gate")
             for b in range(2):
                 for jb in range(0, QUARTER, P):
                     bank = psum.tile([P, 4, P], F32, name="bank", tag="a_or_b")
@@ -124,7 +127,8 @@ def tile_list_carbon_flux_features_kernel(
                         ACT.Abs,
                     )
             log_b[j] = held([P, 2, 4 * QUARTER], F32, f"log_b{j}")
-            nc.scalar.activation(log_b[j][:], abs_b[:], ACT.Ln, bias=TINY)
+            for b in range(2):
+                nc.scalar.activation(log_b[j][:, b, :], abs_b[:, b, :], ACT.Ln, bias=TINY)
 
         def log_half(j0, picked_tag, whole_rows, quarters):
             picked = held([P, 2, 4, HALF], F32, f"picked{j0}", picked_tag)
@@ -143,7 +147,7 @@ def tile_list_carbon_flux_features_kernel(
                 log_quarter(picked, j0, jq, x_tag)
 
         log_half(HALF, "picked", 3, ((0, "x_bf"), (QUARTER, "wl_bf0")))
-        log_half(0, "wl_bf1", 1, ((QUARTER, "x_bf"), (0, "x_bf")))
+        log_half(0, "wl_bf0", 1, ((QUARTER, "x_bf"), (0, "x_bf")))
 
         w_s = held([P, H], U8, "w_s", "x_rows1")
         nc.vector.tensor_copy(
@@ -159,7 +163,7 @@ def tile_list_carbon_flux_features_kernel(
             w1_q[:].bitcast(U16).rearrange("p gb (t c e) -> p gb c t e", t=4, e=4),
             w1_raw[:].bitcast(U16).rearrange("p g (b c e t) -> p (g b) c t e", b=2, t=4, e=4),
         )
-        v_q = [held([P, 2, HALF], U32, f"v_q{half}", tag) for half, tag in enumerate(("wl_bf1", "w1_raw"))]
+        v_q = [held([P, 2, HALF], U32, f"v_q{half}", tag) for half, tag in enumerate(("wl_bf0", "w1_raw"))]
 
         def gather_words(half):
             for g in range(2):
@@ -179,7 +183,7 @@ def tile_list_carbon_flux_features_kernel(
 
         a_kept = [
             [held([P, 4, HALF], F32, f"a_kept{half}{b}", tag) for b, tag in enumerate(tags)]
-            for half, tags in enumerate((("wl_raw0", "wl_raw1"), ("picked", "x_rows0")))
+            for half, tags in enumerate((("wl_raw0", "wl_raw2"), ("picked", "x_rows0")))
         ]
 
         def make_h(b, j0, gate, h_q, h_s):

@@ -99,11 +99,9 @@ def tile_list_carbon_flux_features_kernel(
         def log_quarter(picked, j0, jq, x_tag):
             j = j0 + jq
             x_bf = held([P, 4 * QUARTER], BF16, f"x_bf{j}", x_tag)
-            nc.vector.tensor_tensor(
+            nc.vector.tensor_copy(
                 x_bf[:].rearrange("p (c e i) -> p c i e", e=2, i=4),
-                picked[:, 0, :, jq:jq + QUARTER].rearrange("p i (c e) -> p c i e", e=2),
                 picked[:, 1, :, jq:jq + QUARTER].rearrange("p i (c e) -> p c i e", e=2),
-                ALU.add,
             )
             x_q = held([P, QUARTER], U32, f"x_q{j}")
             x_s = held([P, QUARTER], U8, f"x_s{j}")
@@ -134,16 +132,22 @@ def tile_list_carbon_flux_features_kernel(
             picked = held([P, 2, 4, HALF], F32, f"picked{j0}", picked_tag)
 
             def gather(i, jq, n):
-                for side, list_tile in enumerate((list2, list3)):
-                    nc.vector.tensor_copy(
-                        picked[:, side, i, jq:jq + n], x_rows[i][:].indirect(entries(list_tile, j0 + jq, n))
-                    )
+                first, total = picked[:, 0, i, jq:jq + n], picked[:, 1, i, jq:jq + n]
+                return (
+                    lambda: nc.vector.tensor_copy(first, x_rows[i][:].indirect(entries(list2, j0 + jq, n))),
+                    lambda: nc.vector.tensor_tensor(
+                        total, x_rows[i][:].indirect(entries(list3, j0 + jq, n)), first, ALU.add
+                    ),
+                )
 
             for i in range(whole_rows):
-                gather(i, 0, HALF)
+                for step in gather(i, 0, HALF):
+                    step()
             for jq, x_tag in quarters:
-                for i in range(whole_rows, 4):
-                    gather(i, jq, QUARTER)
+                steps = [gather(i, jq, QUARTER) for i in range(whole_rows, 4)]
+                for stage in range(2):
+                    for pair in steps:
+                        pair[stage]()
                 log_quarter(picked, j0, jq, x_tag)
 
         log_half(HALF, "picked", 3, ((0, "x_bf"), (QUARTER, "wl_bf0")))

@@ -22,6 +22,7 @@ QUARTER = 256
 PER_COLUMN = 16
 WL_PIECE = 256
 BANKS = 4
+TAB_ROW = 24
 TINY = 2.0 ** -60
 
 
@@ -44,35 +45,49 @@ def tile_list_carbon_flux_features_kernel(
         list2 = held([P, S // PER_COLUMN], U16, "list2")
         list3 = held([P, S // PER_COLUMN], U16, "list3")
         x_rows = [held([P, T], F32, f"x_rows{i}") for i in range(4)]
-        wl_raw = [held([P, 4, WL_PIECE], F32, f"wl_raw{n}") for n in range(H // WL_PIECE)]
+        wl_cuts = ((0, HALF), (HALF, WL_PIECE), (HALF + WL_PIECE, WL_PIECE))
+        wl_raw = [held([P, 4, n], F32, f"wl_raw{c}") for c, n in wl_cuts]
         tab_w = [held([P, T], U32, f"tab_w{g}") for g in range(2)]
         tab_s = held([P, T], U8, "tab_s")
         w_s_raw = held([P, H], U8, "w_s_raw")
         w1_raw = held([P, 2, 2 * H], U8, "w1_raw")
         w3_raw = held([P, 2, H], I32, "w3_raw")
         dec_rows = held([P, 2, 4], F32, "dec_rows")
-        v_s1 = held([P, S], U8, "v_s1")
+        v_s = [held([P, S], U8, f"v_s{g}") for g in range(2)]
         w1_s1 = held([P, H], U8, "w1_s1")
 
         one = held([P, 8], F32, "one")
         warm = held([P, 8], F32, "warm")
         nc.vector.memset(one[:], 1.0)
         nc.scalar.activation(warm[:], one[:], ACT.Ln)
-        for scale_tile in (tab_s, w_s_raw, v_s1, w1_s1):
+        for d in range(4):
+            nc.vector.memset(tab_s[32 * d:32 * d + TAB_ROW, :].bitcast(I32), 0)
+        for scale_tile in (w_s_raw, v_s[0], v_s[1], w1_s1):
             nc.vector.memset(scale_tile[:].bitcast(I32), 0)
 
         x_view = xT.rearrange("(p i) t -> p i t", i=4)
         wl_view = wl.rearrange("(p i) r -> p i r", i=4)
-        nc.sync.dma_start(list2[:], offs2)
-        nc.sync.dma_start(list3[:], offs3)
-        for i in range(4):
-            nc.sync.dma_start(x_rows[i][:], x_view[:, i, :])
-        for n, piece in enumerate(wl_raw):
-            nc.sync.dma_start(piece[:], wl_view[:, :, n * WL_PIECE:(n + 1) * WL_PIECE])
+
+        def load_wl(n):
+            c, width = wl_cuts[n]
+            nc.sync.dma_start(wl_raw[n][:], wl_view[:, :, c:c + width])
+
         nc.sync.dma_start(list1[:], offs)
         for d in range(4):
+            nc.sync.dma_start(
+                tab_s[32 * d + TAB_ROW:32 * (d + 1), :].bitcast(I32), tab_scales[:, 4 * d:4 * d + 4, :].bitcast(I32)
+            )
+        nc.sync.dma_start(list2[:], offs2)
+        nc.sync.dma_start(x_rows[0][:], x_view[:, 0, :])
+        nc.sync.dma_start(list3[:], offs3)
+        nc.sync.dma_start(x_rows[1][:], x_view[:, 1, :])
+        nc.sync.dma_start(x_rows[2][:], x_view[:, 2, :])
+        load_wl(0)
+        nc.sync.dma_start(x_rows[3][:], x_view[:, 3, :])
+        load_wl(1)
+        load_wl(2)
+        for d in range(4):
             rows = slice(4 * d, 4 * d + 4)
-            nc.sync.dma_start(tab_s[32 * d:32 * d + 8, :].bitcast(I32), tab_scales[:, rows, :].bitcast(I32))
             nc.sync.dma_start(w_s_raw[32 * d:32 * d + 8, :].bitcast(I32), w1_scales[:, rows, :].bitcast(I32))
             nc.sync.dma_start(w_s_raw[32 * d + 8:32 * d + 16, :].bitcast(I32), w3_scales[:, rows, :].bitcast(I32))
         nc.sync.dma_start(w1_raw[:].bitcast(I32), w1_words.rearrange("g p n -> p g n").bitcast(I32))
@@ -81,100 +96,138 @@ def tile_list_carbon_flux_features_kernel(
         nc.sync.dma_start(dec_rows[:], dec.rearrange("(b p t) -> p b t", b=2, t=4))
         nc.sync.dma_start(w3_raw[:], w3_words.rearrange("g p n i -> p g (n i)").bitcast(I32))
 
+        v_s_low = held([P, S], U8, "v_s_low")
+        nc.vector.tensor_copy(v_s_low[:], tab_s[:].indirect(list1[:]))
+
+        wl_bf = [held([P, 4 * HALF], BF16, f"wl_bf{b}") for b in range(2)]
         wl_q = [held([P, HALF], U32, f"wl_q{b}") for b in range(2)]
         wl_s = [held([P, HALF], U8, f"wl_s{b}") for b in range(2)]
-        for b in range(2):
-            wl_bf = held([P, 4 * HALF], BF16, f"wl_bf{b}")
-            by_column = wl_bf[:].rearrange("p (t c i) -> p c t i", t=4, i=4)
-            for n in range(2):
-                nc.scalar.copy(
-                    by_column[:, n * WL_PIECE // 4:(n + 1) * WL_PIECE // 4],
-                    wl_raw[2 * b + n][:].rearrange("p i (c t) -> p c t i", t=4),
-                )
-            nc.vector.quantize_mx(out=wl_q[b][:].bitcast(FP8X4), scales=wl_s[b][:], in_=wl_bf[:])
 
-        abs_b = held([P, 2, 4 * QUARTER], F32, "abs_b", "odd_gate")
-        log_b = {}
-
-        def log_quarter(picked, j0, jq, x_tag):
-            j = j0 + jq
-            x_bf = held([P, 4 * QUARTER], BF16, f"x_bf{j}", x_tag)
-            nc.vector.tensor_copy(
-                x_bf[:].rearrange("p (c e i) -> p c i e", e=2, i=4),
-                picked[:, 1, :, jq:jq + QUARTER].rearrange("p i (c e) -> p c i e", e=2),
-            )
-            x_q = held([P, QUARTER], U32, f"x_q{j}")
-            x_s = held([P, QUARTER], U8, f"x_s{j}")
-            nc.vector.quantize_mx(out=x_q[:].bitcast(FP8X4), scales=x_s[:], in_=x_bf[:])
-            for b in range(2):
-                for jb in range(0, QUARTER, P):
-                    bank = psum.tile([P, 4, P], F32, name="bank", tag="a_or_b")
-                    for t in range(4):
-                        nc.tensor.matmul_mx(
-                            out=bank[:, t, :],
-                            lhsT=wl_q[b][:, t * P:(t + 1) * P].bitcast(FP8X4),
-                            lhsT_scale=wl_s[b][:, t * P:(t + 1) * P],
-                            rhs=x_q[:, jb:jb + P].bitcast(FP8X4),
-                            rhs_scale=x_s[:, jb:jb + P],
-                            start=True,
-                            stop=True,
-                        )
-                    nc.scalar.activation(
-                        abs_b[:, b, 4 * jb:4 * (jb + P)].rearrange("p (j t) -> p j t", t=4),
-                        bank[:].rearrange("p t j -> p j t"),
-                        ACT.Abs,
+        def quantise_wl(b):
+            by_column = wl_bf[b][:].rearrange("p (t c i) -> p c t i", t=4, i=4)
+            for n, (c, width) in enumerate(wl_cuts):
+                if c // HALF == b:
+                    c0 = c % HALF // 4
+                    nc.scalar.copy(
+                        by_column[:, c0:c0 + width // 4], wl_raw[n][:].rearrange("p i (c t) -> p c t i", t=4)
                     )
-            log_b[j] = held([P, 2, 4 * QUARTER], F32, f"log_b{j}")
-            for b in range(2):
-                nc.scalar.activation(log_b[j][:, b, :], abs_b[:, b, :], ACT.Ln, bias=TINY)
+            nc.vector.quantize_mx(out=wl_q[b][:].bitcast(FP8X4), scales=wl_s[b][:], in_=wl_bf[b][:])
 
-        def log_half(j0, picked_tag, whole_rows, quarters):
-            picked = held([P, 2, 4, HALF], F32, f"picked{j0}", picked_tag)
+        x_sum = [held([P, 4, QUARTER], F32, f"x_sum{q}") for q in range(4)]
+        x_q = [held([P, QUARTER], U32, f"x_q{q}") for q in range(4)]
+        x_s = [held([P, QUARTER], U8, f"x_s{q}") for q in range(4)]
 
-            def gather(i, jq, n):
-                first, total = picked[:, 0, i, jq:jq + n], picked[:, 1, i, jq:jq + n]
-                return (
-                    lambda: nc.vector.tensor_copy(first, x_rows[i][:].indirect(entries(list2, j0 + jq, n))),
-                    lambda: nc.vector.tensor_tensor(
-                        total, x_rows[i][:].indirect(entries(list3, j0 + jq, n)), first, ALU.add
-                    ),
+        x_bf = [held([P, 4 * QUARTER], BF16, f"x_bf{q}") for q in range(4)]
+
+        def pick_first(units, tag):
+            first = held([P, len(units), QUARTER], F32, "first%d%d" % units[0], tag)
+            for u, (i, q) in enumerate(units):
+                nc.vector.tensor_copy(first[:, u, :], x_rows[i][:].indirect(entries(list2, q * QUARTER, QUARTER)))
+            return first
+
+        def add_second(units, first, j=0, width=QUARTER):
+            for u, (i, q) in enumerate(units):
+                nc.vector.tensor_tensor(
+                    x_sum[q][:, i, j:j + width],
+                    x_rows[i][:].indirect(entries(list3, q * QUARTER + j, width)),
+                    first[:, u, j:j + width],
+                    ALU.add,
                 )
 
-            for i in range(whole_rows):
-                for step in gather(i, 0, HALF):
-                    step()
-            for jq, x_tag in quarters:
-                steps = [gather(i, jq, QUARTER) for i in range(whole_rows, 4)]
-                for stage in range(2):
-                    for pair in steps:
-                        pair[stage]()
-                log_quarter(picked, j0, jq, x_tag)
+        def gather_x(units, tag):
+            add_second(units, pick_first(units, tag))
 
-        log_half(HALF, "picked", 3, ((0, "x_bf"), (QUARTER, "wl_bf0")))
-        log_half(0, "wl_bf0", 1, ((QUARTER, "x_bf"), (0, "x_bf")))
+        def quantise_x(q, j=0, width=QUARTER):
+            lines = x_bf[q][:, 4 * j:4 * (j + width)].rearrange("p (c e i) -> p c i e", e=2, i=4)
+            pairs = x_sum[q][:, :, j:j + width].rearrange("p i (c e) -> p c i e", e=2)
+            nc.vector.tensor_copy(lines, pairs)
+            nc.vector.quantize_mx(
+                out=x_q[q][:, j:j + width].bitcast(FP8X4),
+                scales=x_s[q][:, j:j + width],
+                in_=x_bf[q][:, 4 * j:4 * (j + width)],
+            )
 
+        abs_b = held([P, 4, 2, 4 * QUARTER], F32, "abs_b")
+        log_b = held([P, 4, 2, 4 * QUARTER], F32, "log_b")
+
+        def abs_of_b(q, b, jb):
+            bank = psum.tile([P, 4, P], F32, name="bank", tag="a_or_b")
+            for t in range(4):
+                nc.tensor.matmul_mx(
+                    out=bank[:, t, :],
+                    lhsT=wl_q[b][:, t * P:(t + 1) * P].bitcast(FP8X4),
+                    lhsT_scale=wl_s[b][:, t * P:(t + 1) * P],
+                    rhs=x_q[q][:, jb:jb + P].bitcast(FP8X4),
+                    rhs_scale=x_s[q][:, jb:jb + P],
+                    start=True,
+                    stop=True,
+                )
+            nc.scalar.activation(
+                abs_b[:, q, b, 4 * jb:4 * (jb + P)].rearrange("p (j t) -> p j t", t=4),
+                bank[:].rearrange("p t j -> p j t"),
+                ACT.Abs,
+            )
+
+        def log_of_b(q, b, width=QUARTER):
+            for jb in range(0, QUARTER, P):
+                abs_of_b(q, b, jb)
+            for j in range(0, QUARTER, width):
+                columns = slice(4 * j, 4 * (j + width))
+                nc.scalar.activation(log_b[:, q, b, columns], abs_b[:, q, b, columns], ACT.Ln, bias=TINY)
+
+        gather_x([(0, q) for q in range(3)], "early0")
+        gather_x([(1, 0), (1, 1)], "early1")
+        gather_x([(2, 0), (2, 1)], "early2")
+        first = pick_first([(3, 0)], "early3")
+        quantise_wl(0)
+        for j in range(0, QUARTER, P):
+            add_second([(3, 0)], first, j, P)
+        for j in range(0, QUARTER, P):
+            quantise_x(0, j, P)
+        log_of_b(0, 0)
+        gather_x([(3, 1)], "early3")
+        quantise_wl(1)
+        quantise_x(1)
+        log_of_b(0, 1, P)
+        gather_x([(i, 2) for i in range(1, 4)], "wl_bf1")
+        log_of_b(1, 0)
+        log_of_b(1, 1, P)
+        quantise_x(2)
+        last = [(i, 3) for i in range(4)]
+        first = pick_first(last, "wl_bf1")
+        log_of_b(2, 0)
+        log_of_b(2, 1, P)
+        for j in range(0, QUARTER, P):
+            add_second(last, first, j, P)
+            quantise_x(3, j, P)
+            for b in range(2):
+                abs_of_b(3, b, j)
+            columns = slice(4 * j, 4 * (j + P))
+            for b in range(2):
+                nc.scalar.activation(log_b[:, 3, b, columns], abs_b[:, 3, b, columns], ACT.Ln, bias=TINY)
+
+        for g in range(2):
+            shift = TAB_ROW + 4 * g
+            nc.sync.dma_start(v_s[g][0:P - shift, :].bitcast(I32), v_s_low[shift:P, :].bitcast(I32))
         w_s = held([P, H], U8, "w_s", "x_rows1")
         nc.vector.tensor_copy(
             w_s[:].rearrange("p (b t c e) -> p b c t e", b=2, t=4, e=8),
             w_s_raw[:].rearrange("p (b c e t) -> p b c t e", b=2, t=4, e=8),
         )
         nc.sync.dma_start(w1_s1[0:P - 4, :].bitcast(I32), w_s[4:P, :].bitcast(I32))
-        v_s0 = held([P, S], U8, "v_s0", "x_bf")
-        nc.vector.tensor_copy(v_s0[:], tab_s[:].indirect(list1[:]))
-        nc.sync.dma_start(v_s1[0:P - 4, :].bitcast(I32), v_s0[4:P, :].bitcast(I32))
-        w1_q = held([P, 4, 2 * HALF], U8, "w1_q", "x_rows3")
-        nc.vector.tensor_copy(
-            w1_q[:].bitcast(U16).rearrange("p gb (t c e) -> p gb c t e", t=4, e=4),
-            w1_raw[:].bitcast(U16).rearrange("p g (b c e t) -> p (g b) c t e", b=2, t=4, e=4),
-        )
-        v_q = [held([P, 2, HALF], U32, f"v_q{half}", tag) for half, tag in enumerate(("wl_bf0", "w1_raw"))]
+        v_q = [held([P, 2, HALF], U32, f"v_q{half}", tag) for half, tag in enumerate(("x_sum3", "w3_raw"))]
 
         def gather_words(half):
             for g in range(2):
                 nc.vector.tensor_copy(v_q[half][:, g, :], tab_w[g][:].indirect(entries(list1, half * HALF, HALF)))
 
         gather_words(0)
-        w3_q = held([P, 4, HALF], I32, "w3_q", "x_rows2")
+        w1_q = held([P, 4, 2 * HALF], U8, "w1_q", "x_bf3")
+        nc.vector.tensor_copy(
+            w1_q[:].bitcast(U16).rearrange("p gb (t c e) -> p gb c t e", t=4, e=4),
+            w1_raw[:].bitcast(U16).rearrange("p g (b c e t) -> p (g b) c t e", b=2, t=4, e=4),
+        )
+        w3_q = held([P, 4, HALF], I32, "w3_q", "w1_raw")
         nc.vector.tensor_copy(
             w3_q[:].rearrange("p gb (t c e) -> p gb c t e", t=4, e=2),
             w3_raw[:].rearrange("p g (b c e t) -> p (g b) c t e", b=2, t=4, e=2),
@@ -183,17 +236,21 @@ def tile_list_carbon_flux_features_kernel(
         minus_dec = held([P, 2, 4], F32, "minus_dec")
         nc.gpsimd.tensor_scalar(minus_dec[:], dec_rows[:], -1.0, 0.0, ALU.mult, ALU.add)
         w1_s = (w_s, w1_s1)
-        v_s = (v_s0, v_s1)
 
-        a_kept = [
-            [held([P, 4, HALF], F32, f"a_kept{half}{b}", tag) for b, tag in enumerate(tags)]
-            for half, tags in enumerate((("wl_raw0", "wl_raw2"), ("picked", "x_rows0")))
-        ]
+        gate = held([P, 4, 2, 4 * QUARTER], F32, "gate", "abs_b")
+        a_tags = ("x_sum0", "x_sum1", "x_sum2", "wl_bf0", "early0", "x_rows0", "x_rows2", "x_rows3")
+        a_kept = [[held([P, 4, QUARTER], F32, f"a_kept{q}{b}", a_tags[2 * q + b]) for b in range(2)] for q in range(4)]
+        h_q = [[held([P, QUARTER], U32, f"h_q{q}{b}") for b in range(2)] for q in range(4)]
+        h_s = [[held([P, QUARTER], U8, f"h_s{q}{b}") for b in range(2)] for q in range(4)]
 
-        def make_h(b, j0, gate, h_q, h_s):
+        def make_gate(q, b, width=4 * QUARTER):
+            for c in range(0, 4 * QUARTER, width):
+                nc.scalar.activation(gate[:, q, b, c:c + width], log_b[:, q, b, c:c + width], ACT.Sigmoid, scale=2.0)
+
+        def make_h(q, b):
             h_bf = ring.tile([P, 4 * QUARTER], BF16, name="h_bf", align_bytes=64)
             for jb in range(0, QUARTER, P):
-                j = j0 + jb
+                j = q * QUARTER + jb
                 half, jh = divmod(j, HALF)
                 bank = psum.tile([P, 4, P], F32, name="bank", tag="a_or_b")
                 for t in range(4):
@@ -210,54 +267,41 @@ def tile_list_carbon_flux_features_kernel(
                 nc.vector.tensor_tensor(
                     h_bf[:, 4 * jb:4 * (jb + P)].rearrange("p (j t) -> p j t", t=4),
                     bank[:].rearrange("p t j -> p j t"),
-                    gate[:, 4 * jb:4 * (jb + P)].rearrange("p (j t) -> p j t", t=4),
+                    gate[:, q, b, 4 * jb:4 * (jb + P)].rearrange("p (j t) -> p j t", t=4),
                     ALU.mult,
                 )
-                nc.scalar.copy(a_kept[half][b][:, :, jh:jh + P], bank[:])
-            nc.vector.quantize_mx(out=h_q[:].bitcast(FP8X4), scales=h_s[:], in_=h_bf[:])
+                nc.scalar.copy(a_kept[q][b][:, :, jb:jb + P], bank[:])
+            nc.vector.quantize_mx(out=h_q[q][b][:].bitcast(FP8X4), scales=h_s[q][b][:], in_=h_bf[:])
 
         out_view = out.rearrange("(b p t) j -> b p t j", b=2, t=4)
+        result_tags = ("wl_raw0", "wl_raw512", "wl_raw768", "tab_s")
 
-        def finish(j0, h_q, h_s):
-            half, jh = divmod(j0, HALF)
-            for b in range(2):
-                result = ring.tile([P, 4, QUARTER], F32, name="result", align_bytes=64)
-                for t in range(4):
-                    y_bank = psum.tile([P, QUARTER], F32, name="y_bank")
-                    for g in range(2):
-                        nc.tensor.matmul_mx(
-                            out=y_bank[:],
-                            lhsT=w3_q[:, 2 * g + b, t * P:(t + 1) * P].bitcast(FP8X4),
-                            lhsT_scale=w_s[8 + 4 * g:P, b * HALF + t * P:b * HALF + (t + 1) * P],
-                            rhs=h_q[g][:].bitcast(FP8X4),
-                            rhs_scale=h_s[g][:],
-                            start=(g == 0),
-                            stop=(g == 1),
-                        )
-                    nc.vector.scalar_tensor_tensor(
-                        result[:, t, :],
-                        a_kept[half][b][:, t, jh:jh + QUARTER],
-                        minus_dec[:, b, t:t + 1],
-                        y_bank[:],
-                        ALU.mult,
-                        ALU.add,
+        def finish(q, b):
+            j0 = q * QUARTER
+            result = held([P, 4, QUARTER], F32, f"result{q}{b}", result_tags[(2 * q + b) % 4])
+            for t in range(4):
+                y_bank = psum.tile([P, QUARTER], F32, name="y_bank")
+                for g in range(2):
+                    nc.tensor.matmul_mx(
+                        out=y_bank[:],
+                        lhsT=w3_q[:, 2 * g + b, t * P:(t + 1) * P].bitcast(FP8X4),
+                        lhsT_scale=w_s[8 + 4 * g:P, b * HALF + t * P:b * HALF + (t + 1) * P],
+                        rhs=h_q[q][g][:].bitcast(FP8X4),
+                        rhs_scale=h_s[q][g][:],
+                        start=(g == 0),
+                        stop=(g == 1),
                     )
-                    if t % 2 == 1:
-                        nc.sync.dma_start(out_view[b, :, t - 1:t + 1, j0:j0 + QUARTER], result[:, t - 1:t + 1, :])
+                nc.vector.scalar_tensor_tensor(
+                    result[:, t, :], a_kept[q][b][:, t, :], minus_dec[:, b, t:t + 1], y_bank[:], ALU.mult, ALU.add
+                )
+                if t % 2 == 1:
+                    nc.sync.dma_start(out_view[b, :, t - 1:t + 1, j0:j0 + QUARTER], result[:, t - 1:t + 1, :])
 
-        unfinished = None
-        for j0 in range(0, S, QUARTER):
-            gate = held([P, 2, 4 * QUARTER], F32, f"gate{j0}", ("even_gate", "odd_gate")[j0 // QUARTER % 2])
-            h_q = [held([P, QUARTER], U32, f"h_q{b}_{j0}") for b in range(2)]
-            h_s = [held([P, QUARTER], U8, f"h_s{b}_{j0}") for b in range(2)]
-            if unfinished is None:
-                for b in range(2):
-                    nc.scalar.activation(gate[:, b, :], log_b[j0][:, b, :], ACT.Sigmoid, scale=2.0)
-                    make_h(b, j0, gate[:, b, :], h_q[b], h_s[b])
-            else:
-                nc.scalar.activation(gate[:], log_b[j0][:], ACT.Sigmoid, scale=2.0)
-                make_h(0, j0, gate[:, 0, :], h_q[0], h_s[0])
-                finish(*unfinished)
-                make_h(1, j0, gate[:, 1, :], h_q[1], h_s[1])
-            unfinished = (j0, h_q, h_s)
-        finish(*unfinished)
+        make_gate(0, 0, 4 * P)
+        for step in range(10):
+            if step < 7:
+                make_gate(*divmod(step + 1, 2))
+            if step < 8:
+                make_h(*divmod(step, 2))
+            if step >= 2:
+                finish(*divmod(step - 2, 2))

@@ -22,7 +22,8 @@ QUARTER = 256
 PER_COLUMN = 16
 WL_PIECE = 256
 BANKS = 4
-TAB_ROW = 24
+TAB_ROW = 96
+EARLY_COPIES = 1
 TINY = 2.0 ** -60
 
 
@@ -60,8 +61,7 @@ def tile_list_carbon_flux_features_kernel(
         warm = held([P, 8], F32, "warm")
         nc.vector.memset(one[:], 1.0)
         nc.scalar.activation(warm[:], one[:], ACT.Ln)
-        for d in range(4):
-            nc.vector.memset(tab_s[32 * d:32 * d + TAB_ROW, :].bitcast(I32), 0)
+        nc.vector.memset(tab_s[0:TAB_ROW, :].bitcast(I32), 0)
         for scale_tile in (w_s_raw, v_s[0], v_s[1], w1_s1):
             nc.vector.memset(scale_tile[:].bitcast(I32), 0)
 
@@ -73,10 +73,7 @@ def tile_list_carbon_flux_features_kernel(
             nc.sync.dma_start(wl_raw[n][:], wl_view[:, :, c:c + width])
 
         nc.sync.dma_start(list1[:], offs)
-        for d in range(4):
-            nc.sync.dma_start(
-                tab_s[32 * d + TAB_ROW:32 * (d + 1), :].bitcast(I32), tab_scales[:, 4 * d:4 * d + 4, :].bitcast(I32)
-            )
+        nc.sync.dma_start(tab_s[TAB_ROW:P, :].bitcast(I32), tab_scales.rearrange("g q t -> (g q) t").bitcast(I32))
         nc.sync.dma_start(list2[:], offs2)
         nc.sync.dma_start(x_rows[0][:], x_view[:, 0, :])
         nc.sync.dma_start(list3[:], offs3)
@@ -113,34 +110,32 @@ def tile_list_carbon_flux_features_kernel(
                     )
             nc.vector.quantize_mx(out=wl_q[b][:].bitcast(FP8X4), scales=wl_s[b][:], in_=wl_bf[b][:])
 
-        x_sum = [held([P, 4, QUARTER], F32, f"x_sum{q}") for q in range(4)]
+        x_sum = held([P, 4, S], F32, "x_sum")
+        x_bf = [held([P, 4 * QUARTER], BF16, f"x_bf{q}") for q in range(4)]
         x_q = [held([P, QUARTER], U32, f"x_q{q}") for q in range(4)]
         x_s = [held([P, QUARTER], U8, f"x_s{q}") for q in range(4)]
 
-        x_bf = [held([P, 4 * QUARTER], BF16, f"x_bf{q}") for q in range(4)]
-
-        def pick_first(units, tag):
-            first = held([P, len(units), QUARTER], F32, "first%d%d" % units[0], tag)
-            for u, (i, q) in enumerate(units):
-                nc.vector.tensor_copy(first[:, u, :], x_rows[i][:].indirect(entries(list2, q * QUARTER, QUARTER)))
+        def pick_first(rows, j0, n, tag):
+            first = held([P, len(rows), n], F32, f"first{rows[0]}_{j0}", tag)
+            for u, i in enumerate(rows):
+                nc.vector.tensor_copy(first[:, u, :], x_rows[i][:].indirect(entries(list2, j0, n)))
             return first
 
-        def add_second(units, first, j=0, width=QUARTER):
-            for u, (i, q) in enumerate(units):
+        def add_second(rows, first, j0, j, n):
+            for u, i in enumerate(rows):
                 nc.vector.tensor_tensor(
-                    x_sum[q][:, i, j:j + width],
-                    x_rows[i][:].indirect(entries(list3, q * QUARTER + j, width)),
-                    first[:, u, j:j + width],
+                    x_sum[:, i, j:j + n],
+                    x_rows[i][:].indirect(entries(list3, j, n)),
+                    first[:, u, j - j0:j - j0 + n],
                     ALU.add,
                 )
 
-        def gather_x(units, tag):
-            add_second(units, pick_first(units, tag))
-
         def quantise_x(q, j=0, width=QUARTER):
-            lines = x_bf[q][:, 4 * j:4 * (j + width)].rearrange("p (c e i) -> p c i e", e=2, i=4)
-            pairs = x_sum[q][:, :, j:j + width].rearrange("p i (c e) -> p c i e", e=2)
-            nc.vector.tensor_copy(lines, pairs)
+            j0 = q * QUARTER + j
+            nc.vector.tensor_copy(
+                x_bf[q][:, 4 * j:4 * (j + width)].rearrange("p (c e i) -> p c i e", e=2, i=4),
+                x_sum[:, :, j0:j0 + width].rearrange("p i (c e) -> p c i e", e=2),
+            )
             nc.vector.quantize_mx(
                 out=x_q[q][:, j:j + width].bitcast(FP8X4),
                 scales=x_s[q][:, j:j + width],
@@ -151,7 +146,7 @@ def tile_list_carbon_flux_features_kernel(
         log_b = held([P, 4, 2, 4 * QUARTER], F32, "log_b")
 
         def abs_of_b(q, b, jb):
-            bank = psum.tile([P, 4, P], F32, name="bank", tag="a_or_b")
+            bank = psum.tile([P, 4, P], F32, name="bank", tag="a_or_b", bufs=BANKS)
             for t in range(4):
                 nc.tensor.matmul_mx(
                     out=bank[:, t, :],
@@ -175,71 +170,65 @@ def tile_list_carbon_flux_features_kernel(
                 columns = slice(4 * j, 4 * (j + width))
                 nc.scalar.activation(log_b[:, q, b, columns], abs_b[:, q, b, columns], ACT.Ln, bias=TINY)
 
-        gather_x([(0, q) for q in range(3)], "early0")
-        gather_x([(1, 0), (1, 1)], "early1")
-        gather_x([(2, 0), (2, 1)], "early2")
-        first = pick_first([(3, 0)], "early3")
+        for i, n in enumerate((3 * QUARTER, HALF, HALF)):
+            add_second([i], pick_first([i], 0, n, f"early{i}"), 0, 0, n)
+        first = pick_first([3], 0, QUARTER, "early3")
         quantise_wl(0)
-        for j in range(0, QUARTER, P):
-            add_second([(3, 0)], first, j, P)
+        add_second([3], first, 0, 0, QUARTER)
         for j in range(0, QUARTER, P):
             quantise_x(0, j, P)
         log_of_b(0, 0)
-        gather_x([(3, 1)], "early3")
+        add_second([3], pick_first([3], QUARTER, QUARTER, "early3"), QUARTER, QUARTER, QUARTER)
         quantise_wl(1)
         quantise_x(1)
         log_of_b(0, 1, P)
-        gather_x([(i, 2) for i in range(1, 4)], "wl_bf1")
+        late_rows = [1, 2, 3]
+        add_second(late_rows, pick_first(late_rows, HALF, QUARTER, "wl_bf1"), HALF, HALF, QUARTER)
         log_of_b(1, 0)
         log_of_b(1, 1, P)
         quantise_x(2)
-        last = [(i, 3) for i in range(4)]
-        first = pick_first(last, "wl_bf1")
+        last, all_rows = 3 * QUARTER, [0, 1, 2, 3]
+        add_second(all_rows, pick_first(all_rows, last, QUARTER, "wl_bf1"), last, last, QUARTER)
         log_of_b(2, 0)
         log_of_b(2, 1, P)
         for j in range(0, QUARTER, P):
-            add_second(last, first, j, P)
             quantise_x(3, j, P)
-            for b in range(2):
-                abs_of_b(3, b, j)
-            columns = slice(4 * j, 4 * (j + P))
-            for b in range(2):
-                nc.scalar.activation(log_b[:, 3, b, columns], abs_b[:, 3, b, columns], ACT.Ln, bias=TINY)
+        log_of_b(3, 0)
+        log_of_b(3, 1, P)
 
         for g in range(2):
-            shift = TAB_ROW + 4 * g
-            nc.sync.dma_start(v_s[g][0:P - shift, :].bitcast(I32), v_s_low[shift:P, :].bitcast(I32))
+            for d in range(4):
+                row = TAB_ROW + 16 * g + 4 * d
+                nc.sync.dma_start(v_s[g][32 * d:32 * d + 4, :].bitcast(I32), v_s_low[row:row + 4, :].bitcast(I32))
         w_s = held([P, H], U8, "w_s", "x_rows1")
-        nc.vector.tensor_copy(
-            w_s[:].rearrange("p (b t c e) -> p b c t e", b=2, t=4, e=8),
-            w_s_raw[:].rearrange("p (b c e t) -> p b c t e", b=2, t=4, e=8),
-        )
+        for b in range(2):
+            columns = slice(b * HALF, (b + 1) * HALF)
+            nc.vector.tensor_copy(
+                w_s[:, columns].rearrange("p (t c e) -> p c t e", t=4, e=8),
+                w_s_raw[:, columns].rearrange("p (c e t) -> p c t e", t=4, e=8),
+            )
         nc.sync.dma_start(w1_s1[0:P - 4, :].bitcast(I32), w_s[4:P, :].bitcast(I32))
-        v_q = [held([P, 2, HALF], U32, f"v_q{half}", tag) for half, tag in enumerate(("x_sum3", "w3_raw"))]
-
-        def gather_words(half):
-            for g in range(2):
-                nc.vector.tensor_copy(v_q[half][:, g, :], tab_w[g][:].indirect(entries(list1, half * HALF, HALF)))
-
-        gather_words(0)
-        w1_q = held([P, 4, 2 * HALF], U8, "w1_q", "x_bf3")
+        w1_q = held([P, 4, 2 * HALF], U8, "w1_q", "x_rows3")
         nc.vector.tensor_copy(
             w1_q[:].bitcast(U16).rearrange("p gb (t c e) -> p gb c t e", t=4, e=4),
             w1_raw[:].bitcast(U16).rearrange("p g (b c e t) -> p (g b) c t e", b=2, t=4, e=4),
         )
-        w3_q = held([P, 4, HALF], I32, "w3_q", "w1_raw")
+        v_q = [held([P, 2, HALF], U32, f"v_q{half}", tag) for half, tag in enumerate(("x_rows0", "wl_bf1"))]
+        for half in range(2):
+            for g in range(2):
+                nc.vector.tensor_copy(v_q[half][:, g, :], tab_w[g][:].indirect(entries(list1, half * HALF, HALF)))
+        w3_q = held([P, 4, HALF], I32, "w3_q", "x_rows2")
         nc.vector.tensor_copy(
             w3_q[:].rearrange("p gb (t c e) -> p gb c t e", t=4, e=2),
             w3_raw[:].rearrange("p g (b c e t) -> p (g b) c t e", b=2, t=4, e=2),
         )
-        gather_words(1)
         minus_dec = held([P, 2, 4], F32, "minus_dec")
         nc.gpsimd.tensor_scalar(minus_dec[:], dec_rows[:], -1.0, 0.0, ALU.mult, ALU.add)
         w1_s = (w_s, w1_s1)
 
         gate = held([P, 4, 2, 4 * QUARTER], F32, "gate", "abs_b")
-        a_tags = ("x_sum0", "x_sum1", "x_sum2", "wl_bf0", "early0", "x_rows0", "x_rows2", "x_rows3")
-        a_kept = [[held([P, 4, QUARTER], F32, f"a_kept{q}{b}", a_tags[2 * q + b]) for b in range(2)] for q in range(4)]
+        a_halves = [held([P, 4, 4, QUARTER], F32, f"a_half{n}", tag) for n, tag in enumerate(("x_sum", ""))]
+        a_kept = [[a_halves[q // 2][:, 2 * (q % 2) + b] for b in range(2)] for q in range(4)]
         h_q = [[held([P, QUARTER], U32, f"h_q{q}{b}") for b in range(2)] for q in range(4)]
         h_s = [[held([P, QUARTER], U8, f"h_s{q}{b}") for b in range(2)] for q in range(4)]
 
@@ -247,31 +236,43 @@ def tile_list_carbon_flux_features_kernel(
             for c in range(0, 4 * QUARTER, width):
                 nc.scalar.activation(gate[:, q, b, c:c + width], log_b[:, q, b, c:c + width], ACT.Sigmoid, scale=2.0)
 
+        def product_a(q, b, jb):
+            j = q * QUARTER + jb
+            half, jh = divmod(j, HALF)
+            bank = psum.tile([P, 4, P], F32, name="bank", tag="a_or_b", bufs=BANKS)
+            for t in range(4):
+                for g in range(2):
+                    nc.tensor.matmul_mx(
+                        out=bank[:, t, :],
+                        lhsT=w1_q[:, 2 * g + b, 2 * t * P:2 * (t + 1) * P].bitcast(FP4X4),
+                        lhsT_scale=w1_s[g][:, b * HALF + t * P:b * HALF + (t + 1) * P],
+                        rhs=v_q[half][:, g, jh:jh + P].bitcast(FP8X4),
+                        rhs_scale=v_s[g][:, j:j + P],
+                        start=(g == 0),
+                        stop=(g == 1),
+                    )
+            return bank
+
+        def by_plot(ap, jb):
+            return ap[:, 4 * jb:4 * (jb + P)].rearrange("p (j t) -> p j t", t=4)
+
+        def quantise_h(q, b, h_bf):
+            nc.vector.quantize_mx(out=h_q[q][b][:].bitcast(FP8X4), scales=h_s[q][b][:], in_=h_bf[:])
+
         def make_h(q, b):
             h_bf = ring.tile([P, 4 * QUARTER], BF16, name="h_bf", align_bytes=64)
             for jb in range(0, QUARTER, P):
-                j = q * QUARTER + jb
-                half, jh = divmod(j, HALF)
-                bank = psum.tile([P, 4, P], F32, name="bank", tag="a_or_b")
-                for t in range(4):
-                    for g in range(2):
-                        nc.tensor.matmul_mx(
-                            out=bank[:, t, :],
-                            lhsT=w1_q[:, 2 * g + b, 2 * t * P:2 * (t + 1) * P].bitcast(FP4X4),
-                            lhsT_scale=w1_s[g][:, b * HALF + t * P:b * HALF + (t + 1) * P],
-                            rhs=v_q[half][:, g, jh:jh + P].bitcast(FP8X4),
-                            rhs_scale=v_s[g][:, j:j + P],
-                            start=(g == 0),
-                            stop=(g == 1),
-                        )
+                bank = product_a(q, b, jb)
+                kept = a_kept[q][b][:, :, jb:jb + P]
+                early = 4 * q + 2 * b + jb // P < EARLY_COPIES
+                if early:
+                    nc.vector.tensor_copy(kept, bank[:])
                 nc.vector.tensor_tensor(
-                    h_bf[:, 4 * jb:4 * (jb + P)].rearrange("p (j t) -> p j t", t=4),
-                    bank[:].rearrange("p t j -> p j t"),
-                    gate[:, q, b, 4 * jb:4 * (jb + P)].rearrange("p (j t) -> p j t", t=4),
-                    ALU.mult,
+                    by_plot(h_bf[:], jb), bank[:].rearrange("p t j -> p j t"), by_plot(gate[:, q, b, :], jb), ALU.mult
                 )
-                nc.scalar.copy(a_kept[q][b][:, :, jb:jb + P], bank[:])
-            nc.vector.quantize_mx(out=h_q[q][b][:].bitcast(FP8X4), scales=h_s[q][b][:], in_=h_bf[:])
+                if not early:
+                    nc.scalar.copy(kept, bank[:])
+            quantise_h(q, b, h_bf)
 
         out_view = out.rearrange("(b p t) j -> b p t j", b=2, t=4)
         result_tags = ("wl_raw0", "wl_raw512", "wl_raw768", "tab_s")
@@ -280,7 +281,7 @@ def tile_list_carbon_flux_features_kernel(
             j0 = q * QUARTER
             result = held([P, 4, QUARTER], F32, f"result{q}{b}", result_tags[(2 * q + b) % 4])
             for t in range(4):
-                y_bank = psum.tile([P, QUARTER], F32, name="y_bank")
+                y_bank = psum.tile([P, QUARTER], F32, name="y_bank", bufs=8 - BANKS)
                 for g in range(2):
                     nc.tensor.matmul_mx(
                         out=y_bank[:],
@@ -294,7 +295,9 @@ def tile_list_carbon_flux_features_kernel(
                 nc.vector.scalar_tensor_tensor(
                     result[:, t, :], a_kept[q][b][:, t, :], minus_dec[:, b, t:t + 1], y_bank[:], ALU.mult, ALU.add
                 )
-                if t % 2 == 1:
+                if (q, b) == (3, 1) and t >= 2:
+                    nc.sync.dma_start(out_view[b, :, t, j0:j0 + QUARTER], result[:, t, :])
+                elif t % 2 == 1:
                     nc.sync.dma_start(out_view[b, :, t - 1:t + 1, j0:j0 + QUARTER], result[:, t - 1:t + 1, :])
 
         make_gate(0, 0, 4 * P)

@@ -24,6 +24,7 @@ WL_PIECE = 256
 BANKS = 4
 TAB_ROW = 96
 EARLY_COPIES = 1
+EARLY = (768, 512, 512)
 TINY = 2.0 ** -60
 
 
@@ -76,8 +77,8 @@ def tile_list_carbon_flux_features_kernel(
         nc.sync.dma_start(tab_s[TAB_ROW:P, :].bitcast(I32), tab_scales.rearrange("g q t -> (g q) t").bitcast(I32))
         nc.sync.dma_start(list2[:], offs2)
         nc.sync.dma_start(x_rows[0][:], x_view[:, 0, :])
-        nc.sync.dma_start(list3[:], offs3)
         nc.sync.dma_start(x_rows[1][:], x_view[:, 1, :])
+        nc.sync.dma_start(list3[:], offs3)
         nc.sync.dma_start(x_rows[2][:], x_view[:, 2, :])
         load_wl(0)
         nc.sync.dma_start(x_rows[3][:], x_view[:, 3, :])
@@ -170,24 +171,27 @@ def tile_list_carbon_flux_features_kernel(
                 columns = slice(4 * j, 4 * (j + width))
                 nc.scalar.activation(log_b[:, q, b, columns], abs_b[:, q, b, columns], ACT.Ln, bias=TINY)
 
-        for i, n in enumerate((3 * QUARTER, HALF, HALF)):
-            add_second([i], pick_first([i], 0, n, f"early{i}"), 0, 0, n)
-        first = pick_first([3], 0, QUARTER, "early3")
+        firsts = [pick_first([i], 0, EARLY[i], f"early{i}") for i in range(2)]
+        for i in range(2):
+            add_second([i], firsts[i], 0, 0, EARLY[i])
+        add_second([2], pick_first([2], 0, EARLY[2], "early2"), 0, 0, EARLY[2])
+        first = pick_first([3], 0, HALF, "early3")
         quantise_wl(0)
         add_second([3], first, 0, 0, QUARTER)
         for j in range(0, QUARTER, P):
             quantise_x(0, j, P)
         log_of_b(0, 0)
-        add_second([3], pick_first([3], QUARTER, QUARTER, "early3"), QUARTER, QUARTER, QUARTER)
+        add_second([3], first, 0, QUARTER, QUARTER)
         quantise_wl(1)
         quantise_x(1)
         log_of_b(0, 1, P)
-        late_rows = [1, 2, 3]
+        late_rows = [i for i in range(4) if i == 3 or EARLY[i] <= HALF]
         add_second(late_rows, pick_first(late_rows, HALF, QUARTER, "wl_bf1"), HALF, HALF, QUARTER)
         log_of_b(1, 0)
         log_of_b(1, 1, P)
         quantise_x(2)
-        last, all_rows = 3 * QUARTER, [0, 1, 2, 3]
+        last = 3 * QUARTER
+        all_rows = [i for i in range(4) if i == 3 or EARLY[i] <= last]
         add_second(all_rows, pick_first(all_rows, last, QUARTER, "wl_bf1"), last, last, QUARTER)
         log_of_b(2, 0)
         log_of_b(2, 1, P)
@@ -223,7 +227,7 @@ def tile_list_carbon_flux_features_kernel(
             w3_raw[:].rearrange("p g (b c e t) -> p (g b) c t e", b=2, t=4, e=2),
         )
         minus_dec = held([P, 2, 4], F32, "minus_dec")
-        nc.gpsimd.tensor_scalar(minus_dec[:], dec_rows[:], -1.0, 0.0, ALU.mult, ALU.add)
+        nc.scalar.mul(minus_dec[:], dec_rows[:], -1.0)
         w1_s = (w_s, w1_s1)
 
         gate = held([P, 4, 2, 4 * QUARTER], F32, "gate", "abs_b")

@@ -23,7 +23,6 @@ PER_COLUMN = 16
 WL_PIECE = 256
 BANKS = 4
 TAB_ROW = 96
-EARLY_COPIES = 1
 EARLY = (768, 512, 512)
 TINY = 2.0 ** -60
 
@@ -34,7 +33,6 @@ def tile_list_carbon_flux_features_kernel(
     nc = tc.nc
     with ExitStack() as ctx:
         keep = ctx.enter_context(tc.tile_pool(name="keep", bufs=1))
-        ring = ctx.enter_context(tc.tile_pool(name="ring", bufs=2))
         psum = ctx.enter_context(tc.psum_pool(name="psum", bufs=BANKS))
 
         def held(shape, dtype, name, tag=""):
@@ -145,9 +143,12 @@ def tile_list_carbon_flux_features_kernel(
 
         abs_b = held([P, 4, 2, 4 * QUARTER], F32, "abs_b")
         log_b = held([P, 4, 2, 4 * QUARTER], F32, "log_b")
+        abs_of = {(q, b): abs_b[:, q, b, :] for q in range(4) for b in range(2)}
+        log_of = {(q, b): log_b[:, q, b, :] for q in range(4) for b in range(2)}
+        log_of[0, 1] = held([P, 4 * QUARTER], F32, "log_first", "a_half1")[:]
 
         def abs_of_b(q, b, jb):
-            bank = psum.tile([P, 4, P], F32, name="bank", tag="a_or_b", bufs=BANKS)
+            bank = psum.tile([P, 4, P], F32, name="bank", tag=("a_bank", "y_bank")[q % 2], bufs=BANKS)
             for t in range(4):
                 nc.tensor.matmul_mx(
                     out=bank[:, t, :],
@@ -159,7 +160,7 @@ def tile_list_carbon_flux_features_kernel(
                     stop=True,
                 )
             nc.scalar.activation(
-                abs_b[:, q, b, 4 * jb:4 * (jb + P)].rearrange("p (j t) -> p j t", t=4),
+                abs_of[q, b][:, 4 * jb:4 * (jb + P)].rearrange("p (j t) -> p j t", t=4),
                 bank[:].rearrange("p t j -> p j t"),
                 ACT.Abs,
             )
@@ -169,7 +170,7 @@ def tile_list_carbon_flux_features_kernel(
                 abs_of_b(q, b, jb)
             for j in range(0, QUARTER, width):
                 columns = slice(4 * j, 4 * (j + width))
-                nc.scalar.activation(log_b[:, q, b, columns], abs_b[:, q, b, columns], ACT.Ln, bias=TINY)
+                nc.scalar.activation(log_of[q, b][:, columns], abs_of[q, b][:, columns], ACT.Ln, bias=TINY)
 
         firsts = [pick_first([i], 0, EARLY[i], f"early{i}") for i in range(2)]
         for i in range(2):
@@ -197,6 +198,7 @@ def tile_list_carbon_flux_features_kernel(
         log_of_b(2, 1, P)
         for j in range(0, QUARTER, P):
             quantise_x(3, j, P)
+        abs_of[3, 0] = held([P, 4 * QUARTER], F32, "abs_late", "x_sum")[:]
         log_of_b(3, 0)
         log_of_b(3, 1, P)
 
@@ -231,19 +233,21 @@ def tile_list_carbon_flux_features_kernel(
         w1_s = (w_s, w1_s1)
 
         gate = held([P, 4, 2, 4 * QUARTER], F32, "gate", "abs_b")
-        a_halves = [held([P, 4, 4, QUARTER], F32, f"a_half{n}", tag) for n, tag in enumerate(("x_sum", ""))]
-        a_kept = [[a_halves[q // 2][:, 2 * (q % 2) + b] for b in range(2)] for q in range(4)]
-        h_q = [[held([P, QUARTER], U32, f"h_q{q}{b}") for b in range(2)] for q in range(4)]
-        h_s = [[held([P, QUARTER], U8, f"h_s{q}{b}") for b in range(2)] for q in range(4)]
+        a_halves = [held([P, 2, 2, 4 * QUARTER], F32, f"a_half{n}", tag) for n, tag in enumerate(("x_sum", ""))]
+        a_rows = [a_halves[q // 2][:, q % 2, 0].rearrange("p (t j) -> p t j", t=4) for q in range(4)]
+        a_pairs = [a_halves[q // 2][:, q % 2, 1].rearrange("p (c t e) -> p c t e", t=4, e=2) for q in range(4)]
+        h_bf = held([P, 3, 4 * QUARTER], BF16, "h_bf")
+        h_q = [held([P, 2, QUARTER], U32, f"h_q{q}") for q in range(4)]
+        h_s = [held([P, 2, QUARTER], U8, f"h_s{q}") for q in range(4)]
 
-        def make_gate(q, b, width=4 * QUARTER):
-            for c in range(0, 4 * QUARTER, width):
-                nc.scalar.activation(gate[:, q, b, c:c + width], log_b[:, q, b, c:c + width], ACT.Sigmoid, scale=2.0)
+        def make_gate(q, b, j=0, width=QUARTER):
+            columns = slice(4 * j, 4 * (j + width))
+            nc.scalar.activation(gate[:, q, b, columns], log_of[q, b][:, columns], ACT.Sigmoid, scale=2.0)
 
-        def product_a(q, b, jb):
+        def product_a(q, b, jb, tag="a_bank"):
             j = q * QUARTER + jb
             half, jh = divmod(j, HALF)
-            bank = psum.tile([P, 4, P], F32, name="bank", tag="a_or_b", bufs=BANKS)
+            bank = psum.tile([P, 4, P], F32, name="bank", tag=tag, bufs=BANKS)
             for t in range(4):
                 for g in range(2):
                     nc.tensor.matmul_mx(
@@ -260,55 +264,93 @@ def tile_list_carbon_flux_features_kernel(
         def by_plot(ap, jb):
             return ap[:, 4 * jb:4 * (jb + P)].rearrange("p (j t) -> p j t", t=4)
 
-        def quantise_h(q, b, h_bf):
-            nc.vector.quantize_mx(out=h_q[q][b][:].bitcast(FP8X4), scales=h_s[q][b][:], in_=h_bf[:])
+        def keep_pairs(copy, q, jb, bank):
+            copy(a_pairs[q][:, jb // 2:(jb + P) // 2], bank[:].rearrange("p t (c e) -> p c t e", e=2))
 
-        def make_h(q, b):
-            h_bf = ring.tile([P, 4 * QUARTER], BF16, name="h_bf", align_bytes=64)
-            for jb in range(0, QUARTER, P):
-                bank = product_a(q, b, jb)
-                kept = a_kept[q][b][:, :, jb:jb + P]
-                early = 4 * q + 2 * b + jb // P < EARLY_COPIES
-                if early:
-                    nc.vector.tensor_copy(kept, bank[:])
-                nc.vector.tensor_tensor(
-                    by_plot(h_bf[:], jb), bank[:].rearrange("p t j -> p j t"), by_plot(gate[:, q, b, :], jb), ALU.mult
-                )
-                if not early:
-                    nc.scalar.copy(kept, bank[:])
-            quantise_h(q, b, h_bf)
+        def h_from_kept(q, jb):
+            nc.gpsimd.tensor_tensor(
+                h_bf[:, 1, 4 * jb:4 * (jb + P)].rearrange("p (c e t) -> p c e t", e=2, t=4),
+                a_pairs[q][:, jb // 2:(jb + P) // 2].rearrange("p c t e -> p c e t"),
+                gate[:, q, 1, 4 * jb:4 * (jb + P)].rearrange("p (c e t) -> p c e t", e=2, t=4),
+                ALU.mult,
+            )
+
+        def h_from_bank(q, b, jb, bank):
+            nc.vector.tensor_tensor(
+                by_plot(h_bf[:, 2 * (q % 2), :], jb), bank[:].rearrange("p t j -> p j t"), by_plot(gate[:, q, b, :], jb), ALU.mult
+            )
+
+        def quantise_h(q):
+            nc.vector.quantize_mx(
+                out=h_q[q][:].rearrange("p b j -> p (b j)").bitcast(FP8X4),
+                scales=h_s[q][:].rearrange("p b j -> p (b j)"),
+                in_=h_bf[:, q % 2:q % 2 + 2, :].rearrange("p b c -> p (b c)"),
+            )
 
         out_view = out.rearrange("(b p t) j -> b p t j", b=2, t=4)
-        result_tags = ("wl_raw0", "wl_raw512", "wl_raw768", "tab_s")
+        result_tags = ("wl_raw0", "wl_raw512", "wl_raw768", "tab_w1")
 
-        def finish(q, b):
+        results = {}
+
+        def finish(q, b, pairs=(0, 2)):
             j0 = q * QUARTER
-            result = held([P, 4, QUARTER], F32, f"result{q}{b}", result_tags[(2 * q + b) % 4])
-            for t in range(4):
-                y_bank = psum.tile([P, QUARTER], F32, name="y_bank", bufs=8 - BANKS)
-                for g in range(2):
-                    nc.tensor.matmul_mx(
-                        out=y_bank[:],
-                        lhsT=w3_q[:, 2 * g + b, t * P:(t + 1) * P].bitcast(FP8X4),
-                        lhsT_scale=w_s[8 + 4 * g:P, b * HALF + t * P:b * HALF + (t + 1) * P],
-                        rhs=h_q[q][g][:].bitcast(FP8X4),
-                        rhs_scale=h_s[q][g][:],
-                        start=(g == 0),
-                        stop=(g == 1),
+            if (q, b) not in results:
+                results[q, b] = held([P, 4, QUARTER], F32, f"result{q}{b}", result_tags[(2 * q + b) % 4])
+            result = results[q, b]
+            for pair in pairs:
+                y_bank = psum.tile([P, 2, QUARTER], F32, name="y_bank", tag="y_bank", bufs=BANKS)
+                for t in range(pair, pair + 2):
+                    for g in range(2):
+                        nc.tensor.matmul_mx(
+                            out=y_bank[:, t - pair, :],
+                            lhsT=w3_q[:, 2 * g + b, t * P:(t + 1) * P].bitcast(FP8X4),
+                            lhsT_scale=w_s[8 + 4 * g:P, b * HALF + t * P:b * HALF + (t + 1) * P],
+                            rhs=h_q[q][:, (g + q) % 2, :].bitcast(FP8X4),
+                            rhs_scale=h_s[q][:, (g + q) % 2, :],
+                            start=(g == 0),
+                            stop=(g == 1),
+                        )
+                for t in range(pair, pair + 2):
+                    nc.vector.scalar_tensor_tensor(
+                        result[:, t, :].rearrange("p (c e) -> p c e", e=2),
+                        a_pairs[q][:, :, t, :] if b else a_rows[q][:, t, :].rearrange("p (c e) -> p c e", e=2),
+                        minus_dec[:, b, t:t + 1],
+                        y_bank[:, t - pair, :].rearrange("p (c e) -> p c e", e=2),
+                        ALU.mult,
+                        ALU.add,
                     )
-                nc.vector.scalar_tensor_tensor(
-                    result[:, t, :], a_kept[q][b][:, t, :], minus_dec[:, b, t:t + 1], y_bank[:], ALU.mult, ALU.add
-                )
-                if (q, b) == (3, 1) and t >= 2:
-                    nc.sync.dma_start(out_view[b, :, t, j0:j0 + QUARTER], result[:, t, :])
-                elif t % 2 == 1:
-                    nc.sync.dma_start(out_view[b, :, t - 1:t + 1, j0:j0 + QUARTER], result[:, t - 1:t + 1, :])
+                    if (q, b, pair) == (3, 0, 2):
+                        nc.sync.dma_start(out_view[b, :, t, j0:j0 + QUARTER], result[:, t, :])
+                if (q, b, pair) != (3, 0, 2):
+                    nc.sync.dma_start(out_view[b, :, pair:pair + 2, j0:j0 + QUARTER], result[:, pair:pair + 2, :])
 
-        make_gate(0, 0, 4 * P)
-        for step in range(10):
-            if step < 7:
-                make_gate(*divmod(step + 1, 2))
-            if step < 8:
-                make_h(*divmod(step, 2))
-            if step >= 2:
-                finish(*divmod(step - 2, 2))
+        for q in range(2):
+            for jb in (0, P):
+                keep_pairs(nc.vector.tensor_copy, q, jb, product_a(q, 1, jb))
+        waiting = [product_a(2, 1, jb, "y_bank") for jb in (0, P)]
+        for jb in (0, P):
+            for b in (1, 0):
+                make_gate(0, b, jb, P)
+        for q in range(5):
+            if q < 4:
+                banks = [product_a(q, 0, jb, "a_bank" if q else "y_bank") for jb in (0, P)]
+                for jb, bank in zip((0, P), banks):
+                    h_from_kept(q, jb)
+                    h_from_bank(q, 0, jb, bank)
+                    if q == 0:
+                        keep_pairs(nc.vector.tensor_copy, 2, jb, waiting[jb // P])
+                if q < 3:
+                    for b in ((0, 1) if q == 0 else (1, 0)):
+                        make_gate(q + 1, b)
+                for jb, bank in zip((0, P), banks):
+                    nc.scalar.copy(a_rows[q][:, :, jb:jb + P], bank[:])
+                if q == 0:
+                    for jb in (0, P):
+                        keep_pairs(nc.scalar.copy, 3, jb, product_a(3, 1, jb))
+            if q > 0:
+                finish(q - 1, 1)
+                finish(q - 1, 0, (0,) if q in (3,) else (0, 2))
+            if q < 4:
+                quantise_h(q)
+            if q in (3,):
+                finish(q - 1, 0, (2,))

@@ -21,9 +21,9 @@ HALF = 512
 QUARTER = 256
 PER_COLUMN = 16
 WL_PIECE = 256
-BANKS = 4
+BANKS = {"a_bank": 5, "y_bank": 3}
 TAB_ROW = 96
-EARLY = (768, 512, 512)
+EARLY = (768, 768, 512)
 TINY = 2.0 ** -60
 
 
@@ -33,7 +33,7 @@ def tile_list_carbon_flux_features_kernel(
     nc = tc.nc
     with ExitStack() as ctx:
         keep = ctx.enter_context(tc.tile_pool(name="keep", bufs=1))
-        psum = ctx.enter_context(tc.psum_pool(name="psum", bufs=BANKS))
+        psum = ctx.enter_context(tc.psum_pool(name="psum", bufs=1))
 
         def held(shape, dtype, name, tag=""):
             return keep.tile(shape, dtype, name=name, tag=tag or name, align_bytes=64)
@@ -46,7 +46,8 @@ def tile_list_carbon_flux_features_kernel(
         list3 = held([P, S // PER_COLUMN], U16, "list3")
         x_rows = [held([P, T], F32, f"x_rows{i}") for i in range(4)]
         wl_cuts = ((0, HALF), (HALF, WL_PIECE), (HALF + WL_PIECE, WL_PIECE))
-        wl_raw = [held([P, 4, n], F32, f"wl_raw{c}") for c, n in wl_cuts]
+        wl_tags = ("", "", "abs_b")
+        wl_raw = [held([P, 4, n], F32, f"wl_raw{c}", tag) for (c, n), tag in zip(wl_cuts, wl_tags)]
         tab_w = [held([P, T], U32, f"tab_w{g}") for g in range(2)]
         tab_s = held([P, T], U8, "tab_s")
         w_s_raw = held([P, H], U8, "w_s_raw")
@@ -75,8 +76,8 @@ def tile_list_carbon_flux_features_kernel(
         nc.sync.dma_start(tab_s[TAB_ROW:P, :].bitcast(I32), tab_scales.rearrange("g q t -> (g q) t").bitcast(I32))
         nc.sync.dma_start(list2[:], offs2)
         nc.sync.dma_start(x_rows[0][:], x_view[:, 0, :])
-        nc.sync.dma_start(x_rows[1][:], x_view[:, 1, :])
         nc.sync.dma_start(list3[:], offs3)
+        nc.sync.dma_start(x_rows[1][:], x_view[:, 1, :])
         nc.sync.dma_start(x_rows[2][:], x_view[:, 2, :])
         load_wl(0)
         nc.sync.dma_start(x_rows[3][:], x_view[:, 3, :])
@@ -99,7 +100,7 @@ def tile_list_carbon_flux_features_kernel(
         wl_q = [held([P, HALF], U32, f"wl_q{b}") for b in range(2)]
         wl_s = [held([P, HALF], U8, f"wl_s{b}") for b in range(2)]
 
-        def quantise_wl(b):
+        def round_wl(b):
             by_column = wl_bf[b][:].rearrange("p (t c i) -> p c t i", t=4, i=4)
             for n, (c, width) in enumerate(wl_cuts):
                 if c // HALF == b:
@@ -107,10 +108,14 @@ def tile_list_carbon_flux_features_kernel(
                     nc.scalar.copy(
                         by_column[:, c0:c0 + width // 4], wl_raw[n][:].rearrange("p i (c t) -> p c t i", t=4)
                     )
+
+        def quantise_wl(b):
             nc.vector.quantize_mx(out=wl_q[b][:].bitcast(FP8X4), scales=wl_s[b][:], in_=wl_bf[b][:])
 
+        for b in range(2):
+            round_wl(b)
         x_sum = held([P, 4, S], F32, "x_sum")
-        x_bf = [held([P, 4 * QUARTER], BF16, f"x_bf{q}") for q in range(4)]
+        x_bf = {q: held([P, 4 * QUARTER], BF16, f"x_bf{q}")[:] for q in (0, 2, 3)}
         x_q = [held([P, QUARTER], U32, f"x_q{q}") for q in range(4)]
         x_s = [held([P, QUARTER], U8, f"x_s{q}") for q in range(4)]
 
@@ -148,7 +153,8 @@ def tile_list_carbon_flux_features_kernel(
         log_of[0, 1] = held([P, 4 * QUARTER], F32, "log_first", "a_half1")[:]
 
         def abs_of_b(q, b, jb):
-            bank = psum.tile([P, 4, P], F32, name="bank", tag=("a_bank", "y_bank")[q % 2], bufs=BANKS)
+            tag = "a_bank" if (4 * q + 2 * b + jb // P) % 8 < BANKS["a_bank"] else "y_bank"
+            bank = psum.tile([P, 4, P], F32, name="bank", tag=tag, bufs=BANKS[tag])
             for t in range(4):
                 nc.tensor.matmul_mx(
                     out=bank[:, t, :],
@@ -172,22 +178,27 @@ def tile_list_carbon_flux_features_kernel(
                 columns = slice(4 * j, 4 * (j + width))
                 nc.scalar.activation(log_of[q, b][:, columns], abs_of[q, b][:, columns], ACT.Ln, bias=TINY)
 
-        firsts = [pick_first([i], 0, EARLY[i], f"early{i}") for i in range(2)]
-        for i in range(2):
-            add_second([i], firsts[i], 0, 0, EARLY[i])
-        add_second([2], pick_first([2], 0, EARLY[2], "early2"), 0, 0, EARLY[2])
-        first = pick_first([3], 0, HALF, "early3")
+        for i in range(3):
+            cuts = ((0, EARLY[i] - QUARTER), (EARLY[i] - QUARTER, QUARTER))
+            firsts = [pick_first([i], j, n, f"early{u}") for u, (j, n) in enumerate(cuts)]
+            for first, (j, n) in zip(firsts, cuts):
+                add_second([i], first, j, j, n)
+        first = pick_first([3], 0, QUARTER, "early1")
         quantise_wl(0)
-        add_second([3], first, 0, 0, QUARTER)
+        for j in range(0, QUARTER, P):
+            add_second([3], first, 0, j, P)
         for j in range(0, QUARTER, P):
             quantise_x(0, j, P)
-        log_of_b(0, 0)
-        add_second([3], first, 0, QUARTER, QUARTER)
+        log_of_b(0, 0, P)
+        add_second([3], pick_first([3], QUARTER, QUARTER, "early1"), QUARTER, QUARTER, QUARTER)
         quantise_wl(1)
+        behind_wl = held([P, 4, QUARTER], F32, "behind_wl", "wl_bf1")
+        x_bf[1] = behind_wl[:, 2:4, :].rearrange("p u j -> p (u j)").bitcast(BF16)
         quantise_x(1)
         log_of_b(0, 1, P)
-        late_rows = [i for i in range(4) if i == 3 or EARLY[i] <= HALF]
-        add_second(late_rows, pick_first(late_rows, HALF, QUARTER, "wl_bf1"), HALF, HALF, QUARTER)
+        for u, i in enumerate((2, 3)):
+            nc.vector.tensor_copy(behind_wl[:, u, :], x_rows[i][:].indirect(entries(list2, HALF, QUARTER)))
+        add_second([2, 3], behind_wl, HALF, HALF, QUARTER)
         log_of_b(1, 0)
         log_of_b(1, 1, P)
         quantise_x(2)
@@ -228,17 +239,20 @@ def tile_list_carbon_flux_features_kernel(
             w3_q[:].rearrange("p gb (t c e) -> p gb c t e", t=4, e=2),
             w3_raw[:].rearrange("p g (b c e t) -> p (g b) c t e", b=2, t=4, e=2),
         )
-        minus_dec = held([P, 2, 4], F32, "minus_dec")
-        nc.scalar.mul(minus_dec[:], dec_rows[:], -1.0)
+        minus_dec = [held([P, 4], F32, "minus_dec")] + [held([P, 4], F32, f"minus_dec{q}", f"h_s{q + 1}") for q in range(3)]
+        nc.scalar.mul(minus_dec[0][:], dec_rows[:, 0, :], -1.0)
+        minus_dec.append(held([P, 4], F32, "minus_dec_last"))
+        for q in range(4):
+            nc.scalar.mul(minus_dec[1 + q][:], dec_rows[:, 1, :], -1.0)
         w1_s = (w_s, w1_s1)
 
         gate = held([P, 4, 2, 4 * QUARTER], F32, "gate", "abs_b")
         a_halves = [held([P, 2, 2, 4 * QUARTER], F32, f"a_half{n}", tag) for n, tag in enumerate(("x_sum", ""))]
         a_rows = [a_halves[q // 2][:, q % 2, 0].rearrange("p (t j) -> p t j", t=4) for q in range(4)]
         a_pairs = [a_halves[q // 2][:, q % 2, 1].rearrange("p (c t e) -> p c t e", t=4, e=2) for q in range(4)]
-        h_bf = held([P, 3, 4 * QUARTER], BF16, "h_bf")
+        h_bf = held([P, 2, 4 * QUARTER], BF16, "h_bf")
         h_q = [held([P, 2, QUARTER], U32, f"h_q{q}") for q in range(4)]
-        h_s = [held([P, 2, QUARTER], U8, f"h_s{q}") for q in range(4)]
+        h_s = {}
 
         def make_gate(q, b, j=0, width=QUARTER):
             columns = slice(4 * j, 4 * (j + width))
@@ -247,7 +261,7 @@ def tile_list_carbon_flux_features_kernel(
         def product_a(q, b, jb, tag="a_bank"):
             j = q * QUARTER + jb
             half, jh = divmod(j, HALF)
-            bank = psum.tile([P, 4, P], F32, name="bank", tag=tag, bufs=BANKS)
+            bank = psum.tile([P, 4, P], F32, name="bank", tag=tag, bufs=BANKS[tag])
             for t in range(4):
                 for g in range(2):
                     nc.tensor.matmul_mx(
@@ -277,36 +291,37 @@ def tile_list_carbon_flux_features_kernel(
 
         def h_from_bank(q, b, jb, bank):
             nc.vector.tensor_tensor(
-                by_plot(h_bf[:, 2 * (q % 2), :], jb), bank[:].rearrange("p t j -> p j t"), by_plot(gate[:, q, b, :], jb), ALU.mult
+                by_plot(h_bf[:, b, :], jb), bank[:].rearrange("p t j -> p j t"), by_plot(gate[:, q, b, :], jb), ALU.mult
             )
 
         def quantise_h(q):
+            h_s[q] = held([P, 2, QUARTER], U8, f"h_s{q}")
             nc.vector.quantize_mx(
                 out=h_q[q][:].rearrange("p b j -> p (b j)").bitcast(FP8X4),
                 scales=h_s[q][:].rearrange("p b j -> p (b j)"),
-                in_=h_bf[:, q % 2:q % 2 + 2, :].rearrange("p b c -> p (b c)"),
+                in_=h_bf[:].rearrange("p b c -> p (b c)"),
             )
 
         out_view = out.rearrange("(b p t) j -> b p t j", b=2, t=4)
-        result_tags = ("wl_raw0", "wl_raw512", "wl_raw768", "tab_w1")
+        result_tags = ("wl_raw0", "wl_raw512", "tab_w0", "tab_w1")
 
         results = {}
 
-        def finish(q, b, pairs=(0, 2)):
+        def finish(q, b, pairs=(0, 2), tag=""):
             j0 = q * QUARTER
             if (q, b) not in results:
-                results[q, b] = held([P, 4, QUARTER], F32, f"result{q}{b}", result_tags[(2 * q + b) % 4])
+                results[q, b] = held([P, 4, QUARTER], F32, f"result{q}{b}", tag or result_tags[(2 * q + b) % 4])
             result = results[q, b]
             for pair in pairs:
-                y_bank = psum.tile([P, 2, QUARTER], F32, name="y_bank", tag="y_bank", bufs=BANKS)
+                y_bank = psum.tile([P, 2, QUARTER], F32, name="y_bank", tag="y_bank", bufs=BANKS["y_bank"])
                 for t in range(pair, pair + 2):
                     for g in range(2):
                         nc.tensor.matmul_mx(
                             out=y_bank[:, t - pair, :],
                             lhsT=w3_q[:, 2 * g + b, t * P:(t + 1) * P].bitcast(FP8X4),
                             lhsT_scale=w_s[8 + 4 * g:P, b * HALF + t * P:b * HALF + (t + 1) * P],
-                            rhs=h_q[q][:, (g + q) % 2, :].bitcast(FP8X4),
-                            rhs_scale=h_s[q][:, (g + q) % 2, :],
+                            rhs=h_q[q][:, g, :].bitcast(FP8X4),
+                            rhs_scale=h_s[q][:, g, :],
                             start=(g == 0),
                             stop=(g == 1),
                         )
@@ -314,7 +329,7 @@ def tile_list_carbon_flux_features_kernel(
                     nc.vector.scalar_tensor_tensor(
                         result[:, t, :].rearrange("p (c e) -> p c e", e=2),
                         a_pairs[q][:, :, t, :] if b else a_rows[q][:, t, :].rearrange("p (c e) -> p c e", e=2),
-                        minus_dec[:, b, t:t + 1],
+                        minus_dec[b * (1 + q + (q == 2 and pair > 0))][:, t:t + 1],
                         y_bank[:, t - pair, :].rearrange("p (c e) -> p c e", e=2),
                         ALU.mult,
                         ALU.add,
@@ -327,30 +342,38 @@ def tile_list_carbon_flux_features_kernel(
         for q in range(2):
             for jb in (0, P):
                 keep_pairs(nc.vector.tensor_copy, q, jb, product_a(q, 1, jb))
-        waiting = [product_a(2, 1, jb, "y_bank") for jb in (0, P)]
+        banks = {0: [product_a(0, 0, jb, "y_bank") for jb in (0, P)]}
+        pair_banks = {2: [product_a(2, 1, jb) for jb in (0, P)]}
+        banks[1] = [product_a(1, 0, jb) for jb in (0, P)]
         for jb in (0, P):
             for b in (1, 0):
                 make_gate(0, b, jb, P)
-        for q in range(5):
-            if q < 4:
-                banks = [product_a(q, 0, jb, "a_bank" if q else "y_bank") for jb in (0, P)]
-                for jb, bank in zip((0, P), banks):
+        for q in range(4):
+            for jb, bank in zip((0, P), banks[q]):
+                if (q, jb) != (3, P):
                     h_from_kept(q, jb)
-                    h_from_bank(q, 0, jb, bank)
-                    if q == 0:
-                        keep_pairs(nc.vector.tensor_copy, 2, jb, waiting[jb // P])
-                if q < 3:
-                    for b in ((0, 1) if q == 0 else (1, 0)):
-                        make_gate(q + 1, b)
-                for jb, bank in zip((0, P), banks):
-                    nc.scalar.copy(a_rows[q][:, :, jb:jb + P], bank[:])
-                if q == 0:
-                    for jb in (0, P):
-                        keep_pairs(nc.scalar.copy, 3, jb, product_a(3, 1, jb))
-            if q > 0:
+                h_from_bank(q, 0, jb, bank)
+            if q == 3:
+                h_from_bank(q, 1, P, pair_banks[3][1])
+                keep_pairs(nc.scalar.copy, 3, P, pair_banks[3][1])
+                finish(2, 1, (0,))
+            if q in (1, 2):
                 finish(q - 1, 1)
-                finish(q - 1, 0, (0,) if q in (3,) else (0, 2))
-            if q < 4:
-                quantise_h(q)
-            if q in (3,):
-                finish(q - 1, 0, (2,))
+                finish(q - 1, 0)
+                banks[q + 1] = [product_a(q + 1, 0, jb) for jb in (0, P)]
+            if q == 1:
+                pair_banks[3] = [product_a(3, 1, jb) for jb in (0, P)]
+            quantise_h(q)
+            if q < 3:
+                for b in (1, 0):
+                    make_gate(q + 1, b)
+            for jb, bank in zip((0, P), banks[q]):
+                nc.scalar.copy(a_rows[q][:, :, jb:jb + P], bank[:])
+            if q < 2:
+                for jb, bank in zip((0, P), pair_banks[q + 2]):
+                    if (q, jb) != (1, P):
+                        keep_pairs(nc.scalar.copy, q + 2, jb, bank)
+        finish(2, 1, (2,))
+        finish(2, 0)
+        finish(3, 1)
+        finish(3, 0)

@@ -281,11 +281,11 @@ def tile_list_carbon_flux_features_kernel(
         def keep_pairs(copy, q, jb, bank):
             copy(a_pairs[q][:, jb // 2:(jb + P) // 2], bank[:].rearrange("p t (c e) -> p c t e", e=2))
 
-        def h_from_kept(q, jb):
+        def h_from_kept(q, jb, width=P):
             nc.gpsimd.tensor_tensor(
-                h_bf[:, 1, 4 * jb:4 * (jb + P)].rearrange("p (c e t) -> p c e t", e=2, t=4),
-                a_pairs[q][:, jb // 2:(jb + P) // 2].rearrange("p c t e -> p c e t"),
-                gate[:, q, 1, 4 * jb:4 * (jb + P)].rearrange("p (c e t) -> p c e t", e=2, t=4),
+                h_bf[:, 1, 4 * jb:4 * (jb + width)].rearrange("p (c e t) -> p c e t", e=2, t=4),
+                a_pairs[q][:, jb // 2:(jb + width) // 2].rearrange("p c t e -> p c e t"),
+                gate[:, q, 1, 4 * jb:4 * (jb + width)].rearrange("p (c e t) -> p c e t", e=2, t=4),
                 ALU.mult,
             )
 
@@ -343,15 +343,15 @@ def tile_list_carbon_flux_features_kernel(
             for jb in (0, P):
                 keep_pairs(nc.vector.tensor_copy, q, jb, product_a(q, 1, jb))
         banks = {0: [product_a(0, 0, jb, "y_bank") for jb in (0, P)]}
-        pair_banks = {2: [product_a(2, 1, jb) for jb in (0, P)]}
+        pair_banks = {2: [product_a(2, 1, jb) for jb in (0, P)], 3: []}
         banks[1] = [product_a(1, 0, jb) for jb in (0, P)]
         for jb in (0, P):
             for b in (1, 0):
                 make_gate(0, b, jb, P)
         for q in range(4):
             for jb, bank in zip((0, P), banks[q]):
-                if (q, jb) != (3, P):
-                    h_from_kept(q, jb)
+                if jb == 0 or q == 0:
+                    h_from_kept(q, jb, QUARTER if q in (1, 2) else P)
                 h_from_bank(q, 0, jb, bank)
             if q == 3:
                 h_from_bank(q, 1, P, pair_banks[3][1])
@@ -361,12 +361,11 @@ def tile_list_carbon_flux_features_kernel(
                 finish(q - 1, 1)
                 finish(q - 1, 0)
                 banks[q + 1] = [product_a(q + 1, 0, jb) for jb in (0, P)]
-            if q == 1:
-                pair_banks[3] = [product_a(3, 1, jb) for jb in (0, P)]
+            if q in (1, 2):
+                pair_banks[3].append(product_a(3, 1, (q - 1) * P))
             quantise_h(q)
-            if q < 3:
-                for b in (1, 0):
-                    make_gate(q + 1, b)
+            for step in (((1, 1), (1, 0)), ((2, 1), (2, 0), (3, 1)), ((3, 0),), ())[q]:
+                make_gate(*step)
             for jb, bank in zip((0, P), banks[q]):
                 nc.scalar.copy(a_rows[q][:, :, jb:jb + P], bank[:])
             if q < 2:

@@ -90,40 +90,37 @@ def tile_list_carbon_flux_features_kernel(
         nc.sync.dma_start(w1_raw[:].bitcast(I32), w1_words.rearrange("g p n -> p g n").bitcast(I32))
         for g in range(2):
             nc.sync.dma_start(tab_w[g][:].bitcast(I32), tab_words[g].rearrange("p t i -> p (t i)").bitcast(I32))
-        nc.sync.dma_start(dec_rows[:], dec.rearrange("(b p t) -> p b t", b=2, t=4))
+        nc.sync.dma_start(dec_rows[:], dec.rearrange("(side p t) -> p side t", side=2, t=4))
         nc.sync.dma_start(w3_raw[:], w3_words.rearrange("g p n i -> p g (n i)").bitcast(I32))
 
         v_s_low = held([P, S], U8, "v_s_low")
         nc.vector.tensor_copy(v_s_low[:], tab_s[:].indirect(list1[:]))
 
-        wl_bf = [held([P, 4 * HALF], BF16, f"wl_bf{b}") for b in range(2)]
-        wl_q = [held([P, HALF], U32, f"wl_q{b}") for b in range(2)]
-        wl_s = [held([P, HALF], U8, f"wl_s{b}") for b in range(2)]
+        wl_bf = [held([P, 4 * HALF], BF16, f"wl_bf{side}") for side in range(2)]
+        wl_q = [held([P, HALF], U32, f"wl_q{side}") for side in range(2)]
+        wl_s = [held([P, HALF], U8, f"wl_s{side}") for side in range(2)]
+        for raw, (c, width) in zip(wl_raw, wl_cuts):
+            side, c0 = divmod(c, HALF)
+            nc.scalar.copy(
+                wl_bf[side][:].rearrange("p (t c i) -> p c t i", t=4, i=4)[:, c0 // 4:(c0 + width) // 4],
+                raw[:].rearrange("p i (c t) -> p c t i", t=4),
+            )
 
-        def round_wl(b):
-            by_column = wl_bf[b][:].rearrange("p (t c i) -> p c t i", t=4, i=4)
-            for n, (c, width) in enumerate(wl_cuts):
-                if c // HALF == b:
-                    c0 = c % HALF // 4
-                    nc.scalar.copy(
-                        by_column[:, c0:c0 + width // 4], wl_raw[n][:].rearrange("p i (c t) -> p c t i", t=4)
-                    )
+        def quantise_wl(side):
+            nc.vector.quantize_mx(out=wl_q[side][:].bitcast(FP8X4), scales=wl_s[side][:], in_=wl_bf[side][:])
 
-        def quantise_wl(b):
-            nc.vector.quantize_mx(out=wl_q[b][:].bitcast(FP8X4), scales=wl_s[b][:], in_=wl_bf[b][:])
-
-        for b in range(2):
-            round_wl(b)
         x_sum = held([P, 4, S], F32, "x_sum")
         x_bf = {q: held([P, 4 * QUARTER], BF16, f"x_bf{q}")[:] for q in (0, 2, 3)}
         x_q = [held([P, QUARTER], U32, f"x_q{q}") for q in range(4)]
         x_s = [held([P, QUARTER], U8, f"x_s{q}") for q in range(4)]
 
-        def pick_first(rows, j0, n, tag):
-            first = held([P, len(rows), n], F32, f"first{rows[0]}_{j0}", tag)
+        def pick_into(first, rows, j0, n):
             for u, i in enumerate(rows):
                 nc.vector.tensor_copy(first[:, u, :], x_rows[i][:].indirect(entries(list2, j0, n)))
             return first
+
+        def pick_first(rows, j0, n, tag):
+            return pick_into(held([P, len(rows), n], F32, f"first{rows[0]}_{j0}", tag), rows, j0, n)
 
         def add_second(rows, first, j0, j, n):
             for u, i in enumerate(rows):
@@ -148,35 +145,36 @@ def tile_list_carbon_flux_features_kernel(
 
         abs_b = held([P, 4, 2, 4 * QUARTER], F32, "abs_b")
         log_b = held([P, 4, 2, 4 * QUARTER], F32, "log_b")
-        abs_of = {(q, b): abs_b[:, q, b, :] for q in range(4) for b in range(2)}
-        log_of = {(q, b): log_b[:, q, b, :] for q in range(4) for b in range(2)}
+        abs_of = {(q, side): abs_b[:, q, side, :] for q in range(4) for side in range(2)}
+        log_of = {(q, side): log_b[:, q, side, :] for q in range(4) for side in range(2)}
         log_of[0, 1] = held([P, 4 * QUARTER], F32, "log_first", "a_half1")[:]
 
-        def abs_of_b(q, b, jb):
-            tag = "a_bank" if (4 * q + 2 * b + jb // P) % 8 < BANKS["a_bank"] else "y_bank"
+        def abs_of_b(q, side, jb):
+            turn = (4 * q + 2 * side + jb // P) % sum(BANKS.values())
+            tag = "a_bank" if turn < BANKS["a_bank"] else "y_bank"
             bank = psum.tile([P, 4, P], F32, name="bank", tag=tag, bufs=BANKS[tag])
             for t in range(4):
                 nc.tensor.matmul_mx(
                     out=bank[:, t, :],
-                    lhsT=wl_q[b][:, t * P:(t + 1) * P].bitcast(FP8X4),
-                    lhsT_scale=wl_s[b][:, t * P:(t + 1) * P],
+                    lhsT=wl_q[side][:, t * P:(t + 1) * P].bitcast(FP8X4),
+                    lhsT_scale=wl_s[side][:, t * P:(t + 1) * P],
                     rhs=x_q[q][:, jb:jb + P].bitcast(FP8X4),
                     rhs_scale=x_s[q][:, jb:jb + P],
                     start=True,
                     stop=True,
                 )
             nc.scalar.activation(
-                abs_of[q, b][:, 4 * jb:4 * (jb + P)].rearrange("p (j t) -> p j t", t=4),
+                abs_of[q, side][:, 4 * jb:4 * (jb + P)].rearrange("p (j t) -> p j t", t=4),
                 bank[:].rearrange("p t j -> p j t"),
                 ACT.Abs,
             )
 
-        def log_of_b(q, b, width=QUARTER):
+        def log_of_b(q, side, width=QUARTER):
             for jb in range(0, QUARTER, P):
-                abs_of_b(q, b, jb)
+                abs_of_b(q, side, jb)
             for j in range(0, QUARTER, width):
                 columns = slice(4 * j, 4 * (j + width))
-                nc.scalar.activation(log_of[q, b][:, columns], abs_of[q, b][:, columns], ACT.Ln, bias=TINY)
+                nc.scalar.activation(log_of[q, side][:, columns], abs_of[q, side][:, columns], ACT.Ln, bias=TINY)
 
         for i in range(3):
             cuts = ((0, EARLY[i] - QUARTER), (EARLY[i] - QUARTER, QUARTER))
@@ -196,15 +194,12 @@ def tile_list_carbon_flux_features_kernel(
         x_bf[1] = behind_wl[:, 2:4, :].rearrange("p u j -> p (u j)").bitcast(BF16)
         quantise_x(1)
         log_of_b(0, 1, P)
-        for u, i in enumerate((2, 3)):
-            nc.vector.tensor_copy(behind_wl[:, u, :], x_rows[i][:].indirect(entries(list2, HALF, QUARTER)))
-        add_second([2, 3], behind_wl, HALF, HALF, QUARTER)
+        add_second([2, 3], pick_into(behind_wl, [2, 3], HALF, QUARTER), HALF, HALF, QUARTER)
         log_of_b(1, 0)
         log_of_b(1, 1, P)
         quantise_x(2)
         last = 3 * QUARTER
-        all_rows = [i for i in range(4) if i == 3 or EARLY[i] <= last]
-        add_second(all_rows, pick_first(all_rows, last, QUARTER, "wl_bf1"), last, last, QUARTER)
+        add_second(range(4), pick_first(range(4), last, QUARTER, "wl_bf1"), last, last, QUARTER)
         log_of_b(2, 0)
         log_of_b(2, 1, P)
         for j in range(0, QUARTER, P):
@@ -218,17 +213,18 @@ def tile_list_carbon_flux_features_kernel(
                 row = TAB_ROW + 16 * g + 4 * d
                 nc.sync.dma_start(v_s[g][32 * d:32 * d + 4, :].bitcast(I32), v_s_low[row:row + 4, :].bitcast(I32))
         w_s = held([P, H], U8, "w_s", "x_rows1")
-        for b in range(2):
-            columns = slice(b * HALF, (b + 1) * HALF)
+        for side in range(2):
+            columns = slice(side * HALF, (side + 1) * HALF)
             nc.vector.tensor_copy(
                 w_s[:, columns].rearrange("p (t c e) -> p c t e", t=4, e=8),
                 w_s_raw[:, columns].rearrange("p (c e t) -> p c t e", t=4, e=8),
             )
         nc.sync.dma_start(w1_s1[0:P - 4, :].bitcast(I32), w_s[4:P, :].bitcast(I32))
+        w1_s = (w_s, w1_s1)
         w1_q = held([P, 4, 2 * HALF], U8, "w1_q", "x_rows3")
         nc.vector.tensor_copy(
-            w1_q[:].bitcast(U16).rearrange("p gb (t c e) -> p gb c t e", t=4, e=4),
-            w1_raw[:].bitcast(U16).rearrange("p g (b c e t) -> p (g b) c t e", b=2, t=4, e=4),
+            w1_q[:].bitcast(U16).rearrange("p gs (t c e) -> p gs c t e", t=4, e=4),
+            w1_raw[:].bitcast(U16).rearrange("p g (side c e t) -> p (g side) c t e", side=2, t=4, e=4),
         )
         v_q = [held([P, 2, HALF], U32, f"v_q{half}", tag) for half, tag in enumerate(("x_rows0", "wl_bf1"))]
         for half in range(2):
@@ -236,15 +232,15 @@ def tile_list_carbon_flux_features_kernel(
                 nc.vector.tensor_copy(v_q[half][:, g, :], tab_w[g][:].indirect(entries(list1, half * HALF, HALF)))
         w3_q = held([P, 4, HALF], I32, "w3_q", "x_rows2")
         nc.vector.tensor_copy(
-            w3_q[:].rearrange("p gb (t c e) -> p gb c t e", t=4, e=2),
-            w3_raw[:].rearrange("p g (b c e t) -> p (g b) c t e", b=2, t=4, e=2),
+            w3_q[:].rearrange("p gs (t c e) -> p gs c t e", t=4, e=2),
+            w3_raw[:].rearrange("p g (side c e t) -> p (g side) c t e", side=2, t=4, e=2),
         )
-        minus_dec = [held([P, 4], F32, "minus_dec")] + [held([P, 4], F32, f"minus_dec{q}", f"h_s{q + 1}") for q in range(3)]
-        nc.scalar.mul(minus_dec[0][:], dec_rows[:, 0, :], -1.0)
-        minus_dec.append(held([P, 4], F32, "minus_dec_last"))
-        for q in range(4):
-            nc.scalar.mul(minus_dec[1 + q][:], dec_rows[:, 1, :], -1.0)
-        w1_s = (w_s, w1_s1)
+        minus_dec0 = held([P, 4], F32, "minus_dec")
+        minus_dec1 = [held([P, 4], F32, f"minus_dec{q}", f"h_s{q + 1}") for q in range(3)]
+        nc.scalar.mul(minus_dec0[:], dec_rows[:, 0, :], -1.0)
+        minus_dec1.append(held([P, 4], F32, "minus_dec_last"))
+        for minus_dec in minus_dec1:
+            nc.scalar.mul(minus_dec[:], dec_rows[:, 1, :], -1.0)
 
         gate = held([P, 4, 2, 4 * QUARTER], F32, "gate", "abs_b")
         a_halves = [held([P, 2, 2, 4 * QUARTER], F32, f"a_half{n}", tag) for n, tag in enumerate(("x_sum", ""))]
@@ -254,20 +250,21 @@ def tile_list_carbon_flux_features_kernel(
         h_q = [held([P, 2, QUARTER], U32, f"h_q{q}") for q in range(4)]
         h_s = {}
 
-        def make_gate(q, b, j=0, width=QUARTER):
+        def make_gate(q, side, j=0, width=QUARTER):
             columns = slice(4 * j, 4 * (j + width))
-            nc.scalar.activation(gate[:, q, b, columns], log_of[q, b][:, columns], ACT.Sigmoid, scale=2.0)
+            nc.scalar.activation(gate[:, q, side, columns], log_of[q, side][:, columns], ACT.Sigmoid, scale=2.0)
 
-        def product_a(q, b, jb, tag="a_bank"):
+        def product_a(q, side, jb, tag="a_bank"):
             j = q * QUARTER + jb
             half, jh = divmod(j, HALF)
             bank = psum.tile([P, 4, P], F32, name="bank", tag=tag, bufs=BANKS[tag])
             for t in range(4):
+                columns = slice(side * HALF + t * P, side * HALF + (t + 1) * P)
                 for g in range(2):
                     nc.tensor.matmul_mx(
                         out=bank[:, t, :],
-                        lhsT=w1_q[:, 2 * g + b, 2 * t * P:2 * (t + 1) * P].bitcast(FP4X4),
-                        lhsT_scale=w1_s[g][:, b * HALF + t * P:b * HALF + (t + 1) * P],
+                        lhsT=w1_q[:, 2 * g + side, 2 * t * P:2 * (t + 1) * P].bitcast(FP4X4),
+                        lhsT_scale=w1_s[g][:, columns],
                         rhs=v_q[half][:, g, jh:jh + P].bitcast(FP8X4),
                         rhs_scale=v_s[g][:, j:j + P],
                         start=(g == 0),
@@ -275,104 +272,137 @@ def tile_list_carbon_flux_features_kernel(
                     )
             return bank
 
+        def products_a(q, side, tag="a_bank"):
+            return {jb: product_a(q, side, jb, tag) for jb in (0, P)}
+
         def by_plot(ap, jb):
             return ap[:, 4 * jb:4 * (jb + P)].rearrange("p (j t) -> p j t", t=4)
 
         def keep_pairs(copy, q, jb, bank):
             copy(a_pairs[q][:, jb // 2:(jb + P) // 2], bank[:].rearrange("p t (c e) -> p c t e", e=2))
 
-        def h_from_kept(q, jb, width=P):
+        def h_on_gpsimd(q, jb, width):
+            columns = slice(4 * jb, 4 * (jb + width))
             nc.gpsimd.tensor_tensor(
-                h_bf[:, 1, 4 * jb:4 * (jb + width)].rearrange("p (c e t) -> p c e t", e=2, t=4),
+                h_bf[:, 1, columns].rearrange("p (c e t) -> p c e t", e=2, t=4),
                 a_pairs[q][:, jb // 2:(jb + width) // 2].rearrange("p c t e -> p c e t"),
-                gate[:, q, 1, 4 * jb:4 * (jb + width)].rearrange("p (c e t) -> p c e t", e=2, t=4),
+                gate[:, q, 1, columns].rearrange("p (c e t) -> p c e t", e=2, t=4),
                 ALU.mult,
             )
 
-        def h_from_bank(q, b, jb, bank):
+        def h_on_vector(q, side, jb, bank):
             nc.vector.tensor_tensor(
-                by_plot(h_bf[:, b, :], jb), bank[:].rearrange("p t j -> p j t"), by_plot(gate[:, q, b, :], jb), ALU.mult
+                by_plot(h_bf[:, side, :], jb),
+                bank[:].rearrange("p t j -> p j t"),
+                by_plot(gate[:, q, side, :], jb),
+                ALU.mult,
             )
 
         def quantise_h(q):
             h_s[q] = held([P, 2, QUARTER], U8, f"h_s{q}")
             nc.vector.quantize_mx(
-                out=h_q[q][:].rearrange("p b j -> p (b j)").bitcast(FP8X4),
-                scales=h_s[q][:].rearrange("p b j -> p (b j)"),
-                in_=h_bf[:].rearrange("p b c -> p (b c)"),
+                out=h_q[q][:].rearrange("p g j -> p (g j)").bitcast(FP8X4),
+                scales=h_s[q][:].rearrange("p g j -> p (g j)"),
+                in_=h_bf[:].rearrange("p g c -> p (g c)"),
             )
 
-        out_view = out.rearrange("(b p t) j -> b p t j", b=2, t=4)
+        out_view = out.rearrange("(side p t) j -> side p t j", side=2, t=4)
         result_tags = ("wl_raw0", "wl_raw512", "tab_w0", "tab_w1")
-
         results = {}
 
-        def finish(q, b, pairs=(0, 2), tag=""):
-            j0 = q * QUARTER
-            if (q, b) not in results:
-                results[q, b] = held([P, 4, QUARTER], F32, f"result{q}{b}", tag or result_tags[(2 * q + b) % 4])
-            result = results[q, b]
-            for pair in pairs:
-                y_bank = psum.tile([P, 2, QUARTER], F32, name="y_bank", tag="y_bank", bufs=BANKS["y_bank"])
-                for t in range(pair, pair + 2):
-                    for g in range(2):
-                        nc.tensor.matmul_mx(
-                            out=y_bank[:, t - pair, :],
-                            lhsT=w3_q[:, 2 * g + b, t * P:(t + 1) * P].bitcast(FP8X4),
-                            lhsT_scale=w_s[8 + 4 * g:P, b * HALF + t * P:b * HALF + (t + 1) * P],
-                            rhs=h_q[q][:, g, :].bitcast(FP8X4),
-                            rhs_scale=h_s[q][:, g, :],
-                            start=(g == 0),
-                            stop=(g == 1),
-                        )
-                for t in range(pair, pair + 2):
-                    nc.vector.scalar_tensor_tensor(
-                        result[:, t, :].rearrange("p (c e) -> p c e", e=2),
-                        a_pairs[q][:, :, t, :] if b else a_rows[q][:, t, :].rearrange("p (c e) -> p c e", e=2),
-                        minus_dec[b * (1 + q + (q == 2 and pair > 0))][:, t:t + 1],
-                        y_bank[:, t - pair, :].rearrange("p (c e) -> p c e", e=2),
-                        ALU.mult,
-                        ALU.add,
+        def finish_pair(q, side, t0, minus_dec, one_by_one=False, queue=nc.sync):
+            plots = slice(q * QUARTER, (q + 1) * QUARTER)
+            if t0 == 0:
+                results[q, side] = held([P, 4, QUARTER], F32, f"result{q}{side}", result_tags[(2 * q + side) % 4])
+            result = results[q, side]
+            y_bank = psum.tile([P, 2, QUARTER], F32, name="y_bank", tag="y_bank", bufs=BANKS["y_bank"])
+            for t in (t0, t0 + 1):
+                for g in range(2):
+                    nc.tensor.matmul_mx(
+                        out=y_bank[:, t - t0, :],
+                        lhsT=w3_q[:, 2 * g + side, t * P:(t + 1) * P].bitcast(FP8X4),
+                        lhsT_scale=w_s[8 + 4 * g:P, side * HALF + t * P:side * HALF + (t + 1) * P],
+                        rhs=h_q[q][:, g, :].bitcast(FP8X4),
+                        rhs_scale=h_s[q][:, g, :],
+                        start=(g == 0),
+                        stop=(g == 1),
                     )
-                    if (q, b, pair) == (3, 0, 2):
-                        nc.sync.dma_start(out_view[b, :, t, j0:j0 + QUARTER], result[:, t, :])
-                if (q, b, pair) != (3, 0, 2):
-                    nc.sync.dma_start(out_view[b, :, pair:pair + 2, j0:j0 + QUARTER], result[:, pair:pair + 2, :])
+            for t in (t0, t0 + 1):
+                nc.vector.scalar_tensor_tensor(
+                    result[:, t, :].rearrange("p (c e) -> p c e", e=2),
+                    a_pairs[q][:, :, t, :] if side else a_rows[q][:, t, :].rearrange("p (c e) -> p c e", e=2),
+                    minus_dec[:, t:t + 1],
+                    y_bank[:, t - t0, :].rearrange("p (c e) -> p c e", e=2),
+                    ALU.mult,
+                    ALU.add,
+                )
+                if one_by_one:
+                    (nc.sync, nc.scalar)[t - t0].dma_start(out_view[side, :, t, plots], result[:, t, :])
+            if not one_by_one:
+                queue.dma_start(out_view[side, :, t0:t0 + 2, plots], result[:, t0:t0 + 2, :])
+
+        def finish(q, side, minus_dec):
+            for t0 in (0, 2):
+                finish_pair(q, side, t0, minus_dec)
+
+        def multiply(q, gpsimd_pieces):
+            for jb, bank in banks[q].items():
+                if jb in gpsimd_pieces:
+                    h_on_gpsimd(q, jb, gpsimd_pieces[jb])
+                h_on_vector(q, 0, jb, bank)
+
+        def keep_rows(q):
+            for jb, bank in banks[q].items():
+                nc.scalar.copy(a_rows[q][:, :, jb:jb + P], bank[:])
 
         for q in range(2):
             for jb in (0, P):
                 keep_pairs(nc.vector.tensor_copy, q, jb, product_a(q, 1, jb))
-        banks = {0: [product_a(0, 0, jb, "y_bank") for jb in (0, P)]}
-        pair_banks = {2: [product_a(2, 1, jb) for jb in (0, P)], 3: []}
-        banks[1] = [product_a(1, 0, jb) for jb in (0, P)]
+        banks = {0: products_a(0, 0, "y_bank")}
+        third_pairs = products_a(2, 1)
+        banks[1] = products_a(1, 0)
         for jb in (0, P):
-            for b in (1, 0):
-                make_gate(0, b, jb, P)
-        for q in range(4):
-            for jb, bank in zip((0, P), banks[q]):
-                if jb == 0 or q == 0:
-                    h_from_kept(q, jb, QUARTER if q in (1, 2) else P)
-                h_from_bank(q, 0, jb, bank)
-            if q == 3:
-                h_from_bank(q, 1, P, pair_banks[3][1])
-                keep_pairs(nc.scalar.copy, 3, P, pair_banks[3][1])
-                finish(2, 1, (0,))
-            if q in (1, 2):
-                finish(q - 1, 1)
-                finish(q - 1, 0)
-                banks[q + 1] = [product_a(q + 1, 0, jb) for jb in (0, P)]
-            if q in (1, 2):
-                pair_banks[3].append(product_a(3, 1, (q - 1) * P))
-            quantise_h(q)
-            for step in (((1, 1), (1, 0)), ((2, 1), (2, 0), (3, 1)), ((3, 0),), ())[q]:
-                make_gate(*step)
-            for jb, bank in zip((0, P), banks[q]):
-                nc.scalar.copy(a_rows[q][:, :, jb:jb + P], bank[:])
-            if q < 2:
-                for jb, bank in zip((0, P), pair_banks[q + 2]):
-                    if (q, jb) != (1, P):
-                        keep_pairs(nc.scalar.copy, q + 2, jb, bank)
-        finish(2, 1, (2,))
-        finish(2, 0)
-        finish(3, 1)
-        finish(3, 0)
+            for side in (1, 0):
+                make_gate(0, side, jb, P)
+
+        multiply(0, {0: P, P: P})
+        quantise_h(0)
+        make_gate(1, 1)
+        make_gate(1, 0)
+        keep_rows(0)
+        for jb, bank in third_pairs.items():
+            keep_pairs(nc.scalar.copy, 2, jb, bank)
+
+        multiply(1, {0: QUARTER})
+        finish(0, 1, minus_dec1[0])
+        finish(0, 0, minus_dec0)
+        banks[2] = products_a(2, 0)
+        last_pairs = product_a(3, 1, 0)
+        quantise_h(1)
+        make_gate(2, 1)
+        make_gate(2, 0)
+        make_gate(3, 1)
+        keep_rows(1)
+        keep_pairs(nc.scalar.copy, 3, 0, last_pairs)
+
+        multiply(2, {0: QUARTER})
+        finish(1, 1, minus_dec1[1])
+        finish(1, 0, minus_dec0)
+        banks[3] = products_a(3, 0)
+        last_bank = product_a(3, 1, P)
+        quantise_h(2)
+        make_gate(3, 0)
+        keep_rows(2)
+
+        multiply(3, {0: P})
+        h_on_vector(3, 1, P, last_bank)
+        keep_pairs(nc.scalar.copy, 3, P, last_bank)
+        finish_pair(2, 1, 0, minus_dec1[2])
+        quantise_h(3)
+        keep_rows(3)
+        finish_pair(2, 1, 2, minus_dec1[3])
+        for q, side, minus_dec in ((2, 0, minus_dec0), (3, 1, minus_dec1[3])):
+            finish_pair(q, side, 0, minus_dec)
+            finish_pair(q, side, 2, minus_dec, queue=nc.scalar)
+        finish_pair(3, 0, 0, minus_dec0)
+        finish_pair(3, 0, 2, minus_dec0, one_by_one=True)

@@ -23,7 +23,6 @@ PER_COLUMN = 16
 WL_PIECE = 256
 BANKS = {"a_bank": 5, "y_bank": 3}
 TAB_ROW = 96
-EARLY = (768, 768, 512)
 TINY = 2.0 ** -60
 
 
@@ -33,10 +32,14 @@ def tile_list_carbon_flux_features_kernel(
     nc = tc.nc
     with ExitStack() as ctx:
         keep = ctx.enter_context(tc.tile_pool(name="keep", bufs=1))
+        placed = ctx.enter_context(tc.tile_pool(name="placed", bufs=1))
         psum = ctx.enter_context(tc.psum_pool(name="psum", bufs=1))
 
         def held(shape, dtype, name, tag=""):
             return keep.tile(shape, dtype, name=name, tag=tag or name, align_bytes=64)
+
+        def at(offset, shape, dtype, name):
+            return placed.tile(shape, dtype, name=name, align_bytes=64, offset=offset)
 
         def entries(list_tile, j, n):
             return list_tile[:, j // PER_COLUMN:(j + n) // PER_COLUMN]
@@ -45,9 +48,11 @@ def tile_list_carbon_flux_features_kernel(
         list2 = held([P, S // PER_COLUMN], U16, "list2")
         list3 = held([P, S // PER_COLUMN], U16, "list3")
         x_rows = [held([P, T], F32, f"x_rows{i}") for i in range(4)]
-        wl_cuts = ((0, HALF), (HALF, WL_PIECE), (HALF + WL_PIECE, WL_PIECE))
-        wl_tags = ("", "", "abs_b")
-        wl_raw = [held([P, 4, n], F32, f"wl_raw{c}", tag) for (c, n), tag in zip(wl_cuts, wl_tags)]
+        wl_cuts = tuple((c, WL_PIECE) for c in range(0, H, WL_PIECE))
+        piece_bytes = 4 * 4 * WL_PIECE
+        wl_raw = [held([P, 4, n], F32, f"wl_raw{c}") for c, n in wl_cuts[0::2]]
+        wl_raw.insert(1, at(0, [P, 4, WL_PIECE], F32, "wl_raw_last0"))
+        wl_raw.append(at(piece_bytes, [P, 4, WL_PIECE], F32, "wl_raw_last1"))
         tab_w = [held([P, T], U32, f"tab_w{g}") for g in range(2)]
         tab_s = held([P, T], U8, "tab_s")
         w_s_raw = held([P, H], U8, "w_s_raw")
@@ -79,19 +84,18 @@ def tile_list_carbon_flux_features_kernel(
         nc.sync.dma_start(list3[:], offs3)
         nc.sync.dma_start(x_rows[1][:], x_view[:, 1, :])
         nc.sync.dma_start(x_rows[2][:], x_view[:, 2, :])
-        load_wl(0)
         nc.sync.dma_start(x_rows[3][:], x_view[:, 3, :])
-        load_wl(1)
-        load_wl(2)
+        for n in range(len(wl_cuts)):
+            load_wl(n)
         for d in range(4):
             rows = slice(4 * d, 4 * d + 4)
             nc.sync.dma_start(w_s_raw[32 * d:32 * d + 8, :].bitcast(I32), w1_scales[:, rows, :].bitcast(I32))
             nc.sync.dma_start(w_s_raw[32 * d + 8:32 * d + 16, :].bitcast(I32), w3_scales[:, rows, :].bitcast(I32))
         nc.sync.dma_start(w1_raw[:].bitcast(I32), w1_words.rearrange("g p n -> p g n").bitcast(I32))
+        nc.sync.dma_start(w3_raw[:], w3_words.rearrange("g p n i -> p g (n i)").bitcast(I32))
         for g in range(2):
             nc.sync.dma_start(tab_w[g][:].bitcast(I32), tab_words[g].rearrange("p t i -> p (t i)").bitcast(I32))
         nc.sync.dma_start(dec_rows[:], dec.rearrange("(side p t) -> p side t", side=2, t=4))
-        nc.sync.dma_start(w3_raw[:], w3_words.rearrange("g p n i -> p g (n i)").bitcast(I32))
 
         v_s_low = held([P, S], U8, "v_s_low")
         nc.vector.tensor_copy(v_s_low[:], tab_s[:].indirect(list1[:]))
@@ -109,34 +113,25 @@ def tile_list_carbon_flux_features_kernel(
         def quantise_wl(side):
             nc.vector.quantize_mx(out=wl_q[side][:].bitcast(FP8X4), scales=wl_s[side][:], in_=wl_bf[side][:])
 
-        x_sum = held([P, 4, S], F32, "x_sum")
-        x_bf = {q: held([P, 4 * QUARTER], BF16, f"x_bf{q}")[:] for q in (0, 2, 3)}
+        x_sum = [held([P, 4, QUARTER], F32, f"x_sum{q}") for q in range(4)]
         x_q = [held([P, QUARTER], U32, f"x_q{q}") for q in range(4)]
-        x_s = [held([P, QUARTER], U8, f"x_s{q}") for q in range(4)]
+        x_bf = {q: held([P, 4 * QUARTER], BF16, f"x_bf{q}")[:] for q in (0, 2, 3)}
+        x_s = {q: held([P, QUARTER], U8, f"x_s{q}")[:] for q in (2, 3)}
 
-        def pick_into(first, rows, j0, n):
-            for u, i in enumerate(rows):
-                nc.vector.tensor_copy(first[:, u, :], x_rows[i][:].indirect(entries(list2, j0, n)))
-            return first
+        def pick(first, i, q):
+            nc.vector.tensor_copy(first, x_rows[i][:].indirect(entries(list2, q * QUARTER, QUARTER)))
 
-        def pick_first(rows, j0, n, tag):
-            return pick_into(held([P, len(rows), n], F32, f"first{rows[0]}_{j0}", tag), rows, j0, n)
+        def add(first, i, q):
+            picked = x_rows[i][:].indirect(entries(list3, q * QUARTER, QUARTER))
+            nc.vector.tensor_tensor(x_sum[q][:, i, :], picked, first, ALU.add)
 
-        def add_second(rows, first, j0, j, n):
-            for u, i in enumerate(rows):
-                nc.vector.tensor_tensor(
-                    x_sum[:, i, j:j + n],
-                    x_rows[i][:].indirect(entries(list3, j, n)),
-                    first[:, u, j - j0:j - j0 + n],
-                    ALU.add,
-                )
-
-        def quantise_x(q, j=0, width=QUARTER):
-            j0 = q * QUARTER + j
+        def interleave(q, j=0, width=QUARTER):
             nc.vector.tensor_copy(
                 x_bf[q][:, 4 * j:4 * (j + width)].rearrange("p (c e i) -> p c i e", e=2, i=4),
-                x_sum[:, :, j0:j0 + width].rearrange("p i (c e) -> p c i e", e=2),
+                x_sum[q][:, :, j:j + width].rearrange("p i (c e) -> p c i e", e=2),
             )
+
+        def quantise_x(q, j=0, width=QUARTER):
             nc.vector.quantize_mx(
                 out=x_q[q][:, j:j + width].bitcast(FP8X4),
                 scales=x_s[q][:, j:j + width],
@@ -176,35 +171,46 @@ def tile_list_carbon_flux_features_kernel(
                 columns = slice(4 * j, 4 * (j + width))
                 nc.scalar.activation(log_of[q, side][:, columns], abs_of[q, side][:, columns], ACT.Ln, bias=TINY)
 
-        for i in range(3):
-            cuts = ((0, EARLY[i] - QUARTER), (EARLY[i] - QUARTER, QUARTER))
-            firsts = [pick_first([i], j, n, f"early{u}") for u, (j, n) in enumerate(cuts)]
-            for first, (j, n) in zip(firsts, cuts):
-                add_second([i], first, j, j, n)
-        first = pick_first([3], 0, QUARTER, "early1")
+        for i in range(4):
+            firsts = [held([P, QUARTER], F32, f"first{i}{q}", f"early{q}")[:] for q in range(2)]
+            for q in range(2):
+                pick(firsts[q], i, q)
+            for q in range(2):
+                add(firsts[q], i, q)
+        interleave(0)
         quantise_wl(0)
-        for j in range(0, QUARTER, P):
-            add_second([3], first, 0, j, P)
-        for j in range(0, QUARTER, P):
-            quantise_x(0, j, P)
+        x_s[0] = at(0, [P, QUARTER], U8, "x_s0")[:]
+        x_bf[1] = at(QUARTER, [P, 4 * QUARTER], BF16, "x_bf1")[:]
+        quantise_x(0)
         log_of_b(0, 0, P)
-        add_second([3], pick_first([3], QUARTER, QUARTER, "early1"), QUARTER, QUARTER, QUARTER)
+        interleave(1)
         quantise_wl(1)
-        behind_wl = held([P, 4, QUARTER], F32, "behind_wl", "wl_bf1")
-        x_bf[1] = behind_wl[:, 2:4, :].rearrange("p u j -> p (u j)").bitcast(BF16)
+        x_s[1] = at(piece_bytes, [P, QUARTER], U8, "x_s1")[:]
+        third = at(piece_bytes + QUARTER, [P, 4, QUARTER], F32, "third")
+        firsts = [third[:, i, :] for i in range(4)]
         quantise_x(1)
         log_of_b(0, 1, P)
-        add_second([2, 3], pick_into(behind_wl, [2, 3], HALF, QUARTER), HALF, HALF, QUARTER)
+        for i in range(4):
+            pick(firsts[i], i, 2)
+        for i in range(4):
+            add(firsts[i], i, 2)
         log_of_b(1, 0)
         log_of_b(1, 1, P)
+        interleave(2)
         quantise_x(2)
-        last = 3 * QUARTER
-        add_second(range(4), pick_first(range(4), last, QUARTER, "wl_bf1"), last, last, QUARTER)
+        late = held([P, 2, QUARTER], F32, "late", "x_sum2")
+        firsts = [firsts[0], firsts[3], late[:, 0, :], late[:, 1, :]]
+        for i in range(4):
+            pick(firsts[i], i, 3)
+        for i in range(4):
+            add(firsts[i], i, 3)
         log_of_b(2, 0)
         log_of_b(2, 1, P)
-        for j in range(0, QUARTER, P):
+        for j in (0, P):
+            interleave(3, j, P)
+        for j in (0, P):
             quantise_x(3, j, P)
-        abs_of[3, 0] = held([P, 4 * QUARTER], F32, "abs_late", "x_sum")[:]
+        abs_of[3, 0] = held([P, 4 * QUARTER], F32, "abs_late", "x_rows2")[:]
         log_of_b(3, 0)
         log_of_b(3, 1, P)
 
@@ -221,19 +227,20 @@ def tile_list_carbon_flux_features_kernel(
             )
         nc.sync.dma_start(w1_s1[0:P - 4, :].bitcast(I32), w_s[4:P, :].bitcast(I32))
         w1_s = (w_s, w1_s1)
-        w1_q = held([P, 4, 2 * HALF], U8, "w1_q", "x_rows3")
+        w1_q = held([P, 4, 2 * HALF], U8, "w1_q", "x_sum3")
         nc.vector.tensor_copy(
             w1_q[:].bitcast(U16).rearrange("p gs (t c e) -> p gs c t e", t=4, e=4),
             w1_raw[:].bitcast(U16).rearrange("p g (side c e t) -> p (g side) c t e", side=2, t=4, e=4),
         )
-        v_q = [held([P, 2, HALF], U32, f"v_q{half}", tag) for half, tag in enumerate(("x_rows0", "wl_bf1"))]
+        v_words = held([P, 2, 2, HALF], U32, "v_words", "x_bf3")
+        v_q = [v_words[:, half] for half in range(2)]
         for half in range(2):
             for g in range(2):
                 nc.vector.tensor_copy(v_q[half][:, g, :], tab_w[g][:].indirect(entries(list1, half * HALF, HALF)))
-        w3_q = held([P, 4, HALF], I32, "w3_q", "x_rows2")
-        nc.vector.tensor_copy(
-            w3_q[:].rearrange("p gs (t c e) -> p gs c t e", t=4, e=2),
-            w3_raw[:].rearrange("p g (side c e t) -> p (g side) c t e", side=2, t=4, e=2),
+        w3_q = held([P, 4, HALF], I32, "w3_q", "w1_raw")
+        nc.gpsimd.tensor_copy(
+            w3_q[:].rearrange("p gs (t c) -> p gs t c", t=4),
+            w3_raw[:].rearrange("p g (side c t) -> p (g side) t c", side=2, t=4),
         )
         minus_dec0 = held([P, 4], F32, "minus_dec")
         minus_dec1 = [held([P, 4], F32, f"minus_dec{q}", f"h_s{q + 1}") for q in range(3)]
@@ -243,7 +250,7 @@ def tile_list_carbon_flux_features_kernel(
             nc.scalar.mul(minus_dec[:], dec_rows[:, 1, :], -1.0)
 
         gate = held([P, 4, 2, 4 * QUARTER], F32, "gate", "abs_b")
-        a_halves = [held([P, 2, 2, 4 * QUARTER], F32, f"a_half{n}", tag) for n, tag in enumerate(("x_sum", ""))]
+        a_halves = [held([P, 2, 2, 4 * QUARTER], F32, f"a_half{n}", tag) for n, tag in enumerate(("x_rows2", ""))]
         a_rows = [a_halves[q // 2][:, q % 2, 0].rearrange("p (t j) -> p t j", t=4) for q in range(4)]
         a_pairs = [a_halves[q // 2][:, q % 2, 1].rearrange("p (c t e) -> p c t e", t=4, e=2) for q in range(4)]
         h_bf = held([P, 2, 4 * QUARTER], BF16, "h_bf")

@@ -23,6 +23,7 @@ PER_COLUMN = 16
 WL_PIECE = 256
 BANKS = {"a_bank": 5, "y_bank": 3}
 TAB_ROW = 96
+EARLY = (3, 2, 2)
 TINY = 2.0 ** -60
 
 
@@ -48,11 +49,10 @@ def tile_list_carbon_flux_features_kernel(
         list2 = held([P, S // PER_COLUMN], U16, "list2")
         list3 = held([P, S // PER_COLUMN], U16, "list3")
         x_rows = [held([P, T], F32, f"x_rows{i}") for i in range(4)]
-        wl_cuts = tuple((c, WL_PIECE) for c in range(0, H, WL_PIECE))
+        wl_cuts = ((0, HALF), (HALF, WL_PIECE), (HALF + WL_PIECE, WL_PIECE))
         piece_bytes = 4 * 4 * WL_PIECE
-        wl_raw = [held([P, 4, n], F32, f"wl_raw{c}") for c, n in wl_cuts[0::2]]
-        wl_raw.insert(1, at(0, [P, 4, WL_PIECE], F32, "wl_raw_last0"))
-        wl_raw.append(at(piece_bytes, [P, 4, WL_PIECE], F32, "wl_raw_last1"))
+        wl_raw = [held([P, 4, n], F32, f"wl_raw{c}") for c, n in wl_cuts[0:2]]
+        wl_raw.append(at(piece_bytes - 64, [P, 4, WL_PIECE], F32, "wl_raw_last"))
         tab_w = [held([P, T], U32, f"tab_w{g}") for g in range(2)]
         tab_s = held([P, T], U8, "tab_s")
         w_s_raw = held([P, H], U8, "w_s_raw")
@@ -84,9 +84,10 @@ def tile_list_carbon_flux_features_kernel(
         nc.sync.dma_start(list3[:], offs3)
         nc.sync.dma_start(x_rows[1][:], x_view[:, 1, :])
         nc.sync.dma_start(x_rows[2][:], x_view[:, 2, :])
+        load_wl(0)
         nc.sync.dma_start(x_rows[3][:], x_view[:, 3, :])
-        for n in range(len(wl_cuts)):
-            load_wl(n)
+        load_wl(1)
+        load_wl(2)
         for d in range(4):
             rows = slice(4 * d, 4 * d + 4)
             nc.sync.dma_start(w_s_raw[32 * d:32 * d + 8, :].bitcast(I32), w1_scales[:, rows, :].bitcast(I32))
@@ -106,8 +107,8 @@ def tile_list_carbon_flux_features_kernel(
         for raw, (c, width) in zip(wl_raw, wl_cuts):
             side, c0 = divmod(c, HALF)
             nc.scalar.copy(
-                wl_bf[side][:].rearrange("p (t c i) -> p c t i", t=4, i=4)[:, c0 // 4:(c0 + width) // 4],
-                raw[:].rearrange("p i (c t) -> p c t i", t=4),
+                wl_bf[side][:].rearrange("p (u e c i) -> p c u i e", u=2, e=2, i=4)[:, c0 // 4:(c0 + width) // 4],
+                raw[:].rearrange("p i (c u e) -> p c u i e", u=2, e=2),
             )
 
         def quantise_wl(side):
@@ -116,14 +117,14 @@ def tile_list_carbon_flux_features_kernel(
         x_sum = [held([P, 4, QUARTER], F32, f"x_sum{q}") for q in range(4)]
         x_q = [held([P, QUARTER], U32, f"x_q{q}") for q in range(4)]
         x_bf = {q: held([P, 4 * QUARTER], BF16, f"x_bf{q}")[:] for q in (0, 2, 3)}
-        x_s = {q: held([P, QUARTER], U8, f"x_s{q}")[:] for q in (2, 3)}
+        x_s = {q: held([P, QUARTER], U8, f"x_s{q}")[:] for q in (0, 2, 3)}
 
-        def pick(first, i, q):
-            nc.vector.tensor_copy(first, x_rows[i][:].indirect(entries(list2, q * QUARTER, QUARTER)))
+        def pick(first, i, q, j=0, width=QUARTER):
+            nc.vector.tensor_copy(first, x_rows[i][:].indirect(entries(list2, q * QUARTER + j, width)))
 
-        def add(first, i, q):
-            picked = x_rows[i][:].indirect(entries(list3, q * QUARTER, QUARTER))
-            nc.vector.tensor_tensor(x_sum[q][:, i, :], picked, first, ALU.add)
+        def add(first, i, q, j=0, width=QUARTER):
+            picked = x_rows[i][:].indirect(entries(list3, q * QUARTER + j, width))
+            nc.vector.tensor_tensor(x_sum[q][:, i, j:j + width], picked, first, ALU.add)
 
         def interleave(q, j=0, width=QUARTER):
             nc.vector.tensor_copy(
@@ -171,35 +172,45 @@ def tile_list_carbon_flux_features_kernel(
                 columns = slice(4 * j, 4 * (j + width))
                 nc.scalar.activation(log_of[q, side][:, columns], abs_of[q, side][:, columns], ACT.Ln, bias=TINY)
 
-        for i in range(4):
-            firsts = [held([P, QUARTER], F32, f"first{i}{q}", f"early{q}")[:] for q in range(2)]
-            for q in range(2):
+        for i, quarters in enumerate(EARLY):
+            firsts = [held([P, QUARTER], F32, f"first{i}{q}", f"early{q}")[:] for q in range(quarters)]
+            pick(firsts[0], i, 0)
+            for q in range(1, quarters):
                 pick(firsts[q], i, q)
-            for q in range(2):
-                add(firsts[q], i, q)
-        interleave(0)
+                add(firsts[q - 1], i, q - 1)
+            add(firsts[-1], i, quarters - 1)
+        first = held([P, QUARTER], F32, "first30", "early0")
+        pick(first[:, 0:P], 3, 0, 0, P)
         quantise_wl(0)
-        x_s[0] = at(0, [P, QUARTER], U8, "x_s0")[:]
-        x_bf[1] = at(QUARTER, [P, 4 * QUARTER], BF16, "x_bf1")[:]
-        quantise_x(0)
+        add(first[:, 0:P], 3, 0, 0, P)
+        pick(first[:, P:], 3, 0, P, P)
+        interleave(0, 0, P)
+        add(first[:, P:], 3, 0, P, P)
+        quantise_x(0, 0, P)
+        first = held([P, QUARTER], F32, "first31", "early0")[:]
+        pick(first, 3, 1)
+        interleave(0, P, P)
+        add(first, 3, 1)
+        quantise_x(0, P, P)
+        abs_of[0, 0] = at(0, [P, 4 * QUARTER], F32, "abs_first")[:]
         log_of_b(0, 0, P)
-        interleave(1)
         quantise_wl(1)
         x_s[1] = at(piece_bytes, [P, QUARTER], U8, "x_s1")[:]
-        third = at(piece_bytes + QUARTER, [P, 4, QUARTER], F32, "third")
-        firsts = [third[:, i, :] for i in range(4)]
+        x_bf[1] = at(piece_bytes + QUARTER, [P, 4 * QUARTER], BF16, "x_bf1")[:]
+        third = at(piece_bytes + 9 * QUARTER, [P, 3, QUARTER], F32, "third")
+        interleave(1)
         quantise_x(1)
         log_of_b(0, 1, P)
-        for i in range(4):
-            pick(firsts[i], i, 2)
-        for i in range(4):
-            add(firsts[i], i, 2)
+        for i in range(1, 4):
+            pick(third[:, i - 1, :], i, 2)
+        for i in range(1, 4):
+            add(third[:, i - 1, :], i, 2)
         log_of_b(1, 0)
         log_of_b(1, 1, P)
         interleave(2)
         quantise_x(2)
         late = held([P, 2, QUARTER], F32, "late", "x_sum2")
-        firsts = [firsts[0], firsts[3], late[:, 0, :], late[:, 1, :]]
+        firsts = [third[:, 0, :], third[:, 2, :], late[:, 0, :], late[:, 1, :]]
         for i in range(4):
             pick(firsts[i], i, 3)
         for i in range(4):
@@ -253,8 +264,9 @@ def tile_list_carbon_flux_features_kernel(
         a_halves = [held([P, 2, 2, 4 * QUARTER], F32, f"a_half{n}", tag) for n, tag in enumerate(("x_rows2", ""))]
         a_rows = [a_halves[q // 2][:, q % 2, 0].rearrange("p (t j) -> p t j", t=4) for q in range(4)]
         a_pairs = [a_halves[q // 2][:, q % 2, 1].rearrange("p (c t e) -> p c t e", t=4, e=2) for q in range(4)]
-        h_bf = held([P, 2, 4 * QUARTER], BF16, "h_bf")
-        h_q = [held([P, 2, QUARTER], U32, f"h_q{q}") for q in range(4)]
+        h_bf = held([P, 2, 4 * QUARTER], BF16, "h_bf", "wl_bf0")
+        h_tags = ("wl_bf1", "x_sum0", "x_sum1", "x_rows3")
+        h_q = [held([P, 2, QUARTER], U32, f"h_q{q}", tag) for q, tag in enumerate(h_tags)]
         h_s = {}
 
         def make_gate(q, side, j=0, width=QUARTER):

@@ -55,8 +55,9 @@ def tile_list_carbon_flux_features_kernel(
         wl_raw.append(at(piece_bytes - 64, [P, 4, WL_PIECE], F32, "wl_raw_last"))
         tab_w = [held([P, T], U32, f"tab_w{g}") for g in range(2)]
         tab_s = held([P, T], U8, "tab_s")
-        w_s_raw = held([P, H], U8, "w_s_raw")
-        w1_raw = held([P, 2, 2 * H], U8, "w1_raw")
+        raw_place = piece_bytes + 41 * QUARTER
+        w_s_raw = at(raw_place, [P, H], U8, "w_s_raw")
+        w1_raw = at(raw_place + H, [P, 2, 2 * H], U8, "w1_raw")
         w3_raw = held([P, 2, H], I32, "w3_raw")
         dec_rows = held([P, 2, 4], F32, "dec_rows")
         v_s = [held([P, S], U8, f"v_s{g}") for g in range(2)]
@@ -114,7 +115,9 @@ def tile_list_carbon_flux_features_kernel(
         def quantise_wl(side):
             nc.vector.quantize_mx(out=wl_q[side][:].bitcast(FP8X4), scales=wl_s[side][:], in_=wl_bf[side][:])
 
-        x_sum = [held([P, 4, QUARTER], F32, f"x_sum{q}") for q in range(4)]
+        x_sum = {q: held([P, 4, QUARTER], F32, f"x_sum{q}") for q in range(2)}
+        sum_place = piece_bytes + 21 * QUARTER
+        x_sum[2] = at(sum_place, [P, 4, QUARTER], F32, "x_sum2")
         x_q = [held([P, QUARTER], U32, f"x_q{q}") for q in range(4)]
         x_bf = {q: held([P, 4 * QUARTER], BF16, f"x_bf{q}")[:] for q in (0, 2, 3)}
         x_s = {q: held([P, QUARTER], U8, f"x_s{q}")[:] for q in (0, 2, 3)}
@@ -180,18 +183,17 @@ def tile_list_carbon_flux_features_kernel(
                 add(firsts[q - 1], i, q - 1)
             add(firsts[-1], i, quarters - 1)
         first = held([P, QUARTER], F32, "first30", "early0")
-        pick(first[:, 0:P], 3, 0, 0, P)
+        pick(first[:], 3, 0)
         quantise_wl(0)
-        add(first[:, 0:P], 3, 0, 0, P)
-        pick(first[:, P:], 3, 0, P, P)
-        interleave(0, 0, P)
-        add(first[:, P:], 3, 0, P, P)
-        quantise_x(0, 0, P)
+        for j in (0, P):
+            add(first[:, j:j + P], 3, 0, j, P)
+        for j in (0, P):
+            interleave(0, j, P)
+        for j in (0, P):
+            quantise_x(0, j, P)
         first = held([P, QUARTER], F32, "first31", "early0")[:]
         pick(first, 3, 1)
-        interleave(0, P, P)
         add(first, 3, 1)
-        quantise_x(0, P, P)
         abs_of[0, 0] = at(0, [P, 4 * QUARTER], F32, "abs_first")[:]
         log_of_b(0, 0, P)
         quantise_wl(1)
@@ -207,10 +209,13 @@ def tile_list_carbon_flux_features_kernel(
             add(third[:, i - 1, :], i, 2)
         log_of_b(1, 0)
         log_of_b(1, 1, P)
-        interleave(2)
+        nc.gpsimd.tensor_scalar(
+            x_bf[2].rearrange("p (c i) -> p c i", i=4), x_sum[2][:].rearrange("p i c -> p c i"), 1.0, 0.0, ALU.mult, ALU.add
+        )
         quantise_x(2)
-        late = held([P, 2, QUARTER], F32, "late", "x_sum2")
-        firsts = [third[:, 0, :], third[:, 2, :], late[:, 0, :], late[:, 1, :]]
+        late = at(sum_place, [P, QUARTER], F32, "late")
+        x_sum[3] = at(sum_place + 4 * QUARTER, [P, 4, QUARTER], F32, "x_sum3")
+        firsts = [third[:, 0, :], third[:, 1, :], third[:, 2, :], late[:]]
         for i in range(4):
             pick(firsts[i], i, 3)
         for i in range(4):
@@ -230,15 +235,13 @@ def tile_list_carbon_flux_features_kernel(
                 row = TAB_ROW + 16 * g + 4 * d
                 nc.sync.dma_start(v_s[g][32 * d:32 * d + 4, :].bitcast(I32), v_s_low[row:row + 4, :].bitcast(I32))
         w_s = held([P, H], U8, "w_s", "x_rows1")
-        for side in range(2):
-            columns = slice(side * HALF, (side + 1) * HALF)
-            nc.vector.tensor_copy(
-                w_s[:, columns].rearrange("p (t c e) -> p c t e", t=4, e=8),
-                w_s_raw[:, columns].rearrange("p (c e t) -> p c t e", t=4, e=8),
-            )
+        nc.vector.tensor_copy(
+            w_s[:].rearrange("p (side t c e) -> p side c t e", side=2, t=4, e=8),
+            w_s_raw[:].rearrange("p (side c e t) -> p side c t e", side=2, t=4, e=8),
+        )
         nc.sync.dma_start(w1_s1[0:P - 4, :].bitcast(I32), w_s[4:P, :].bitcast(I32))
         w1_s = (w_s, w1_s1)
-        w1_q = held([P, 4, 2 * HALF], U8, "w1_q", "x_sum3")
+        w1_q = at(sum_place + 4 * QUARTER, [P, 4, 2 * HALF], U8, "w1_q")
         nc.vector.tensor_copy(
             w1_q[:].bitcast(U16).rearrange("p gs (t c e) -> p gs c t e", t=4, e=4),
             w1_raw[:].bitcast(U16).rearrange("p g (side c e t) -> p (g side) c t e", side=2, t=4, e=4),
@@ -248,7 +251,7 @@ def tile_list_carbon_flux_features_kernel(
         for half in range(2):
             for g in range(2):
                 nc.vector.tensor_copy(v_q[half][:, g, :], tab_w[g][:].indirect(entries(list1, half * HALF, HALF)))
-        w3_q = held([P, 4, HALF], I32, "w3_q", "w1_raw")
+        w3_q = at(raw_place, [P, 4, HALF], I32, "w3_q")
         nc.gpsimd.tensor_copy(
             w3_q[:].rearrange("p gs (t c) -> p gs t c", t=4),
             w3_raw[:].rearrange("p g (side c t) -> p (g side) t c", side=2, t=4),
@@ -385,12 +388,12 @@ def tile_list_carbon_flux_features_kernel(
                 make_gate(0, side, jb, P)
 
         multiply(0, {0: P, P: P})
+        for jb, bank in third_pairs.items():
+            keep_pairs(nc.vector.tensor_copy, 2, jb, bank)
         quantise_h(0)
         make_gate(1, 1)
         make_gate(1, 0)
         keep_rows(0)
-        for jb, bank in third_pairs.items():
-            keep_pairs(nc.scalar.copy, 2, jb, bank)
 
         multiply(1, {0: QUARTER})
         finish(0, 1, minus_dec1[0])

@@ -115,9 +115,10 @@ def tile_list_carbon_flux_features_kernel(
         def quantise_wl(side):
             nc.vector.quantize_mx(out=wl_q[side][:].bitcast(FP8X4), scales=wl_s[side][:], in_=wl_bf[side][:])
 
-        x_sum = {q: held([P, 4, QUARTER], F32, f"x_sum{q}") for q in range(2)}
+        x_sum = {0: held([P, 4, QUARTER], F32, "x_sum0")}
         sum_place = piece_bytes + 21 * QUARTER
-        x_sum[2] = at(sum_place, [P, 4, QUARTER], F32, "x_sum2")
+        middle = at(sum_place, [P, 5, QUARTER], F32, "x_sum_middle")
+        x_sum[1], x_sum[2] = middle[:, 1:5], middle[:, 0:4]
         x_q = [held([P, QUARTER], U32, f"x_q{q}") for q in range(4)]
         x_bf = {q: held([P, 4 * QUARTER], BF16, f"x_bf{q}")[:] for q in (0, 2, 3)}
         x_s = {q: held([P, QUARTER], U8, f"x_s{q}")[:] for q in (0, 2, 3)}
@@ -133,6 +134,11 @@ def tile_list_carbon_flux_features_kernel(
             nc.vector.tensor_copy(
                 x_bf[q][:, 4 * j:4 * (j + width)].rearrange("p (c e i) -> p c i e", e=2, i=4),
                 x_sum[q][:, :, j:j + width].rearrange("p i (c e) -> p c i e", e=2),
+            )
+
+        def interleave_on_gpsimd(q):
+            nc.gpsimd.tensor_scalar(
+                x_bf[q].rearrange("p (c i) -> p c i", i=4), x_sum[q].rearrange("p i c -> p c i"), 1.0, 0.0, ALU.mult, ALU.add
             )
 
         def quantise_x(q, j=0, width=QUARTER):
@@ -198,9 +204,9 @@ def tile_list_carbon_flux_features_kernel(
         log_of_b(0, 0, P)
         quantise_wl(1)
         x_s[1] = at(piece_bytes, [P, QUARTER], U8, "x_s1")[:]
-        x_bf[1] = at(piece_bytes + QUARTER, [P, 4 * QUARTER], BF16, "x_bf1")[:]
+        x_bf[1] = held([P, 4 * QUARTER], BF16, "x_bf1", "wl_bf1")[:]
         third = at(piece_bytes + 9 * QUARTER, [P, 3, QUARTER], F32, "third")
-        interleave(1)
+        interleave_on_gpsimd(1)
         quantise_x(1)
         log_of_b(0, 1, P)
         for i in range(1, 4):
@@ -209,9 +215,7 @@ def tile_list_carbon_flux_features_kernel(
             add(third[:, i - 1, :], i, 2)
         log_of_b(1, 0)
         log_of_b(1, 1, P)
-        nc.gpsimd.tensor_scalar(
-            x_bf[2].rearrange("p (c i) -> p c i", i=4), x_sum[2][:].rearrange("p i c -> p c i"), 1.0, 0.0, ALU.mult, ALU.add
-        )
+        interleave_on_gpsimd(2)
         quantise_x(2)
         late = at(sum_place, [P, QUARTER], F32, "late")
         x_sum[3] = at(sum_place + 4 * QUARTER, [P, 4, QUARTER], F32, "x_sum3")
@@ -268,7 +272,7 @@ def tile_list_carbon_flux_features_kernel(
         a_rows = [a_halves[q // 2][:, q % 2, 0].rearrange("p (t j) -> p t j", t=4) for q in range(4)]
         a_pairs = [a_halves[q // 2][:, q % 2, 1].rearrange("p (c t e) -> p c t e", t=4, e=2) for q in range(4)]
         h_bf = held([P, 2, 4 * QUARTER], BF16, "h_bf", "wl_bf0")
-        h_tags = ("wl_bf1", "x_sum0", "x_sum1", "x_rows3")
+        h_tags = ("wl_bf1", "x_sum0", "x_bf0", "x_rows3")
         h_q = [held([P, 2, QUARTER], U32, f"h_q{q}", tag) for q, tag in enumerate(h_tags)]
         h_s = {}
 
@@ -373,9 +377,12 @@ def tile_list_carbon_flux_features_kernel(
                     h_on_gpsimd(q, jb, gpsimd_pieces[jb])
                 h_on_vector(q, 0, jb, bank)
 
+        def keep_row(copy, q, jb):
+            copy(a_rows[q][:, :, jb:jb + P], banks[q][jb][:])
+
         def keep_rows(q):
-            for jb, bank in banks[q].items():
-                nc.scalar.copy(a_rows[q][:, :, jb:jb + P], bank[:])
+            for jb in (0, P):
+                keep_row(nc.scalar.copy, q, jb)
 
         for q in range(2):
             for jb in (0, P):
@@ -383,6 +390,7 @@ def tile_list_carbon_flux_features_kernel(
         banks = {0: products_a(0, 0, "y_bank")}
         third_pairs = products_a(2, 1)
         banks[1] = products_a(1, 0)
+        keep_row(nc.vector.tensor_copy, 0, 0)
         for jb in (0, P):
             for side in (1, 0):
                 make_gate(0, side, jb, P)
@@ -393,7 +401,7 @@ def tile_list_carbon_flux_features_kernel(
         quantise_h(0)
         make_gate(1, 1)
         make_gate(1, 0)
-        keep_rows(0)
+        keep_row(nc.scalar.copy, 0, P)
 
         multiply(1, {0: QUARTER})
         finish(0, 1, minus_dec1[0])

@@ -24,6 +24,13 @@ WL_PIECE = 256
 BANKS = {"a_bank": 5, "y_bank": 3}
 TAB_ROW = 96
 EARLY = (3, 2, 2)
+RUN = 4 * QUARTER
+ABS_AT = 0
+WL_AT = 4 * RUN - 64
+X_S_AT = 4 * RUN
+PICKS_AT = X_S_AT + 9 * QUARTER
+SUMS_AT = PICKS_AT + 3 * RUN
+RAW_AT = SUMS_AT + 5 * RUN
 TINY = 2.0 ** -60
 
 
@@ -50,14 +57,12 @@ def tile_list_carbon_flux_features_kernel(
         list3 = held([P, S // PER_COLUMN], U16, "list3")
         x_rows = [held([P, T], F32, f"x_rows{i}") for i in range(4)]
         wl_cuts = ((0, HALF), (HALF, WL_PIECE), (HALF + WL_PIECE, WL_PIECE))
-        piece_bytes = 4 * 4 * WL_PIECE
         wl_raw = [held([P, 4, n], F32, f"wl_raw{c}") for c, n in wl_cuts[0:2]]
-        wl_raw.append(at(piece_bytes - 64, [P, 4, WL_PIECE], F32, "wl_raw_last"))
+        wl_raw.append(at(WL_AT, [P, 4, WL_PIECE], F32, "wl_raw_last"))
         tab_w = [held([P, T], U32, f"tab_w{g}") for g in range(2)]
         tab_s = held([P, T], U8, "tab_s")
-        raw_place = piece_bytes + 41 * QUARTER
-        w_s_raw = at(raw_place, [P, H], U8, "w_s_raw")
-        w1_raw = at(raw_place + H, [P, 2, 2 * H], U8, "w1_raw")
+        w_s_raw = at(RAW_AT, [P, H], U8, "w_s_raw")
+        w1_raw = at(RAW_AT + H, [P, 2, 2 * H], U8, "w1_raw")
         w3_raw = held([P, 2, H], I32, "w3_raw")
         dec_rows = held([P, 2, 4], F32, "dec_rows")
         v_s = [held([P, S], U8, f"v_s{g}") for g in range(2)]
@@ -90,9 +95,9 @@ def tile_list_carbon_flux_features_kernel(
         load_wl(1)
         load_wl(2)
         for d in range(4):
-            rows = slice(4 * d, 4 * d + 4)
-            nc.sync.dma_start(w_s_raw[32 * d:32 * d + 8, :].bitcast(I32), w1_scales[:, rows, :].bitcast(I32))
-            nc.sync.dma_start(w_s_raw[32 * d + 8:32 * d + 16, :].bitcast(I32), w3_scales[:, rows, :].bitcast(I32))
+            blocks = slice(4 * d, 4 * d + 4)
+            nc.sync.dma_start(w_s_raw[32 * d:32 * d + 8, :].bitcast(I32), w1_scales[:, blocks, :].bitcast(I32))
+            nc.sync.dma_start(w_s_raw[32 * d + 8:32 * d + 16, :].bitcast(I32), w3_scales[:, blocks, :].bitcast(I32))
         nc.sync.dma_start(w1_raw[:].bitcast(I32), w1_words.rearrange("g p n -> p g n").bitcast(I32))
         nc.sync.dma_start(w3_raw[:], w3_words.rearrange("g p n i -> p g (n i)").bitcast(I32))
         for g in range(2):
@@ -116,8 +121,7 @@ def tile_list_carbon_flux_features_kernel(
             nc.vector.quantize_mx(out=wl_q[side][:].bitcast(FP8X4), scales=wl_s[side][:], in_=wl_bf[side][:])
 
         x_sum = {0: held([P, 4, QUARTER], F32, "x_sum0")}
-        sum_place = piece_bytes + 21 * QUARTER
-        middle = at(sum_place, [P, 5, QUARTER], F32, "x_sum_middle")
+        middle = at(SUMS_AT, [P, 5, QUARTER], F32, "x_sum_middle")
         x_sum[1], x_sum[2] = middle[:, 1:5], middle[:, 0:4]
         x_q = [held([P, QUARTER], U32, f"x_q{q}") for q in range(4)]
         x_bf = {q: held([P, 4 * QUARTER], BF16, f"x_bf{q}")[:] for q in (0, 2, 3)}
@@ -137,9 +141,8 @@ def tile_list_carbon_flux_features_kernel(
             )
 
         def interleave_on_gpsimd(q):
-            nc.gpsimd.tensor_scalar(
-                x_bf[q].rearrange("p (c i) -> p c i", i=4), x_sum[q].rearrange("p i c -> p c i"), 1.0, 0.0, ALU.mult, ALU.add
-            )
+            by_word = x_bf[q].rearrange("p (c i) -> p c i", i=4)
+            nc.gpsimd.tensor_scalar(by_word, x_sum[q].rearrange("p i c -> p c i"), 1.0, 0.0, ALU.mult, ALU.add)
 
         def quantise_x(q, j=0, width=QUARTER):
             nc.vector.quantize_mx(
@@ -200,12 +203,12 @@ def tile_list_carbon_flux_features_kernel(
         first = held([P, QUARTER], F32, "first31", "early0")[:]
         pick(first, 3, 1)
         add(first, 3, 1)
-        abs_of[0, 0] = at(0, [P, 4 * QUARTER], F32, "abs_first")[:]
+        abs_of[0, 0] = at(ABS_AT, [P, 4 * QUARTER], F32, "abs_first")[:]
         log_of_b(0, 0, P)
         quantise_wl(1)
-        x_s[1] = at(piece_bytes, [P, QUARTER], U8, "x_s1")[:]
+        x_s[1] = at(X_S_AT, [P, QUARTER], U8, "x_s1")[:]
         x_bf[1] = held([P, 4 * QUARTER], BF16, "x_bf1", "wl_bf1")[:]
-        third = at(piece_bytes + 9 * QUARTER, [P, 3, QUARTER], F32, "third")
+        third = at(PICKS_AT, [P, 3, QUARTER], F32, "third")
         interleave_on_gpsimd(1)
         quantise_x(1)
         log_of_b(0, 1, P)
@@ -217,8 +220,8 @@ def tile_list_carbon_flux_features_kernel(
         log_of_b(1, 1, P)
         interleave_on_gpsimd(2)
         quantise_x(2)
-        late = at(sum_place, [P, QUARTER], F32, "late")
-        x_sum[3] = at(sum_place + 4 * QUARTER, [P, 4, QUARTER], F32, "x_sum3")
+        late = at(SUMS_AT, [P, QUARTER], F32, "late")
+        x_sum[3] = at(SUMS_AT + RUN, [P, 4, QUARTER], F32, "x_sum3")
         firsts = [third[:, 0, :], third[:, 1, :], third[:, 2, :], late[:]]
         for i in range(4):
             pick(firsts[i], i, 3)
@@ -245,7 +248,7 @@ def tile_list_carbon_flux_features_kernel(
         )
         nc.sync.dma_start(w1_s1[0:P - 4, :].bitcast(I32), w_s[4:P, :].bitcast(I32))
         w1_s = (w_s, w1_s1)
-        w1_q = at(sum_place + 4 * QUARTER, [P, 4, 2 * HALF], U8, "w1_q")
+        w1_q = at(SUMS_AT + RUN, [P, 4, 2 * HALF], U8, "w1_q")
         nc.vector.tensor_copy(
             w1_q[:].bitcast(U16).rearrange("p gs (t c e) -> p gs c t e", t=4, e=4),
             w1_raw[:].bitcast(U16).rearrange("p g (side c e t) -> p (g side) c t e", side=2, t=4, e=4),
@@ -255,7 +258,7 @@ def tile_list_carbon_flux_features_kernel(
         for half in range(2):
             for g in range(2):
                 nc.vector.tensor_copy(v_q[half][:, g, :], tab_w[g][:].indirect(entries(list1, half * HALF, HALF)))
-        w3_q = at(raw_place, [P, 4, HALF], I32, "w3_q")
+        w3_q = at(RAW_AT, [P, 4, HALF], I32, "w3_q")
         nc.gpsimd.tensor_copy(
             w3_q[:].rearrange("p gs (t c) -> p gs t c", t=4),
             w3_raw[:].rearrange("p g (side c t) -> p (g side) t c", side=2, t=4),
@@ -396,12 +399,12 @@ def tile_list_carbon_flux_features_kernel(
                 make_gate(0, side, jb, P)
 
         multiply(0, {0: P, P: P})
-        for jb, bank in third_pairs.items():
-            keep_pairs(nc.vector.tensor_copy, 2, jb, bank)
         quantise_h(0)
         make_gate(1, 1)
         make_gate(1, 0)
         keep_row(nc.scalar.copy, 0, P)
+        for jb, bank in third_pairs.items():
+            keep_pairs(nc.scalar.copy, 2, jb, bank)
 
         multiply(1, {0: QUARTER})
         finish(0, 1, minus_dec1[0])

@@ -113,8 +113,8 @@ def tile_list_carbon_flux_features_kernel(
         for raw, (c, width) in zip(wl_raw, wl_cuts):
             side, c0 = divmod(c, HALF)
             nc.scalar.copy(
-                wl_bf[side][:].rearrange("p (u e c i) -> p c u i e", u=2, e=2, i=4)[:, c0 // 4:(c0 + width) // 4],
-                raw[:].rearrange("p i (c u e) -> p c u i e", u=2, e=2),
+                wl_bf[side][:].rearrange("p (u e c i) -> p u c i e", u=2, e=2, i=4)[:, :, c0 // 4:(c0 + width) // 4],
+                raw[:].rearrange("p i (c u e) -> p u c i e", u=2, e=2),
             )
 
         def quantise_wl(side):

@@ -31,6 +31,7 @@ X_S_AT = 4 * RUN
 PICKS_AT = X_S_AT + 9 * QUARTER
 SUMS_AT = PICKS_AT + 3 * RUN
 RAW_AT = SUMS_AT + 5 * RUN
+PIECE_AT = RAW_AT + 8 * RUN
 TINY = 2.0 ** -60
 
 
@@ -56,8 +57,9 @@ def tile_list_carbon_flux_features_kernel(
         list2 = held([P, S // PER_COLUMN], U16, "list2")
         list3 = held([P, S // PER_COLUMN], U16, "list3")
         x_rows = [held([P, T], F32, f"x_rows{i}") for i in range(4)]
-        wl_cuts = ((0, HALF), (HALF, WL_PIECE), (HALF + WL_PIECE, WL_PIECE))
+        wl_cuts = [(c, WL_PIECE) for c in range(0, H, WL_PIECE)]
         wl_raw = [held([P, 4, n], F32, f"wl_raw{c}") for c, n in wl_cuts[0:2]]
+        wl_raw.append(at(PIECE_AT, [P, 4, WL_PIECE], F32, "wl_raw_third"))
         wl_raw.append(at(WL_AT, [P, 4, WL_PIECE], F32, "wl_raw_last"))
         tab_w = [held([P, T], U32, f"tab_w{g}") for g in range(2)]
         tab_s = held([P, T], U8, "tab_s")
@@ -91,9 +93,10 @@ def tile_list_carbon_flux_features_kernel(
         nc.sync.dma_start(x_rows[1][:], x_view[:, 1, :])
         nc.sync.dma_start(x_rows[2][:], x_view[:, 2, :])
         load_wl(0)
-        nc.sync.dma_start(x_rows[3][:], x_view[:, 3, :])
         load_wl(1)
+        nc.sync.dma_start(x_rows[3][:], x_view[:, 3, :])
         load_wl(2)
+        load_wl(3)
         for d in range(4):
             blocks = slice(4 * d, 4 * d + 4)
             nc.sync.dma_start(w_s_raw[32 * d:32 * d + 8, :].bitcast(I32), w1_scales[:, blocks, :].bitcast(I32))
@@ -192,15 +195,16 @@ def tile_list_carbon_flux_features_kernel(
                 add(firsts[q - 1], i, q - 1)
             add(firsts[-1], i, quarters - 1)
         first = held([P, QUARTER], F32, "first30", "early0")
-        pick(first[:], 3, 0)
         quantise_wl(0)
+        for j in (0, P):
+            pick(first[:, j:j + P], 3, 0, j, P)
         for j in (0, P):
             add(first[:, j:j + P], 3, 0, j, P)
         for j in (0, P):
             interleave(0, j, P)
         for j in (0, P):
             quantise_x(0, j, P)
-        first = held([P, QUARTER], F32, "first31", "early0")[:]
+        first = at(PIECE_AT, [P, QUARTER], F32, "first31")[:]
         pick(first, 3, 1)
         add(first, 3, 1)
         abs_of[0, 0] = at(ABS_AT, [P, 4 * QUARTER], F32, "abs_first")[:]
@@ -336,7 +340,7 @@ def tile_list_carbon_flux_features_kernel(
             )
 
         out_view = out.rearrange("(side p t) j -> side p t j", side=2, t=4)
-        result_tags = ("wl_raw0", "wl_raw512", "tab_w0", "tab_w1")
+        result_tags = ("wl_raw0", "wl_raw256", "tab_w0", "tab_w1")
         results = {}
 
         def finish_pair(q, side, t0, minus_dec, one_by_one=False, queue=nc.sync):

from contextlib import ExitStack

import concourse.mybir as mybir

K, K2, H, T, S = 1024, 512, 1024, 2048, 1024
FLOPS = 2 * S * H * (K + K2 + H)

F32 = mybir.dt.float32
BF16 = mybir.dt.bfloat16
I32 = mybir.dt.int32
U32 = mybir.dt.uint32
U16 = mybir.dt.uint16
U8 = mybir.dt.uint8
FP8X4 = mybir.dt.float8_e4m3fn_x4
FP4X4 = mybir.dt.float4_e2m1fn_x4
ACT = mybir.ActivationFunctionType
ALU = mybir.AluOpType

P = 128
HALF = 512
QUARTER = 256
PER_COLUMN = 16
WL_PIECE = 256
BANKS = {"a_bank": 5, "y_bank": 3}
TAB_ROW = 96
EARLY = (3, 2, 2)
RUN = 4 * QUARTER
ABS_AT = 0
WL_AT = 4 * RUN - 64
X_S_AT = 4 * RUN
PICKS_AT = X_S_AT + 9 * QUARTER
SUMS_AT = PICKS_AT + 3 * RUN
RAW_AT = SUMS_AT + 5 * RUN
PIECE_AT = RAW_AT + 8 * RUN
TINY = 2.0 ** -60


def tile_list_carbon_flux_features_kernel(
    tc, tab_words, tab_scales, offs, xT, offs2, offs3, w1_words, w1_scales, wl, w3_words, w3_scales, dec, out
):
    nc = tc.nc
    with ExitStack() as ctx:
        keep = ctx.enter_context(tc.tile_pool(name="keep", bufs=1))
        placed = ctx.enter_context(tc.tile_pool(name="placed", bufs=1))
        psum = ctx.enter_context(tc.psum_pool(name="psum", bufs=1))

        def held(shape, dtype, name, tag=""):
            return keep.tile(shape, dtype, name=name, tag=tag or name, align_bytes=64)

        def at(offset, shape, dtype, name):
            return placed.tile(shape, dtype, name=name, align_bytes=64, offset=offset)

        def entries(list_tile, j, n):
            return list_tile[:, j // PER_COLUMN:(j + n) // PER_COLUMN]

        list1 = held([P, S // PER_COLUMN], U16, "list1")
        list2 = held([P, S // PER_COLUMN], U16, "list2")
        list3 = held([P, S // PER_COLUMN], U16, "list3")
        x_rows = [held([P, T], F32, f"x_rows{i}") for i in range(4)]
        wl_cuts = [(c, WL_PIECE) for c in range(0, H, WL_PIECE)]
        wl_raw = [held([P, 4, n], F32, f"wl_raw{c}") for c, n in wl_cuts[0:2]]
        wl_raw.append(at(PIECE_AT, [P, 4, WL_PIECE], F32, "wl_raw_third"))
        wl_raw.append(at(WL_AT, [P, 4, WL_PIECE], F32, "wl_raw_last"))
        tab_w = [held([P, T], U32, f"tab_w{g}") for g in range(2)]
        tab_s = held([P, T], U8, "tab_s")
        w_s_raw = at(RAW_AT, [P, H], U8, "w_s_raw")
        w1_raw = at(RAW_AT + H, [P, 2, 2 * H], U8, "w1_raw")
        w3_raw = held([P, 2, H], I32, "w3_raw")
        dec_rows = held([P, 2, 4], F32, "dec_rows")
        v_s = [held([P, S], U8, f"v_s{g}") for g in range(2)]
        w1_s1 = held([P, H], U8, "w1_s1")

        one = held([P, 8], F32, "one")
        warm = held([P, 8], F32, "warm")
        nc.vector.memset(one[:], 1.0)
        nc.scalar.activation(warm[:], one[:], ACT.Ln)
        nc.vector.memset(tab_s[0:TAB_ROW, :].bitcast(I32), 0)
        for scale_tile in (w_s_raw, v_s[0], v_s[1], w1_s1):
            nc.vector.memset(scale_tile[:].bitcast(I32), 0)

        x_view = xT.rearrange("(p i) t -> p i t", i=4)
        wl_view = wl.rearrange("(p i) r -> p i r", i=4)

        def load_wl(n):
            c, width = wl_cuts[n]
            nc.sync.dma_start(wl_raw[n][:], wl_view[:, :, c:c + width])

        nc.sync.dma_start(list1[:], offs)
        nc.sync.dma_start(tab_s[TAB_ROW:P, :].bitcast(I32), tab_scales.rearrange("g q t -> (g q) t").bitcast(I32))
        nc.sync.dma_start(list2[:], offs2)
        nc.sync.dma_start(x_rows[0][:], x_view[:, 0, :])
        nc.sync.dma_start(list3[:], offs3)
        nc.sync.dma_start(x_rows[1][:], x_view[:, 1, :])
        nc.sync.dma_start(x_rows[2][:], x_view[:, 2, :])
        load_wl(0)
        load_wl(1)
        nc.sync.dma_start(x_rows[3][:], x_view[:, 3, :])
        load_wl(2)
        load_wl(3)
        for d in range(4):
            blocks = slice(4 * d, 4 * d + 4)
            nc.sync.dma_start(w_s_raw[32 * d:32 * d + 8, :].bitcast(I32), w1_scales[:, blocks, :].bitcast(I32))
            nc.sync.dma_start(w_s_raw[32 * d + 8:32 * d + 16, :].bitcast(I32), w3_scales[:, blocks, :].bitcast(I32))
        nc.sync.dma_start(w1_raw[:].bitcast(I32), w1_words.rearrange("g p n -> p g n").bitcast(I32))
        nc.sync.dma_start(w3_raw[:], w3_words.rearrange("g p n i -> p g (n i)").bitcast(I32))
        for g in range(2):
            nc.sync.dma_start(tab_w[g][:].bitcast(I32), tab_words[g].rearrange("p t i -> p (t i)").bitcast(I32))
        nc.sync.dma_start(dec_rows[:], dec.rearrange("(side p t) -> p side t", side=2, t=4))

        v_s_low = held([P, S], U8, "v_s_low")
        nc.vector.tensor_copy(v_s_low[:], tab_s[:].indirect(list1[:]))

        wl_bf = [held([P, 4 * HALF], BF16, f"wl_bf{side}") for side in range(2)]
        wl_q = [held([P, HALF], U32, f"wl_q{side}") for side in range(2)]
        wl_s = [held([P, HALF], U8, f"wl_s{side}") for side in range(2)]
        for raw, (c, width) in zip(wl_raw, wl_cuts):
            side, c0 = divmod(c, HALF)
            nc.scalar.copy(
                wl_bf[side][:].rearrange("p (u e c i) -> p u c i e", u=2, e=2, i=4)[:, :, c0 // 4:(c0 + width) // 4],
                raw[:].rearrange("p i (c u e) -> p u c i e", u=2, e=2),
            )

        def quantise_wl(side):
            nc.vector.quantize_mx(out=wl_q[side][:].bitcast(FP8X4), scales=wl_s[side][:], in_=wl_bf[side][:])

        x_sum = {0: held([P, 4, QUARTER], F32, "x_sum0")}
        middle = at(SUMS_AT, [P, 5, QUARTER], F32, "x_sum_middle")
        x_sum[1], x_sum[2] = middle[:, 1:5], middle[:, 0:4]
        x_q = [held([P, QUARTER], U32, f"x_q{q}") for q in range(4)]
        x_bf = {q: held([P, 4 * QUARTER], BF16, f"x_bf{q}")[:] for q in (0, 2, 3)}
        x_s = {q: held([P, QUARTER], U8, f"x_s{q}")[:] for q in (0, 2, 3)}

        def pick(first, i, q, j=0, width=QUARTER):
            nc.vector.tensor_copy(first, x_rows[i][:].indirect(entries(list2, q * QUARTER + j, width)))

        def add(first, i, q, j=0, width=QUARTER):
            picked = x_rows[i][:].indirect(entries(list3, q * QUARTER + j, width))
            nc.vector.tensor_tensor(x_sum[q][:, i, j:j + width], picked, first, ALU.add)

        def interleave(q, j=0, width=QUARTER):
            nc.vector.tensor_copy(
                x_bf[q][:, 4 * j:4 * (j + width)].rearrange("p (c e i) -> p c i e", e=2, i=4),
                x_sum[q][:, :, j:j + width].rearrange("p i (c e) -> p c i e", e=2),
            )

        def interleave_on_gpsimd(q):
            by_word = x_bf[q].rearrange("p (c i) -> p c i", i=4)
            nc.gpsimd.tensor_scalar(by_word, x_sum[q].rearrange("p i c -> p c i"), 1.0, 0.0, ALU.mult, ALU.add)

        def quantise_x(q, j=0, width=QUARTER):
            nc.vector.quantize_mx(
                out=x_q[q][:, j:j + width].bitcast(FP8X4),
                scales=x_s[q][:, j:j + width],
                in_=x_bf[q][:, 4 * j:4 * (j + width)],
            )

        abs_b = held([P, 4, 2, 4 * QUARTER], F32, "abs_b")
        log_b = held([P, 4, 2, 4 * QUARTER], F32, "log_b")
        abs_of = {(q, side): abs_b[:, q, side, :] for q in range(4) for side in range(2)}
        log_of = {(q, side): log_b[:, q, side, :] for q in range(4) for side in range(2)}
        log_of[0, 1] = held([P, 4 * QUARTER], F32, "log_first", "a_half1")[:]

        def abs_of_b(q, side, jb):
            turn = (4 * q + 2 * side + jb // P) % sum(BANKS.values())
            tag = "a_bank" if turn < BANKS["a_bank"] else "y_bank"
            bank = psum.tile([P, 4, P], F32, name="bank", tag=tag, bufs=BANKS[tag])
            for t in range(4):
                nc.tensor.matmul_mx(
                    out=bank[:, t, :],
                    lhsT=wl_q[side][:, t * P:(t + 1) * P].bitcast(FP8X4),
                    lhsT_scale=wl_s[side][:, t * P:(t + 1) * P],
                    rhs=x_q[q][:, jb:jb + P].bitcast(FP8X4),
                    rhs_scale=x_s[q][:, jb:jb + P],
                    start=True,
                    stop=True,
                )
            nc.scalar.activation(
                abs_of[q, side][:, 4 * jb:4 * (jb + P)].rearrange("p (j t) -> p j t", t=4),
                bank[:].rearrange("p t j -> p j t"),
                ACT.Abs,
            )

        def log_of_b(q, side, width=QUARTER):
            for jb in range(0, QUARTER, P):
                abs_of_b(q, side, jb)
            for j in range(0, QUARTER, width):
                columns = slice(4 * j, 4 * (j + width))
                nc.scalar.activation(log_of[q, side][:, columns], abs_of[q, side][:, columns], ACT.Ln, bias=TINY)

        for i, quarters in enumerate(EARLY):
            firsts = [held([P, QUARTER], F32, f"first{i}{q}", f"early{q}")[:] for q in range(quarters)]
            pick(firsts[0], i, 0)
            for q in range(1, quarters):
                pick(firsts[q], i, q)
                add(firsts[q - 1], i, q - 1)
            add(firsts[-1], i, quarters - 1)
        first = held([P, QUARTER], F32, "first30", "early0")
        quantise_wl(0)
        for j in (0, P):
            pick(first[:, j:j + P], 3, 0, j, P)
        for j in (0, P):
            add(first[:, j:j + P], 3, 0, j, P)
        for j in (0, P):
            interleave(0, j, P)
        for j in (0, P):
            quantise_x(0, j, P)
        first = at(PIECE_AT, [P, QUARTER], F32, "first31")[:]
        pick(first, 3, 1)
        add(first, 3, 1)
        abs_of[0, 0] = at(ABS_AT, [P, 4 * QUARTER], F32, "abs_first")[:]
        log_of_b(0, 0, P)
        quantise_wl(1)
        x_s[1] = at(X_S_AT, [P, QUARTER], U8, "x_s1")[:]
        x_bf[1] = held([P, 4 * QUARTER], BF16, "x_bf1", "wl_bf1")[:]
        third = at(PICKS_AT, [P, 3, QUARTER], F32, "third")
        interleave_on_gpsimd(1)
        quantise_x(1)
        log_of_b(0, 1, P)
        for i in range(1, 4):
            pick(third[:, i - 1, :], i, 2)
        for i in range(1, 4):
            add(third[:, i - 1, :], i, 2)
        log_of_b(1, 0)
        log_of_b(1, 1, P)
        interleave_on_gpsimd(2)
        quantise_x(2)
        late = at(SUMS_AT, [P, QUARTER], F32, "late")
        x_sum[3] = at(SUMS_AT + RUN, [P, 4, QUARTER], F32, "x_sum3")
        firsts = [third[:, 0, :], third[:, 1, :], third[:, 2, :], late[:]]
        for i in range(4):
            pick(firsts[i], i, 3)
        for i in range(4):
            add(firsts[i], i, 3)
        log_of_b(2, 0)
        log_of_b(2, 1, P)
        for j in (0, P):
            interleave(3, j, P)
        for j in (0, P):
            quantise_x(3, j, P)
        abs_of[3, 0] = held([P, 4 * QUARTER], F32, "abs_late", "x_rows2")[:]
        log_of_b(3, 0)
        log_of_b(3, 1, P)

        for g in range(2):
            for d in range(4):
                row = TAB_ROW + 16 * g + 4 * d
                nc.sync.dma_start(v_s[g][32 * d:32 * d + 4, :].bitcast(I32), v_s_low[row:row + 4, :].bitcast(I32))
        w_s = held([P, H], U8, "w_s", "x_rows1")
        nc.vector.tensor_copy(
            w_s[:].rearrange("p (side t c e) -> p side c t e", side=2, t=4, e=8),
            w_s_raw[:].rearrange("p (side c e t) -> p side c t e", side=2, t=4, e=8),
        )
        nc.sync.dma_start(w1_s1[0:P - 4, :].bitcast(I32), w_s[4:P, :].bitcast(I32))
        w1_s = (w_s, w1_s1)
        w1_q = at(SUMS_AT + RUN, [P, 4, 2 * HALF], U8, "w1_q")
        nc.vector.tensor_copy(
            w1_q[:].bitcast(U16).rearrange("p gs (t c e) -> p gs c t e", t=4, e=4),
            w1_raw[:].bitcast(U16).rearrange("p g (side c e t) -> p (g side) c t e", side=2, t=4, e=4),
        )
        v_words = held([P, 2, 2, HALF], U32, "v_words", "x_bf3")
        v_q = [v_words[:, half] for half in range(2)]
        for half in range(2):
            for g in range(2):
                nc.vector.tensor_copy(v_q[half][:, g, :], tab_w[g][:].indirect(entries(list1, half * HALF, HALF)))
        w3_q = at(RAW_AT, [P, 4, HALF], I32, "w3_q")
        nc.gpsimd.tensor_copy(
            w3_q[:].rearrange("p gs (t c) -> p gs t c", t=4),
            w3_raw[:].rearrange("p g (side c t) -> p (g side) t c", side=2, t=4),
        )
        minus_dec0 = held([P, 4], F32, "minus_dec")
        minus_dec1 = [held([P, 4], F32, f"minus_dec{q}", f"h_s{q + 1}") for q in range(3)]
        nc.scalar.mul(minus_dec0[:], dec_rows[:, 0, :], -1.0)
        minus_dec1.append(held([P, 4], F32, "minus_dec_last"))
        for minus_dec in minus_dec1:
            nc.scalar.mul(minus_dec[:], dec_rows[:, 1, :], -1.0)

        gate = held([P, 4, 2, 4 * QUARTER], F32, "gate", "abs_b")
        a_halves = [held([P, 2, 2, 4 * QUARTER], F32, f"a_half{n}", tag) for n, tag in enumerate(("x_rows2", ""))]
        a_rows = [a_halves[q // 2][:, q % 2, 0].rearrange("p (t j) -> p t j", t=4) for q in range(4)]
        a_pairs = [a_halves[q // 2][:, q % 2, 1].rearrange("p (c t e) -> p c t e", t=4, e=2) for q in range(4)]
        h_bf = held([P, 2, 4 * QUARTER], BF16, "h_bf", "wl_bf0")
        h_tags = ("wl_bf1", "x_sum0", "x_bf0", "x_rows3")
        h_q = [held([P, 2, QUARTER], U32, f"h_q{q}", tag) for q, tag in enumerate(h_tags)]
        h_s = {}

        def make_gate(q, side, j=0, width=QUARTER):
            columns = slice(4 * j, 4 * (j + width))
            nc.scalar.activation(gate[:, q, side, columns], log_of[q, side][:, columns], ACT.Sigmoid, scale=2.0)

        def product_a(q, side, jb, tag="a_bank"):
            j = q * QUARTER + jb
            half, jh = divmod(j, HALF)
            bank = psum.tile([P, 4, P], F32, name="bank", tag=tag, bufs=BANKS[tag])
            for t in range(4):
                columns = slice(side * HALF + t * P, side * HALF + (t + 1) * P)
                for g in range(2):
                    nc.tensor.matmul_mx(
                        out=bank[:, t, :],
                        lhsT=w1_q[:, 2 * g + side, 2 * t * P:2 * (t + 1) * P].bitcast(FP4X4),
                        lhsT_scale=w1_s[g][:, columns],
                        rhs=v_q[half][:, g, jh:jh + P].bitcast(FP8X4),
                        rhs_scale=v_s[g][:, j:j + P],
                        start=(g == 0),
                        stop=(g == 1),
                    )
            return bank

        def products_a(q, side, tag="a_bank"):
            return {jb: product_a(q, side, jb, tag) for jb in (0, P)}

        def by_plot(ap, jb):
            return ap[:, 4 * jb:4 * (jb + P)].rearrange("p (j t) -> p j t", t=4)

        def keep_pairs(copy, q, jb, bank):
            copy(a_pairs[q][:, jb // 2:(jb + P) // 2], bank[:].rearrange("p t (c e) -> p c t e", e=2))

        def h_on_gpsimd(q, jb, width):
            columns = slice(4 * jb, 4 * (jb + width))
            nc.gpsimd.tensor_tensor(
                h_bf[:, 1, columns].rearrange("p (c e t) -> p c e t", e=2, t=4),
                a_pairs[q][:, jb // 2:(jb + width) // 2].rearrange("p c t e -> p c e t"),
                gate[:, q, 1, columns].rearrange("p (c e t) -> p c e t", e=2, t=4),
                ALU.mult,
            )

        def h_on_vector(q, side, jb, bank):
            nc.vector.tensor_tensor(
                by_plot(h_bf[:, side, :], jb),
                bank[:].rearrange("p t j -> p j t"),
                by_plot(gate[:, q, side, :], jb),
                ALU.mult,
            )

        def quantise_h(q):
            h_s[q] = held([P, 2, QUARTER], U8, f"h_s{q}")
            nc.vector.quantize_mx(
                out=h_q[q][:].rearrange("p g j -> p (g j)").bitcast(FP8X4),
                scales=h_s[q][:].rearrange("p g j -> p (g j)"),
                in_=h_bf[:].rearrange("p g c -> p (g c)"),
            )

        out_view = out.rearrange("(side p t) j -> side p t j", side=2, t=4)
        result_tags = ("wl_raw0", "wl_raw256", "tab_w0", "tab_w1")
        results = {}

        def finish_pair(q, side, t0, minus_dec, one_by_one=False, queue=nc.sync):
            plots = slice(q * QUARTER, (q + 1) * QUARTER)
            if t0 == 0:
                results[q, side] = held([P, 4, QUARTER], F32, f"result{q}{side}", result_tags[(2 * q + side) % 4])
            result = results[q, side]
            y_bank = psum.tile([P, 2, QUARTER], F32, name="y_bank", tag="y_bank", bufs=BANKS["y_bank"])
            for t in (t0, t0 + 1):
                for g in range(2):
                    nc.tensor.matmul_mx(
                        out=y_bank[:, t - t0, :],
                        lhsT=w3_q[:, 2 * g + side, t * P:(t + 1) * P].bitcast(FP8X4),
                        lhsT_scale=w_s[8 + 4 * g:P, side * HALF + t * P:side * HALF + (t + 1) * P],
                        rhs=h_q[q][:, g, :].bitcast(FP8X4),
                        rhs_scale=h_s[q][:, g, :],
                        start=(g == 0),
                        stop=(g == 1),
                    )
            for t in (t0, t0 + 1):
                nc.vector.scalar_tensor_tensor(
                    result[:, t, :].rearrange("p (c e) -> p c e", e=2),
                    a_pairs[q][:, :, t, :] if side else a_rows[q][:, t, :].rearrange("p (c e) -> p c e", e=2),
                    minus_dec[:, t:t + 1],
                    y_bank[:, t - t0, :].rearrange("p (c e) -> p c e", e=2),
                    ALU.mult,
                    ALU.add,
                )
                if one_by_one:
                    (nc.sync, nc.scalar)[t - t0].dma_start(out_view[side, :, t, plots], result[:, t, :])
            if not one_by_one:
                queue.dma_start(out_view[side, :, t0:t0 + 2, plots], result[:, t0:t0 + 2, :])

        def finish(q, side, minus_dec):
            for t0 in (0, 2):
                finish_pair(q, side, t0, minus_dec)

        def multiply(q, gpsimd_pieces):
            for jb, bank in banks[q].items():
                if jb in gpsimd_pieces:
                    h_on_gpsimd(q, jb, gpsimd_pieces[jb])
                h_on_vector(q, 0, jb, bank)

        def keep_row(copy, q, jb):
            copy(a_rows[q][:, :, jb:jb + P], banks[q][jb][:])

        def keep_rows(q):
            for jb in (0, P):
                keep_row(nc.scalar.copy, q, jb)

        for q in range(2):
            for jb in (0, P):
                keep_pairs(nc.vector.tensor_copy, q, jb, product_a(q, 1, jb))
        banks = {0: products_a(0, 0, "y_bank")}
        third_pairs = products_a(2, 1)
        banks[1] = products_a(1, 0)
        keep_row(nc.vector.tensor_copy, 0, 0)
        for jb in (0, P):
            for side in (1, 0):
                make_gate(0, side, jb, P)

        multiply(0, {0: P, P: P})
        quantise_h(0)
        make_gate(1, 1)
        make_gate(1, 0)
        keep_row(nc.scalar.copy, 0, P)
        for jb, bank in third_pairs.items():
            keep_pairs(nc.scalar.copy, 2, jb, bank)

        multiply(1, {0: QUARTER})
        finish(0, 1, minus_dec1[0])
        finish(0, 0, minus_dec0)
        banks[2] = products_a(2, 0)
        last_pairs = product_a(3, 1, 0)
        quantise_h(1)
        make_gate(2, 1)
        make_gate(2, 0)
        make_gate(3, 1)
        keep_rows(1)
        keep_pairs(nc.scalar.copy, 3, 0, last_pairs)

        multiply(2, {0: QUARTER})
        finish(1, 1, minus_dec1[1])
        finish(1, 0, minus_dec0)
        banks[3] = products_a(3, 0)
        last_bank = product_a(3, 1, P)
        quantise_h(2)
        make_gate(3, 0)
        keep_rows(2)

        multiply(3, {0: P})
        h_on_vector(3, 1, P, last_bank)
        keep_pairs(nc.scalar.copy, 3, P, last_bank)
        finish_pair(2, 1, 0, minus_dec1[2])
        quantise_h(3)
        keep_rows(3)
        finish_pair(2, 1, 2, minus_dec1[3])
        for q, side, minus_dec in ((2, 0, minus_dec0), (3, 1, minus_dec1[3])):
            finish_pair(q, side, 0, minus_dec)
            finish_pair(q, side, 2, minus_dec, queue=nc.scalar)
        finish_pair(3, 0, 0, minus_dec0)
        finish_pair(3, 0, 2, minus_dec0, one_by_one=True)
